import numpy as np
import ml_dtypes


def mxq(x, axis, fmt="e4m3"):
    dtype, down = {"e4m3": (ml_dtypes.float8_e4m3fn, 7), "e5m2": (ml_dtypes.float8_e5m2, 14)}[fmt]
    v = np.moveaxis(np.asarray(x, np.float32).astype(ml_dtypes.bfloat16).astype(np.float64), axis, -1)
    blocks = v.reshape(v.shape[:-1] + (-1, 32))
    amax = np.abs(blocks).max(-1, keepdims=True)
    byte = np.maximum(np.where(amax > 0, np.frexp(amax)[1] - 1 + 127, 0) - down, 1)
    scale = np.exp2(byte - 127.0)
    codes = (blocks / scale).astype(np.float32).astype(dtype).astype(np.float64)
    return np.moveaxis((codes * scale).reshape(v.shape), -1, axis)


WIDE = False


def mx_kscale(k):
    if not WIDE:
        return np.ones(k)
    levels = np.array([24, -24, 12, -12, 0])
    if k % 512:
        return np.exp2(np.random.permutation(np.resize(levels, k // 32))).repeat(32)
    a = np.empty((k // 512, 16))
    for p in range(k // 512):
        a[p, :8] = np.random.permutation(np.resize(levels, 8))
        for g in range(8):
            far = levels[np.abs(levels - a[p, g]) >= 10]
            a[p, g + 8] = far[np.random.randint(len(far))]
    return np.exp2(a.ravel()).repeat(32)


def f64(x):
    return np.asarray(x).astype(np.float64)


def striped(idx):
    return np.tile(idx.reshape(-1, 16).T, (8, 1)).astype(np.uint16)


def unstriped(offs):
    return offs[:16].T.reshape(-1).astype(np.int64)


E2M1 = np.array([0.0, 0.5, 1.0, 1.5, 2.0, 3.0, 4.0, 6.0, -0.0, -0.5, -1.0, -1.5, -2.0, -3.0, -4.0, -6.0])


def pack_weight(w, fmt):
    k, n = w.shape
    w = f64(np.asarray(w, np.float32).astype(ml_dtypes.bfloat16)).reshape(k // 32, 32, n)
    amax = np.abs(w).max(1)
    if fmt == "e4m3":
        byte = np.frexp(amax)[1] - 1 + 127 - 7
    else:
        mant, ex = np.frexp(amax / 6.0)
        byte = np.where(mant > 0.5, ex, ex - 1) + 127
    byte = np.clip(np.where(amax > 0, byte, 1), 1, 254)
    scaled = (w * np.exp2(127.0 - byte)[:, None, :]).reshape(k, n).astype(np.float32)
    by_word = np.ascontiguousarray(scaled.reshape(k // 512, 128, 4, n).transpose(0, 1, 3, 2))
    if fmt == "e4m3":
        words = by_word.astype(ml_dtypes.float8_e4m3fn).view(np.uint8)
    else:
        c = by_word.astype(ml_dtypes.float4_e2m1fn).view(np.uint8) & 0xF
        words = (c[..., 0::2] | (c[..., 1::2] << 4)).reshape(k // 512, 128, 2 * n)
    return np.ascontiguousarray(words), np.ascontiguousarray(byte.astype(np.uint8).reshape(k // 512, 16, n))


def unpack_weight(words, scales, fmt):
    g, _, n = scales.shape
    words = np.ascontiguousarray(words).reshape(g, 128, n, -1)
    if fmt == "e4m3":
        vals = words.view(ml_dtypes.float8_e4m3fn).astype(np.float64)
    else:
        nib = np.empty((g, 128, n, 4), np.uint8)
        nib[..., 0::2] = words & 0xF
        nib[..., 1::2] = words >> 4
        vals = E2M1[nib]
    vals = vals * np.repeat(np.exp2(scales.astype(np.float64) - 127.0), 8, axis=1)[..., None]
    return vals.transpose(0, 1, 3, 2).reshape(g * 512, n)


def planes(y):
    n, m = y.shape
    v = y.astype(np.float32).astype(ml_dtypes.bfloat16).astype(np.float64).reshape(n // 32, 32, m)
    top = np.abs(v).max(1)
    byte = np.clip(np.where(top > 0, np.frexp(top)[1] - 1 + 127 - 7, 1), 1, 254)
    codes = (v * np.exp2(127.0 - byte)[:, None, :]).reshape(n, m).astype(np.float32).astype(ml_dtypes.float8_e4m3fn).view(np.uint8)
    words = codes.reshape(n // 512, 128, 4, m).transpose(0, 1, 3, 2)
    return np.ascontiguousarray(words), np.ascontiguousarray(byte.astype(np.uint8).reshape(n // 512, 16, m))


def sigm(f):
    return 1.0 / (1.0 + np.exp(-np.maximum(f, -700.0)))


K, N, T, J = 512, 512, 2048, 1024


def setup_inputs():
    n = np.random.standard_normal
    s = mx_kscale(K)[:, None]
    p_tab = pack_weight(n((K, T)) * s, "e4m3")
    return {
        "tab_words": p_tab[0],
        "tab_scales": p_tab[1],
        "wk": (n((K, N)) / np.sqrt(K) / s).astype(np.float32),
        "wv": (n((K, N)) / np.sqrt(K) / s).astype(np.float32),
        "st": (n((N, J))).astype(np.float32),
        "rT": (n((N, T))).astype(np.float32),
        "offs": striped(np.random.permutation(T)[:J]),
    }


def reference(tab_words, tab_scales, wk, wv, st, rT, offs):
    idx = unstriped(offs)
    tab_ = unpack_weight(tab_words, tab_scales, "e4m3")[:, idx]
    wk_ = mxq(f64(wk), 0, "e4m3")
    wv_ = mxq(f64(wv), 0, "e4m3")
    ke = wk_.T @ tab_
    ve = wv_.T @ tab_
    gate = sigm(ke + f64(st))
    out_0 = f64(rT)[:, idx] + gate * ve
    return (out_0,) + planes(out_0)

@@ -1,0 +1,203 @@
+from contextlib import ExitStack
+
+import concourse.mybir as mybir
+
+K, N, T, J = 512, 512, 2048, 1024
+FLOPS = 2 * 2 * K * N * J
+
+F32 = mybir.dt.float32
+BF16 = mybir.dt.bfloat16
+I32 = mybir.dt.int32
+U32 = mybir.dt.uint32
+U16 = mybir.dt.uint16
+U8 = mybir.dt.uint8
+FP8X4 = mybir.dt.float8_e4m3fn_x4
+ADD = mybir.AluOpType.add
+MULT = mybir.AluOpType.mult
+SIGMOID = mybir.ActivationFunctionType.Sigmoid
+
+P = 128
+PACK = 4
+BANK = 512
+CHUNK = 256
+
+
+def tile_list_engram_addLP_kernel(
+    tc, tab_words, tab_scales, wk, wv, st, rT, offs, out_0, out_1, out_2
+):
+    nc = tc.nc
+    with ExitStack() as ctx:
+        keep = ctx.enter_context(tc.tile_pool(name="keep", bufs=1))
+        psum = ctx.enter_context(tc.psum_pool(name="psum", bufs=4))
+
+        offsets = keep.tile([P, J // 16], U16, name="offsets")
+        scale_win = keep.tile([P, T], U8, name="scale_win", align_bytes=64)
+        word_win = keep.tile([P, T], I32, name="word_win", align_bytes=64)
+        w_raw = [keep.tile([P, PACK, N], F32, name=f"w_raw{i}", align_bytes=64) for i in range(2)]
+        w_bf = [keep.tile([P, PACK, P, PACK], BF16, name=f"w_bf{i}", align_bytes=64) for i in range(2)]
+        w_codes = [keep.tile([P, N], U32, name=f"w_codes{i}", align_bytes=64) for i in range(2)]
+        w_scales = [keep.tile([P, N], U8, name=f"w_scales{i}", align_bytes=64) for i in range(2)]
+        st_sb = [keep.tile([P, J], F32, name=f"st{t}", align_bytes=64) for t in range(PACK)]
+        r_win = [keep.tile([P, T], F32, name=f"r_win{t}", align_bytes=64) for t in range(PACK)]
+        r_got = [keep.tile([P, J], F32, name=f"r_got{t}", align_bytes=64) for t in range(PACK)]
+        key = [keep.tile([P, J], F32, name=f"key{t}", align_bytes=64) for t in range(PACK)]
+        gate = [keep.tile([P, J], F32, name=f"gate{t}", align_bytes=64) for t in range(PACK)]
+        gated = [keep.tile([P, J], F32, name=f"gated{t}", align_bytes=64) for t in range(PACK)]
+        tab_codes = keep.tile([P, J], U32, name="tab_codes", align_bytes=64)
+        tab_sc = keep.tile([P, J], U8, name="tab_sc", align_bytes=64)
+        result = [keep.tile([P, PACK * BANK], F32, name=f"result{h}", align_bytes=64) for h in range(J // BANK)]
+        res_bf = [keep.tile([P, CHUNK, PACK], BF16, name=f"res_bf{c}", align_bytes=64) for c in range(J // CHUNK)]
+        res_codes = keep.tile([P, J], U32, name="res_codes", align_bytes=64)
+        res_scales = keep.tile([P, J], U8, name="res_scales", align_bytes=64)
+        warm = keep.tile([P, 2], F32, name="warm", align_bytes=64)
+
+        st_rows = st.rearrange("(p t) j -> p t j", t=PACK)
+        r_rows = rT.rearrange("(p t) c -> p t c", t=PACK)
+        out_rows = out_0.rearrange("(p t) j -> p t j", t=PACK)
+        weights = [wk, wv]
+
+        nc.gpsimd.memset(warm[:, 0:1], 0.0)
+        nc.scalar.activation(warm[:, 1:2], warm[:, 0:1], SIGMOID)
+
+        def load(what, i=0):
+            if what == "offs":
+                nc.sync.dma_start(offsets[:], offs)
+            elif what == "scales":
+                for q in range(4):
+                    nc.sync.dma_start(
+                        scale_win[32 * q : 32 * q + 32, :].bitcast(I32),
+                        tab_scales[0, 4 * q : 4 * q + 4, :].bitcast(I32).unsqueeze(0).to_broadcast([8, 4, T // 4]),
+                    )
+            elif what == "words":
+                nc.sync.dma_start(word_win[:], tab_words[0].rearrange("p t i -> p (t i)").bitcast(I32))
+            elif what == "w":
+                nc.sync.dma_start(w_raw[i][:], weights[i].rearrange("(p i) c -> p i c", i=PACK))
+            elif what == "st":
+                nc.sync.dma_start(st_sb[i][:], st_rows[:, i, :])
+            else:
+                nc.sync.dma_start(r_win[i][:], r_rows[:, i, :])
+
+        for what, i in (("offs", 0), ("scales", 0), ("words", 0), ("w", 0), ("w", 1), ("st", 0), ("st", 1), ("r", 0), ("st", 2), ("st", 3), ("r", 1), ("r", 2), ("r", 3)):
+            load(what, i)
+
+        def cast_w(i, m0, m1, eng):
+            dst = w_bf[i][:, :, m0:m1, :].rearrange("p t m i -> p m i t")
+            src = w_raw[i][:].rearrange("p i (m t) -> p m i t", t=PACK)[:, m0:m1]
+            if eng == "V":
+                nc.vector.tensor_copy(dst, src)
+            else:
+                nc.scalar.copy(dst, src)
+
+        def quant_w(i):
+            nc.vector.quantize_mx(
+                out=w_codes[i][:].bitcast(FP8X4),
+                scales=w_scales[i][:],
+                in_=w_bf[i][:].rearrange("p t m i -> p (t m i)"),
+            )
+
+        def product(i, t, h):
+            acc = psum.tile([P, BANK], F32, name=f"acc{i}")
+            rows = slice(t * P, (t + 1) * P)
+            cols = slice(h * BANK, (h + 1) * BANK)
+            nc.tensor.matmul_mx(
+                out=acc[:],
+                lhsT=w_codes[i][:, rows].bitcast(FP8X4),
+                lhsT_scale=w_scales[i][:, rows],
+                rhs=tab_codes[:, cols].bitcast(FP8X4),
+                rhs_scale=tab_sc[:, cols],
+                start=True,
+                stop=True,
+            )
+            return acc
+
+        def gate_of(t, eng):
+            for h in range(J // BANK):
+                cols = slice(h * BANK, (h + 1) * BANK)
+                acc = product(0, t, h)
+                if eng == "V":
+                    nc.vector.tensor_tensor(key[t][:, cols], acc[:], st_sb[t][:, cols], ADD)
+                else:
+                    nc.scalar.copy(gate[t][:, cols], acc[:])
+                    nc.gpsimd.tensor_tensor(key[t][:, cols], gate[t][:, cols], st_sb[t][:, cols], ADD)
+            for h in range(J // BANK):
+                cols = slice(h * BANK, (h + 1) * BANK)
+                nc.scalar.activation(gate[t][:, cols], key[t][:, cols], SIGMOID)
+
+        def gated_of(t):
+            for h in range(J // BANK):
+                cols = slice(h * BANK, (h + 1) * BANK)
+                acc = product(1, t, h)
+                nc.vector.tensor_tensor(gated[t][:, cols], acc[:], gate[t][:, cols], MULT)
+
+        def gather_r(t, c0, c1):
+            nc.vector.tensor_copy(r_got[t][:, c0:c1], r_win[t][:].indirect(offsets[:, c0 // 16 : c1 // 16]))
+
+        def add_r(t, c0, c1, eng):
+            e = nc.vector if eng == "V" else nc.gpsimd
+            h, lo = divmod(c0, BANK)
+            e.tensor_tensor(result[h][:, t * BANK + lo : t * BANK + lo + c1 - c0], r_got[t][:, c0:c1], gated[t][:, c0:c1], ADD)
+
+        def store_plane(t, h):
+            nc.sync.dma_start(out_rows[:, t, h * BANK : (h + 1) * BANK], result[h][:, t * BANK : (t + 1) * BANK])
+
+        def round_chunk(c, eng):
+            h, lo = divmod(c * CHUNK, BANK)
+            cols = slice(lo, lo + CHUNK)
+            dst = res_bf[c][:].rearrange("p (g i) t -> p g t i", i=4)
+            src = result[h][:].rearrange("p (t j) -> p t j", t=PACK)[:, :, cols].rearrange("p t (g i) -> p g t i", i=4)
+            if eng == "V":
+                nc.vector.tensor_copy(dst, src)
+            else:
+                nc.scalar.copy(dst, src)
+
+        def quant_chunk(c):
+            cols = slice(c * CHUNK, (c + 1) * CHUNK)
+            nc.vector.quantize_mx(
+                out=res_codes[:, cols].bitcast(FP8X4),
+                scales=res_scales[:, cols],
+                in_=res_bf[c][:].rearrange("p j t -> p (j t)"),
+            )
+
+        out_words = out_1[0].rearrange("p j i -> p (j i)").bitcast(I32)
+
+        def store_codes(c0, c1):
+            nc.sync.dma_start(out_words[:, c0:c1], res_codes[:, c0:c1].bitcast(I32))
+
+        def store_scales():
+            for q in range(4):
+                e = nc.sync if q % 2 == 0 else nc.scalar
+                e.dma_start(
+                    out_2[0, 4 * q : 4 * q + 4, :].bitcast(I32), res_scales[32 * q : 32 * q + 4, :].bitcast(I32)
+                )
+
+        nc.vector.tensor_copy(tab_sc[:], scale_win[:].indirect(offsets[:]))
+        nc.vector.tensor_copy(tab_codes[:], word_win[:].bitcast(U32).indirect(offsets[:]))
+        cast_w(0, 0, 64, "S")
+        cast_w(0, 64, 128, "V")
+        quant_w(0)
+        cast_w(1, 0, 64, "S")
+        cast_w(1, 64, 128, "V")
+        quant_w(1)
+        gate_of(0, "V")
+        gate_of(1, "G")
+        gated_of(0)
+        for t in range(3):
+            for h in range(2):
+                gather_r(t, h * BANK, (h + 1) * BANK)
+                add_r(t, h * BANK, (h + 1) * BANK, "G")
+                store_plane(t, h)
+            if t == 0:
+                gate_of(2, "V")
+                gate_of(3, "G")
+            gated_of(t + 1)
+        for h in range(2):
+            gather_r(3, h * BANK, (h + 1) * BANK)
+            add_r(3, h * BANK, (h + 1) * BANK, "V")
+            store_plane(3, h)
+            for c in (2 * h, 2 * h + 1):
+                round_chunk(c, "V" if c == 2 else "S")
+        for c in range(4):
+            quant_chunk(c)
+            if c % 2 == 1:
+                store_codes((c - 1) * CHUNK, (c + 1) * CHUNK)
+        store_scales()

@@ -1,6 +1,7 @@
 from contextlib import ExitStack
 
 import concourse.mybir as mybir
+from concourse.masks import make_identity
 
 K, N, T, J = 512, 512, 2048, 1024
 FLOPS = 2 * 2 * K * N * J
@@ -18,8 +19,18 @@ SIGMOID = mybir.ActivationFunctionType.Sigmoid
 
 P = 128
 PACK = 4
-BANK = 512
-CHUNK = 256
+RUN = 4
+GROUP = 16
+QUADRANT = 32
+HALF = J // 2
+QUARTER = J // 4
+KEY, VALUE = 0, 1
+
+KEY_BANKS = (0, 6, 0, 6)
+LOGIT_BANK = 2
+VALUE_BANKS = (4, 5, 0, 1, 6, 7, 0, 1)
+BACK_BANKS = ((6, 7, 4, 5), (4, 6, 7, 5))
+SCALAR_COLS = 128
 
 
 def tile_list_engram_addLP_kernel(
@@ -28,176 +39,217 @@ def tile_list_engram_addLP_kernel(
     nc = tc.nc
     with ExitStack() as ctx:
         keep = ctx.enter_context(tc.tile_pool(name="keep", bufs=1))
-        psum = ctx.enter_context(tc.psum_pool(name="psum", bufs=4))
+        psum = ctx.enter_context(tc.psum_pool(name="psum", bufs=1))
 
-        offsets = keep.tile([P, J // 16], U16, name="offsets")
-        scale_win = keep.tile([P, T], U8, name="scale_win", align_bytes=64)
-        word_win = keep.tile([P, T], I32, name="word_win", align_bytes=64)
-        w_raw = [keep.tile([P, PACK, N], F32, name=f"w_raw{i}", align_bytes=64) for i in range(2)]
-        w_bf = [keep.tile([P, PACK, P, PACK], BF16, name=f"w_bf{i}", align_bytes=64) for i in range(2)]
-        w_codes = [keep.tile([P, N], U32, name=f"w_codes{i}", align_bytes=64) for i in range(2)]
-        w_scales = [keep.tile([P, N], U8, name=f"w_scales{i}", align_bytes=64) for i in range(2)]
-        st_sb = [keep.tile([P, J], F32, name=f"st{t}", align_bytes=64) for t in range(PACK)]
-        r_win = [keep.tile([P, T], F32, name=f"r_win{t}", align_bytes=64) for t in range(PACK)]
-        r_got = [keep.tile([P, J], F32, name=f"r_got{t}", align_bytes=64) for t in range(PACK)]
-        key = [keep.tile([P, J], F32, name=f"key{t}", align_bytes=64) for t in range(PACK)]
-        gate = [keep.tile([P, J], F32, name=f"gate{t}", align_bytes=64) for t in range(PACK)]
-        gated = [keep.tile([P, J], F32, name=f"gated{t}", align_bytes=64) for t in range(PACK)]
-        tab_codes = keep.tile([P, J], U32, name="tab_codes", align_bytes=64)
-        tab_sc = keep.tile([P, J], U8, name="tab_sc", align_bytes=64)
-        result = [keep.tile([P, PACK * BANK], F32, name=f"result{h}", align_bytes=64) for h in range(J // BANK)]
-        res_bf = [keep.tile([P, CHUNK, PACK], BF16, name=f"res_bf{c}", align_bytes=64) for c in range(J // CHUNK)]
-        res_codes = keep.tile([P, J], U32, name="res_codes", align_bytes=64)
-        res_scales = keep.tile([P, J], U8, name="res_scales", align_bytes=64)
-        warm = keep.tile([P, 2], F32, name="warm", align_bytes=64)
+        def sbuf(name, shape, dtype, tag=None):
+            return keep.tile(shape, dtype, name=name, tag=tag or name, align_bytes=64)
 
-        st_rows = st.rearrange("(p t) j -> p t j", t=PACK)
+        def bank(name, number):
+            return psum.tile([P, HALF], F32, name=name, tag=f"bank{number}")
+
+        offsets = keep.tile([P, J // GROUP], U16, name="offsets")
+        scale_win = sbuf("scale_win", [P, T], U8)
+        word_win = sbuf("word_win", [P, T], I32)
+        w_raw = [sbuf(f"w_raw{w}", [P, PACK, N], F32) for w in (KEY, VALUE)]
+        w_bf = [sbuf(f"w_bf{w}", [P, N, PACK], BF16) for w in (KEY, VALUE)]
+        w_codes = [sbuf(f"w_codes{w}", [P, N], U32) for w in (KEY, VALUE)]
+        w_scales = [sbuf(f"w_scales{w}", [P, N], U8) for w in (KEY, VALUE)]
+        st_sb = [sbuf(f"st{q}", [P, N // P, QUARTER], F32) for q in range(J // QUARTER)]
+        r_win = [sbuf(f"r_win{t}", [P, T], F32) for t in range(PACK)]
+        gate = [sbuf(f"gate{b}", [P, N], F32) for b in range(J // P)]
+        codes_head = sbuf("codes_head", [P, QUARTER], U32)
+        codes_rest = sbuf("codes_rest", [P, J - QUARTER], U32)
+        tab_sc = sbuf("tab_sc", [P, J], U8)
+        res_bf = [sbuf(f"res_bf{h}", [P, HALF, PACK], BF16) for h in range(2)]
+        res_codes = sbuf("res_codes", [P, J], U32)
+        res_scales = sbuf("res_scales", [P, J], U8)
+        ident = sbuf("ident", [P, P], F32)
+        warm = sbuf("warm", [P, 2], F32)
+
+        st_rows = st.rearrange("(a p) j -> p a j", p=P)
         r_rows = rT.rearrange("(p t) c -> p t c", t=PACK)
         out_rows = out_0.rearrange("(p t) j -> p t j", t=PACK)
-        weights = [wk, wv]
+        out_words = out_1[0].rearrange("p j i -> p (j i)").bitcast(I32)
+        halves = [slice(h * HALF, (h + 1) * HALF) for h in range(2)]
 
-        nc.gpsimd.memset(warm[:, 0:1], 0.0)
+        make_identity(nc, ident[:])
+        nc.vector.memset(warm[:, 0:1], 0.0)
         nc.scalar.activation(warm[:, 1:2], warm[:, 0:1], SIGMOID)
 
-        def load(what, i=0):
-            if what == "offs":
-                nc.sync.dma_start(offsets[:], offs)
-            elif what == "scales":
-                for q in range(4):
-                    nc.sync.dma_start(
-                        scale_win[32 * q : 32 * q + 32, :].bitcast(I32),
-                        tab_scales[0, 4 * q : 4 * q + 4, :].bitcast(I32).unsqueeze(0).to_broadcast([8, 4, T // 4]),
+        def load_w(w):
+            nc.sync.dma_start(w_raw[w][:], (wk, wv)[w].rearrange("(p i) c -> p i c", i=PACK))
+
+        def load_st(q):
+            nc.sync.dma_start(st_sb[q][:], st_rows[:, :, q * QUARTER : (q + 1) * QUARTER])
+
+        def load_r(t):
+            nc.sync.dma_start(r_win[t][:], r_rows[:, t, :])
+
+        nc.sync.dma_start(offsets[:], offs)
+        for quad in range(P // QUADRANT):
+            nc.sync.dma_start(
+                scale_win[QUADRANT * quad : QUADRANT * (quad + 1), :].bitcast(I32),
+                tab_scales[0, 4 * quad : 4 * quad + 4, :].bitcast(I32).unsqueeze(0).to_broadcast([QUADRANT // 4, 4, T // 4]),
+            )
+        load_w(KEY)
+        nc.sync.dma_start(word_win[:], tab_words[0].rearrange("p t i -> p (t i)").bitcast(I32))
+        load_w(VALUE)
+        load_r(0)
+        load_st(0)
+        load_r(1)
+        load_st(1)
+        load_st(2)
+        load_r(2)
+        load_st(3)
+        load_r(3)
+
+        def tab_codes(c0, c1):
+            if c0 < QUARTER:
+                return codes_head[:, c0:c1]
+            return codes_rest[:, c0 - QUARTER : c1 - QUARTER]
+
+        def weave_w(w, c0, c1, copy):
+            copy(
+                w_bf[w][:, c0:c1, :].rearrange("p (g e) i -> p g i e", e=RUN),
+                w_raw[w][:, :, c0:c1].rearrange("p i (g e) -> p g i e", e=RUN),
+            )
+
+        def quantise_w(w):
+            nc.vector.quantize_mx(
+                out=w_codes[w][:].bitcast(FP8X4),
+                scales=w_scales[w][:],
+                in_=w_bf[w][:].rearrange("p c i -> p (c i)"),
+            )
+
+        def keys_of(q):
+            keys = []
+            c0, c1 = q * QUARTER, (q + 1) * QUARTER
+            for u in range(2):
+                acc = bank(f"key_acc{q}_{u}", KEY_BANKS[q] + u)
+                for e in range(2):
+                    rows = slice((2 * u + e) * P, (2 * u + e + 1) * P)
+                    nc.tensor.matmul_mx(
+                        out=acc[:, e * QUARTER : (e + 1) * QUARTER],
+                        lhsT=w_codes[KEY][:, rows].bitcast(FP8X4),
+                        lhsT_scale=w_scales[KEY][:, rows],
+                        rhs=tab_codes(c0, c1).bitcast(FP8X4),
+                        rhs_scale=tab_sc[:, c0:c1],
+                        start=True,
+                        stop=True,
                     )
-            elif what == "words":
-                nc.sync.dma_start(word_win[:], tab_words[0].rearrange("p t i -> p (t i)").bitcast(I32))
-            elif what == "w":
-                nc.sync.dma_start(w_raw[i][:], weights[i].rearrange("(p i) c -> p i c", i=PACK))
-            elif what == "st":
-                nc.sync.dma_start(st_sb[i][:], st_rows[:, i, :])
-            else:
-                nc.sync.dma_start(r_win[i][:], r_rows[:, i, :])
+                key = sbuf(f"key{q}_{u}", [P, HALF], F32)
+                nc.scalar.copy(key[:], acc[:])
+                keys.append(key)
+            return keys
 
-        for what, i in (("offs", 0), ("scales", 0), ("words", 0), ("w", 0), ("w", 1), ("st", 0), ("st", 1), ("r", 0), ("st", 2), ("st", 3), ("r", 1), ("r", 2), ("r", 3)):
-            load(what, i)
-
-        def cast_w(i, m0, m1, eng):
-            dst = w_bf[i][:, :, m0:m1, :].rearrange("p t m i -> p m i t")
-            src = w_raw[i][:].rearrange("p i (m t) -> p m i t", t=PACK)[:, m0:m1]
-            if eng == "V":
-                nc.vector.tensor_copy(dst, src)
-            else:
-                nc.scalar.copy(dst, src)
-
-        def quant_w(i):
-            nc.vector.quantize_mx(
-                out=w_codes[i][:].bitcast(FP8X4),
-                scales=w_scales[i][:],
-                in_=w_bf[i][:].rearrange("p t m i -> p (t m i)"),
-            )
-
-        def product(i, t, h):
-            acc = psum.tile([P, BANK], F32, name=f"acc{i}")
-            rows = slice(t * P, (t + 1) * P)
-            cols = slice(h * BANK, (h + 1) * BANK)
-            nc.tensor.matmul_mx(
-                out=acc[:],
-                lhsT=w_codes[i][:, rows].bitcast(FP8X4),
-                lhsT_scale=w_scales[i][:, rows],
-                rhs=tab_codes[:, cols].bitcast(FP8X4),
-                rhs_scale=tab_sc[:, cols],
-                start=True,
-                stop=True,
-            )
-            return acc
-
-        def gate_of(t, eng):
-            for h in range(J // BANK):
-                cols = slice(h * BANK, (h + 1) * BANK)
-                acc = product(0, t, h)
-                if eng == "V":
-                    nc.vector.tensor_tensor(key[t][:, cols], acc[:], st_sb[t][:, cols], ADD)
-                else:
-                    nc.scalar.copy(gate[t][:, cols], acc[:])
-                    nc.gpsimd.tensor_tensor(key[t][:, cols], gate[t][:, cols], st_sb[t][:, cols], ADD)
-            for h in range(J // BANK):
-                cols = slice(h * BANK, (h + 1) * BANK)
-                nc.scalar.activation(gate[t][:, cols], key[t][:, cols], SIGMOID)
-
-        def gated_of(t):
-            for h in range(J // BANK):
-                cols = slice(h * BANK, (h + 1) * BANK)
-                acc = product(1, t, h)
-                nc.vector.tensor_tensor(gated[t][:, cols], acc[:], gate[t][:, cols], MULT)
-
-        def gather_r(t, c0, c1):
-            nc.vector.tensor_copy(r_got[t][:, c0:c1], r_win[t][:].indirect(offsets[:, c0 // 16 : c1 // 16]))
-
-        def add_r(t, c0, c1, eng):
-            e = nc.vector if eng == "V" else nc.gpsimd
-            h, lo = divmod(c0, BANK)
-            e.tensor_tensor(result[h][:, t * BANK + lo : t * BANK + lo + c1 - c0], r_got[t][:, c0:c1], gated[t][:, c0:c1], ADD)
-
-        def store_plane(t, h):
-            nc.sync.dma_start(out_rows[:, t, h * BANK : (h + 1) * BANK], result[h][:, t * BANK : (t + 1) * BANK])
-
-        def round_chunk(c, eng):
-            h, lo = divmod(c * CHUNK, BANK)
-            cols = slice(lo, lo + CHUNK)
-            dst = res_bf[c][:].rearrange("p (g i) t -> p g t i", i=4)
-            src = result[h][:].rearrange("p (t j) -> p t j", t=PACK)[:, :, cols].rearrange("p t (g i) -> p g t i", i=4)
-            if eng == "V":
-                nc.vector.tensor_copy(dst, src)
-            else:
-                nc.scalar.copy(dst, src)
-
-        def quant_chunk(c):
-            cols = slice(c * CHUNK, (c + 1) * CHUNK)
-            nc.vector.quantize_mx(
-                out=res_codes[:, cols].bitcast(FP8X4),
-                scales=res_scales[:, cols],
-                in_=res_bf[c][:].rearrange("p j t -> p (j t)"),
-            )
-
-        out_words = out_1[0].rearrange("p j i -> p (j i)").bitcast(I32)
-
-        def store_codes(c0, c1):
-            nc.sync.dma_start(out_words[:, c0:c1], res_codes[:, c0:c1].bitcast(I32))
-
-        def store_scales():
-            for q in range(4):
-                e = nc.sync if q % 2 == 0 else nc.scalar
-                e.dma_start(
-                    out_2[0, 4 * q : 4 * q + 4, :].bitcast(I32), res_scales[32 * q : 32 * q + 4, :].bitcast(I32)
+        def gates_of(q, keys):
+            for e in range(2):
+                b = 2 * q + e
+                acc = bank(f"logit{b}", LOGIT_BANK + e)
+                for a in range(N // P):
+                    nc.tensor.matmul(
+                        acc[:, a * P : (a + 1) * P], st_sb[q][:, a, e * P : (e + 1) * P], ident[:],
+                        start=(a == 0), stop=False, is_transpose=True,
+                    )
+                for a in range(N // P):
+                    at = (a % 2) * QUARTER + e * P
+                    nc.tensor.matmul(
+                        acc[:, a * P : (a + 1) * P], keys[a // 2][:, at : at + P], ident[:],
+                        start=False, stop=(a == N // P - 1), is_transpose=True,
+                    )
+                nc.scalar.activation(
+                    gate[b][:].rearrange("p (t m) -> p t m", t=PACK), acc[:].rearrange("p (m t) -> p t m", t=PACK), SIGMOID
                 )
 
+        gated = {}
+
+        def gated_values(blocks, tag=None):
+            shared = sbuf(f"gated{blocks[0]}", [P, len(blocks) * N], F32, tag=tag)
+            for place, b in enumerate(blocks):
+                gated[b] = shared[:, place * N : (place + 1) * N]
+                acc = bank(f"value{b}", VALUE_BANKS[b])
+                nc.tensor.matmul_mx(
+                    out=acc[:],
+                    lhsT=tab_codes(b * P, (b + 1) * P).bitcast(FP8X4),
+                    lhsT_scale=tab_sc[:, b * P : (b + 1) * P],
+                    rhs=w_codes[VALUE][:].bitcast(FP8X4),
+                    rhs_scale=w_scales[VALUE][:],
+                    start=True,
+                    stop=True,
+                )
+                nc.vector.tensor_tensor(
+                    gated[b].rearrange("p (t m) -> p t m", t=PACK),
+                    acc[:].rearrange("p (m t) -> p t m", t=PACK),
+                    gate[b][:].rearrange("p (t m) -> p t m", t=PACK),
+                    MULT,
+                )
+
+        record = {}
+
+        def gather_record(t, tag=None):
+            record[t] = sbuf(f"record{t}", [P, J], F32, tag=tag)
+            nc.vector.tensor_copy(record[t][:], r_win[t][:].indirect(offsets[:]))
+
+        def add_record(t, h):
+            acc = bank(f"back{t}_{h}", BACK_BANKS[h][t])
+            blocks = HALF // P
+            for e in range(blocks):
+                nc.tensor.transpose(acc[:, e * P : (e + 1) * P], gated[blocks * h + e][:, t * P : (t + 1) * P], ident[:])
+            plane = result[h][:, t * HALF : (t + 1) * HALF]
+            nc.vector.tensor_tensor(plane, acc[:], record[t][:, halves[h]], ADD)
+            nc.sync.dma_start(out_rows[:, t, halves[h]], plane)
+
+        def weave_result(h, c0, c1, copy):
+            copy(
+                res_bf[h][:, c0:c1, :].rearrange("p (g e) t -> p g t e", e=RUN),
+                result[h][:].rearrange("p (t j) -> p t j", t=PACK)[:, :, c0:c1].rearrange("p t (g e) -> p g t e", e=RUN),
+            )
+
+        def quantise_result(h):
+            nc.vector.quantize_mx(
+                out=res_codes[:, halves[h]].bitcast(FP8X4),
+                scales=res_scales[:, halves[h]],
+                in_=res_bf[h][:].rearrange("p j t -> p (j t)"),
+            )
+            nc.sync.dma_start(out_words[:, halves[h]], res_codes[:, halves[h]].bitcast(I32))
+
         nc.vector.tensor_copy(tab_sc[:], scale_win[:].indirect(offsets[:]))
-        nc.vector.tensor_copy(tab_codes[:], word_win[:].bitcast(U32).indirect(offsets[:]))
-        cast_w(0, 0, 64, "S")
-        cast_w(0, 64, 128, "V")
-        quant_w(0)
-        cast_w(1, 0, 64, "S")
-        cast_w(1, 64, 128, "V")
-        quant_w(1)
-        gate_of(0, "V")
-        gate_of(1, "G")
-        gated_of(0)
-        for t in range(3):
-            for h in range(2):
-                gather_r(t, h * BANK, (h + 1) * BANK)
-                add_r(t, h * BANK, (h + 1) * BANK, "G")
-                store_plane(t, h)
-            if t == 0:
-                gate_of(2, "V")
-                gate_of(3, "G")
-            gated_of(t + 1)
-        for h in range(2):
-            gather_r(3, h * BANK, (h + 1) * BANK)
-            add_r(3, h * BANK, (h + 1) * BANK, "V")
-            store_plane(3, h)
-            for c in (2 * h, 2 * h + 1):
-                round_chunk(c, "V" if c == 2 else "S")
-        for c in range(4):
-            quant_chunk(c)
-            if c % 2 == 1:
-                store_codes((c - 1) * CHUNK, (c + 1) * CHUNK)
-        store_scales()
+        weave_w(KEY, 0, N // 2, nc.scalar.copy)
+        weave_w(KEY, N // 2, N, nc.vector.tensor_copy)
+        quantise_w(KEY)
+        nc.vector.tensor_copy(codes_head[:], word_win[:].bitcast(U32).indirect(offsets[:, 0 : QUARTER // GROUP]))
+        nc.vector.tensor_copy(codes_rest[:], word_win[:].bitcast(U32).indirect(offsets[:, QUARTER // GROUP : J // GROUP]))
+        weave_w(VALUE, 0, N, nc.vector.tensor_copy)
+        quantise_w(VALUE)
+        all_keys = [keys_of(q) for q in range(J // QUARTER)]
+
+        gather_record(0)
+        gates_of(0, all_keys[0])
+        gated_values((0,), "r_win0")
+        gather_record(1, "gate0")
+        gates_of(1, all_keys[1])
+        gated_values((1, 2, 3), "r_win1")
+        gather_record(2, "gate2")
+        result = [sbuf("result0", [P, PACK * HALF], F32, tag="r_win2"), sbuf("result1", [P, PACK * HALF], F32)]
+        for t in range(PACK - 1):
+            add_record(t, 0)
+        gates_of(2, all_keys[2])
+        gated_values((4, 5))
+        gather_record(3, "gate4")
+        gates_of(3, all_keys[3])
+        gated_values((6, 7), "r_win3")
+
+        add_record(PACK - 1, 0)
+        weave_result(0, 0, HALF, nc.scalar.copy)
+        for t in range(PACK):
+            add_record(t, 1)
+        weave_result(1, 0, SCALAR_COLS, nc.scalar.copy)
+        weave_result(1, SCALAR_COLS, HALF, nc.vector.tensor_copy)
+        quantise_result(0)
+        quantise_result(1)
+        for quad in range(P // QUADRANT):
+            queue = nc.sync if quad % 2 else nc.scalar
+            queue.dma_start(
+                out_2[0, 4 * quad : 4 * quad + 4, :].bitcast(I32),
+                res_scales[QUADRANT * quad : QUADRANT * quad + 4, :].bitcast(I32),
+            )

@@ -1,7 +1,6 @@
 from contextlib import ExitStack
 
 import concourse.mybir as mybir
-from concourse.masks import make_identity
 
 K, N, T, J = 512, 512, 2048, 1024
 FLOPS = 2 * 2 * K * N * J
@@ -26,12 +25,6 @@ HALF = J // 2
 QUARTER = J // 4
 KEY, VALUE = 0, 1
 
-KEY_BANKS = (0, 6, 0, 6)
-LOGIT_BANK = 2
-VALUE_BANKS = (4, 5, 0, 1, 6, 7, 0, 1)
-BACK_BANKS = ((6, 7, 4, 5), (4, 6, 7, 5))
-SCALAR_COLS = 128
-
 
 def tile_list_engram_addLP_kernel(
     tc, tab_words, tab_scales, wk, wv, st, rT, offs, out_0, out_1, out_2
@@ -50,37 +43,36 @@ def tile_list_engram_addLP_kernel(
         offsets = keep.tile([P, J // GROUP], U16, name="offsets")
         scale_win = sbuf("scale_win", [P, T], U8)
         word_win = sbuf("word_win", [P, T], I32)
-        w_raw = [sbuf(f"w_raw{w}", [P, PACK, N], F32) for w in (KEY, VALUE)]
-        w_bf = [sbuf(f"w_bf{w}", [P, N, PACK], BF16) for w in (KEY, VALUE)]
+        w_raw = [[sbuf(f"w_raw{w}_{c}", [P, PACK, N // 2], F32) for c in range(2)] for w in (KEY, VALUE)]
+        w_bf = [sbuf(f"w_bf{w}", [P, N * PACK], BF16) for w in (KEY, VALUE)]
         w_codes = [sbuf(f"w_codes{w}", [P, N], U32) for w in (KEY, VALUE)]
         w_scales = [sbuf(f"w_scales{w}", [P, N], U8) for w in (KEY, VALUE)]
-        st_sb = [sbuf(f"st{q}", [P, N // P, QUARTER], F32) for q in range(J // QUARTER)]
+        st_sb = [sbuf(f"st{t}", [P, J], F32) for t in range(PACK)]
         r_win = [sbuf(f"r_win{t}", [P, T], F32) for t in range(PACK)]
-        gate = [sbuf(f"gate{b}", [P, N], F32) for b in range(J // P)]
-        codes_head = sbuf("codes_head", [P, QUARTER], U32)
-        codes_rest = sbuf("codes_rest", [P, J - QUARTER], U32)
+        tab_codes = [sbuf(f"tab_codes{h}", [P, HALF], U32) for h in range(2)]
         tab_sc = sbuf("tab_sc", [P, J], U8)
-        res_bf = [sbuf(f"res_bf{h}", [P, HALF, PACK], BF16) for h in range(2)]
+        result = [sbuf(f"result{h}", [P, PACK * HALF], F32) for h in range(2)]
+        res_bf = [sbuf(f"res_bf{h}", [P, HALF * PACK], BF16) for h in range(2)]
         res_codes = sbuf("res_codes", [P, J], U32)
         res_scales = sbuf("res_scales", [P, J], U8)
-        ident = sbuf("ident", [P, P], F32)
         warm = sbuf("warm", [P, 2], F32)
 
-        st_rows = st.rearrange("(a p) j -> p a j", p=P)
+        st_rows = st.rearrange("(p t) j -> p t j", t=PACK)
         r_rows = rT.rearrange("(p t) c -> p t c", t=PACK)
         out_rows = out_0.rearrange("(p t) j -> p t j", t=PACK)
         out_words = out_1[0].rearrange("p j i -> p (j i)").bitcast(I32)
         halves = [slice(h * HALF, (h + 1) * HALF) for h in range(2)]
 
-        make_identity(nc, ident[:])
         nc.vector.memset(warm[:, 0:1], 0.0)
         nc.scalar.activation(warm[:, 1:2], warm[:, 0:1], SIGMOID)
 
         def load_w(w):
-            nc.sync.dma_start(w_raw[w][:], (wk, wv)[w].rearrange("(p i) c -> p i c", i=PACK))
+            rows = (wk, wv)[w].rearrange("(p i) c -> p i c", i=PACK)
+            for c in range(2):
+                nc.sync.dma_start(w_raw[w][c][:], rows[:, :, c * N // 2 : (c + 1) * N // 2])
 
-        def load_st(q):
-            nc.sync.dma_start(st_sb[q][:], st_rows[:, :, q * QUARTER : (q + 1) * QUARTER])
+        def load_st(t):
+            nc.sync.dma_start(st_sb[t][:], st_rows[:, t, :])
 
         def load_r(t):
             nc.sync.dma_start(r_win[t][:], r_rows[:, t, :])
@@ -91,161 +83,108 @@ def tile_list_engram_addLP_kernel(
                 scale_win[QUADRANT * quad : QUADRANT * (quad + 1), :].bitcast(I32),
                 tab_scales[0, 4 * quad : 4 * quad + 4, :].bitcast(I32).unsqueeze(0).to_broadcast([QUADRANT // 4, 4, T // 4]),
             )
-        load_w(KEY)
         nc.sync.dma_start(word_win[:], tab_words[0].rearrange("p t i -> p (t i)").bitcast(I32))
-        load_w(VALUE)
-        load_r(0)
+        load_w(KEY)
         load_st(0)
-        load_r(1)
-        load_st(1)
-        load_st(2)
-        load_r(2)
-        load_st(3)
-        load_r(3)
+        load_w(VALUE)
+        for t in range(PACK):
+            if t + 1 < PACK:
+                load_st(t + 1)
+            load_r(t)
 
-        def tab_codes(c0, c1):
-            if c0 < QUARTER:
-                return codes_head[:, c0:c1]
-            return codes_rest[:, c0 - QUARTER : c1 - QUARTER]
+        def entries(c0, c1):
+            return offsets[:, c0 // GROUP : c1 // GROUP]
 
-        def weave_w(w, c0, c1, copy):
+        def weave_w(w, c, copy):
+            m0, m1 = c * P // 2, (c + 1) * P // 2
             copy(
-                w_bf[w][:, c0:c1, :].rearrange("p (g e) i -> p g i e", e=RUN),
-                w_raw[w][:, :, c0:c1].rearrange("p i (g e) -> p g i e", e=RUN),
+                w_bf[w][:].rearrange("p (t m i) -> p m t i", t=PACK, i=PACK)[:, m0:m1],
+                w_raw[w][c][:].rearrange("p i (m t) -> p m t i", t=PACK),
             )
 
         def quantise_w(w):
-            nc.vector.quantize_mx(
-                out=w_codes[w][:].bitcast(FP8X4),
-                scales=w_scales[w][:],
-                in_=w_bf[w][:].rearrange("p c i -> p (c i)"),
+            nc.vector.quantize_mx(out=w_codes[w][:].bitcast(FP8X4), scales=w_scales[w][:], in_=w_bf[w][:])
+
+        def product(w, t, h):
+            acc = bank(f"acc{w}_{t}_{h}", 4 * w + 2 * (t % 2) + h)
+            rows = slice(t * P, (t + 1) * P)
+            nc.tensor.matmul_mx(
+                out=acc[:],
+                lhsT=w_codes[w][:, rows].bitcast(FP8X4),
+                lhsT_scale=w_scales[w][:, rows],
+                rhs=tab_codes[h][:].bitcast(FP8X4),
+                rhs_scale=tab_sc[:, halves[h]],
+                start=True,
+                stop=True,
             )
+            return acc
 
-        def keys_of(q):
-            keys = []
-            c0, c1 = q * QUARTER, (q + 1) * QUARTER
-            for u in range(2):
-                acc = bank(f"key_acc{q}_{u}", KEY_BANKS[q] + u)
-                for e in range(2):
-                    rows = slice((2 * u + e) * P, (2 * u + e + 1) * P)
-                    nc.tensor.matmul_mx(
-                        out=acc[:, e * QUARTER : (e + 1) * QUARTER],
-                        lhsT=w_codes[KEY][:, rows].bitcast(FP8X4),
-                        lhsT_scale=w_scales[KEY][:, rows],
-                        rhs=tab_codes(c0, c1).bitcast(FP8X4),
-                        rhs_scale=tab_sc[:, c0:c1],
-                        start=True,
-                        stop=True,
-                    )
-                key = sbuf(f"key{q}_{u}", [P, HALF], F32)
-                nc.scalar.copy(key[:], acc[:])
-                keys.append(key)
-            return keys
-
-        def gates_of(q, keys):
-            for e in range(2):
-                b = 2 * q + e
-                acc = bank(f"logit{b}", LOGIT_BANK + e)
-                for a in range(N // P):
-                    nc.tensor.matmul(
-                        acc[:, a * P : (a + 1) * P], st_sb[q][:, a, e * P : (e + 1) * P], ident[:],
-                        start=(a == 0), stop=False, is_transpose=True,
-                    )
-                for a in range(N // P):
-                    at = (a % 2) * QUARTER + e * P
-                    nc.tensor.matmul(
-                        acc[:, a * P : (a + 1) * P], keys[a // 2][:, at : at + P], ident[:],
-                        start=False, stop=(a == N // P - 1), is_transpose=True,
-                    )
-                nc.scalar.activation(
-                    gate[b][:].rearrange("p (t m) -> p t m", t=PACK), acc[:].rearrange("p (m t) -> p t m", t=PACK), SIGMOID
-                )
-
+        gate = {}
         gated = {}
 
-        def gated_values(blocks, tag=None):
-            shared = sbuf(f"gated{blocks[0]}", [P, len(blocks) * N], F32, tag=tag)
-            for place, b in enumerate(blocks):
-                gated[b] = shared[:, place * N : (place + 1) * N]
-                acc = bank(f"value{b}", VALUE_BANKS[b])
-                nc.tensor.matmul_mx(
-                    out=acc[:],
-                    lhsT=tab_codes(b * P, (b + 1) * P).bitcast(FP8X4),
-                    lhsT_scale=tab_sc[:, b * P : (b + 1) * P],
-                    rhs=w_codes[VALUE][:].bitcast(FP8X4),
-                    rhs_scale=w_scales[VALUE][:],
-                    start=True,
-                    stop=True,
-                )
-                nc.vector.tensor_tensor(
-                    gated[b].rearrange("p (t m) -> p t m", t=PACK),
-                    acc[:].rearrange("p (m t) -> p t m", t=PACK),
-                    gate[b][:].rearrange("p (t m) -> p t m", t=PACK),
-                    MULT,
-                )
+        def gate_of(t, h):
+            logit = sbuf(f"logit{t}_{h}", [P, HALF], F32)
+            nc.vector.tensor_tensor(logit[:], product(KEY, t, h)[:], st_sb[t][:, halves[h]], ADD)
+            gate[t, h] = sbuf(f"gate{t}_{h}", [P, HALF], F32)
+            nc.scalar.activation(gate[t, h][:], logit[:], SIGMOID)
 
-        record = {}
+        def gated_value(t, h, place=None):
+            if place is None:
+                place = sbuf(f"gated{t}_{h}", [P, HALF], F32, tag=f"gated{h}")[:]
+            gated[t, h] = place
+            nc.vector.tensor_tensor(place, product(VALUE, t, h)[:], gate[t, h][:], MULT)
 
-        def gather_record(t, tag=None):
-            record[t] = sbuf(f"record{t}", [P, J], F32, tag=tag)
-            nc.vector.tensor_copy(record[t][:], r_win[t][:].indirect(offsets[:]))
-
-        def add_record(t, h):
-            acc = bank(f"back{t}_{h}", BACK_BANKS[h][t])
-            blocks = HALF // P
-            for e in range(blocks):
-                nc.tensor.transpose(acc[:, e * P : (e + 1) * P], gated[blocks * h + e][:, t * P : (t + 1) * P], ident[:])
-            plane = result[h][:, t * HALF : (t + 1) * HALF]
-            nc.vector.tensor_tensor(plane, acc[:], record[t][:, halves[h]], ADD)
-            nc.sync.dma_start(out_rows[:, t, halves[h]], plane)
+        def add_record(t, h, c0, c1):
+            plane = result[h][:, t * HALF + c0 : t * HALF + c1]
+            nc.vector.tensor_tensor(
+                plane, r_win[t][:].indirect(entries(h * HALF + c0, h * HALF + c1)), gated[t, h][:, c0:c1], ADD
+            )
+            nc.sync.dma_start(out_rows[:, t, h * HALF + c0 : h * HALF + c1], plane)
 
         def weave_result(h, c0, c1, copy):
             copy(
-                res_bf[h][:, c0:c1, :].rearrange("p (g e) t -> p g t e", e=RUN),
+                res_bf[h][:, c0 * PACK : c1 * PACK].rearrange("p (g e t) -> p g t e", e=RUN, t=PACK),
                 result[h][:].rearrange("p (t j) -> p t j", t=PACK)[:, :, c0:c1].rearrange("p t (g e) -> p g t e", e=RUN),
             )
 
         def quantise_result(h):
             nc.vector.quantize_mx(
-                out=res_codes[:, halves[h]].bitcast(FP8X4),
-                scales=res_scales[:, halves[h]],
-                in_=res_bf[h][:].rearrange("p j t -> p (j t)"),
+                out=res_codes[:, halves[h]].bitcast(FP8X4), scales=res_scales[:, halves[h]], in_=res_bf[h][:]
             )
             nc.sync.dma_start(out_words[:, halves[h]], res_codes[:, halves[h]].bitcast(I32))
 
         nc.vector.tensor_copy(tab_sc[:], scale_win[:].indirect(offsets[:]))
-        weave_w(KEY, 0, N // 2, nc.scalar.copy)
-        weave_w(KEY, N // 2, N, nc.vector.tensor_copy)
-        quantise_w(KEY)
-        nc.vector.tensor_copy(codes_head[:], word_win[:].bitcast(U32).indirect(offsets[:, 0 : QUARTER // GROUP]))
-        nc.vector.tensor_copy(codes_rest[:], word_win[:].bitcast(U32).indirect(offsets[:, QUARTER // GROUP : J // GROUP]))
-        weave_w(VALUE, 0, N, nc.vector.tensor_copy)
-        quantise_w(VALUE)
-        all_keys = [keys_of(q) for q in range(J // QUARTER)]
+        for h in range(2):
+            nc.vector.tensor_copy(tab_codes[h][:], word_win[:].bitcast(U32).indirect(entries(h * HALF, (h + 1) * HALF)))
+        for w in (KEY, VALUE):
+            weave_w(w, 0, nc.scalar.copy)
+            weave_w(w, 1, nc.vector.tensor_copy)
+            quantise_w(w)
+            if w == KEY:
+                for h in range(2):
+                    gate_of(0, h)
 
-        gather_record(0)
-        gates_of(0, all_keys[0])
-        gated_values((0,), "r_win0")
-        gather_record(1, "gate0")
-        gates_of(1, all_keys[1])
-        gated_values((1, 2, 3), "r_win1")
-        gather_record(2, "gate2")
-        result = [sbuf("result0", [P, PACK * HALF], F32, tag="r_win2"), sbuf("result1", [P, PACK * HALF], F32)]
         for t in range(PACK - 1):
-            add_record(t, 0)
-        gates_of(2, all_keys[2])
-        gated_values((4, 5))
-        gather_record(3, "gate4")
-        gates_of(3, all_keys[3])
-        gated_values((6, 7), "r_win3")
-
-        add_record(PACK - 1, 0)
-        weave_result(0, 0, HALF, nc.scalar.copy)
-        for t in range(PACK):
-            add_record(t, 1)
-        weave_result(1, 0, SCALAR_COLS, nc.scalar.copy)
-        weave_result(1, SCALAR_COLS, HALF, nc.vector.tensor_copy)
+            for h in range(2):
+                gated_value(t, h)
+            for h in range(2):
+                gate_of(t + 1, h)
+            add_record(t, 0, 0, HALF)
+            if t < 2:
+                add_record(t, 1, 0, HALF)
+        last = PACK - 1
+        parked = last * HALF - QUARTER
+        gated_value(last, 0, result[1][:, parked : parked + HALF])
+        gated_value(last, 1, sbuf("gated_last", [P, HALF], F32)[:])
+        for c0 in (0, QUARTER):
+            add_record(last, 0, c0, c0 + QUARTER)
+            weave_result(0, c0, c0 + QUARTER, nc.scalar.copy)
+        add_record(last - 1, 1, 0, HALF)
+        add_record(last, 1, 0, QUARTER)
+        weave_result(1, 0, QUARTER, nc.scalar.copy)
+        add_record(last, 1, QUARTER, HALF)
         quantise_result(0)
+        weave_result(1, QUARTER, HALF, nc.vector.tensor_copy)
         quantise_result(1)
         for quad in range(P // QUADRANT):
             queue = nc.sync if quad % 2 else nc.scalar

@@ -24,6 +24,7 @@ QUADRANT = 32
 HALF = J // 2
 QUARTER = J // 4
 KEY, VALUE = 0, 1
+SCALAR_M = (128, 96)
 
 
 def tile_list_engram_addLP_kernel(
@@ -43,7 +44,7 @@ def tile_list_engram_addLP_kernel(
         offsets = keep.tile([P, J // GROUP], U16, name="offsets")
         scale_win = sbuf("scale_win", [P, T], U8)
         word_win = sbuf("word_win", [P, T], I32)
-        w_raw = [[sbuf(f"w_raw{w}_{c}", [P, PACK, N // 2], F32) for c in range(2)] for w in (KEY, VALUE)]
+        w_raw = [sbuf(f"w_raw{w}", [P, PACK, N], F32) for w in (KEY, VALUE)]
         w_bf = [sbuf(f"w_bf{w}", [P, N * PACK], BF16) for w in (KEY, VALUE)]
         w_codes = [sbuf(f"w_codes{w}", [P, N], U32) for w in (KEY, VALUE)]
         w_scales = [sbuf(f"w_scales{w}", [P, N], U8) for w in (KEY, VALUE)]
@@ -63,13 +64,12 @@ def tile_list_engram_addLP_kernel(
         out_words = out_1[0].rearrange("p j i -> p (j i)").bitcast(I32)
         halves = [slice(h * HALF, (h + 1) * HALF) for h in range(2)]
 
+        nc.gpsimd.memset(scale_win[:].bitcast(I32), 0)
         nc.vector.memset(warm[:, 0:1], 0.0)
         nc.scalar.activation(warm[:, 1:2], warm[:, 0:1], SIGMOID)
 
         def load_w(w):
-            rows = (wk, wv)[w].rearrange("(p i) c -> p i c", i=PACK)
-            for c in range(2):
-                nc.sync.dma_start(w_raw[w][c][:], rows[:, :, c * N // 2 : (c + 1) * N // 2])
+            nc.sync.dma_start(w_raw[w][:], (wk, wv)[w].rearrange("(p i) c -> p i c", i=PACK))
 
         def load_st(t):
             nc.sync.dma_start(st_sb[t][:], st_rows[:, t, :])
@@ -80,13 +80,13 @@ def tile_list_engram_addLP_kernel(
         nc.sync.dma_start(offsets[:], offs)
         for quad in range(P // QUADRANT):
             nc.sync.dma_start(
-                scale_win[QUADRANT * quad : QUADRANT * (quad + 1), :].bitcast(I32),
-                tab_scales[0, 4 * quad : 4 * quad + 4, :].bitcast(I32).unsqueeze(0).to_broadcast([QUADRANT // 4, 4, T // 4]),
+                scale_win[QUADRANT * quad : QUADRANT * quad + 4, :].bitcast(I32),
+                tab_scales[0, 4 * quad : 4 * quad + 4, :].bitcast(I32),
             )
         nc.sync.dma_start(word_win[:], tab_words[0].rearrange("p t i -> p (t i)").bitcast(I32))
         load_w(KEY)
-        load_st(0)
         load_w(VALUE)
+        load_st(0)
         for t in range(PACK):
             if t + 1 < PACK:
                 load_st(t + 1)
@@ -95,11 +95,10 @@ def tile_list_engram_addLP_kernel(
         def entries(c0, c1):
             return offsets[:, c0 // GROUP : c1 // GROUP]
 
-        def weave_w(w, c, copy):
-            m0, m1 = c * P // 2, (c + 1) * P // 2
+        def weave_w(w, m0, m1, copy):
             copy(
                 w_bf[w][:].rearrange("p (t m i) -> p m t i", t=PACK, i=PACK)[:, m0:m1],
-                w_raw[w][c][:].rearrange("p i (m t) -> p m t i", t=PACK),
+                w_raw[w][:].rearrange("p i (m t) -> p m t i", t=PACK)[:, m0:m1],
             )
 
         def quantise_w(w):
@@ -153,12 +152,13 @@ def tile_list_engram_addLP_kernel(
             )
             nc.sync.dma_start(out_words[:, halves[h]], res_codes[:, halves[h]].bitcast(I32))
 
-        nc.vector.tensor_copy(tab_sc[:], scale_win[:].indirect(offsets[:]))
         for h in range(2):
             nc.vector.tensor_copy(tab_codes[h][:], word_win[:].bitcast(U32).indirect(entries(h * HALF, (h + 1) * HALF)))
+        nc.vector.tensor_copy(tab_sc[:], scale_win[:].indirect(offsets[:]))
         for w in (KEY, VALUE):
-            weave_w(w, 0, nc.scalar.copy)
-            weave_w(w, 1, nc.vector.tensor_copy)
+            weave_w(w, 0, SCALAR_M[w], nc.scalar.copy)
+            if SCALAR_M[w] < P:
+                weave_w(w, SCALAR_M[w], P, nc.vector.tensor_copy)
             quantise_w(w)
             if w == KEY:
                 for h in range(2):

@@ -24,7 +24,8 @@ QUADRANT = 32
 HALF = J // 2
 QUARTER = J // 4
 KEY, VALUE = 0, 1
-SCALAR_M = (128, 96)
+BANKS = (((0, 2), (5, 1), (3, 4), (6, 7)), ((3, 4), (6, 7), (0, 2), (1, 5)))
+SCALAR_M = (128, 80)
 
 
 def tile_list_engram_addLP_kernel(
@@ -52,7 +53,7 @@ def tile_list_engram_addLP_kernel(
         r_win = [sbuf(f"r_win{t}", [P, T], F32) for t in range(PACK)]
         tab_codes = [sbuf(f"tab_codes{h}", [P, HALF], U32) for h in range(2)]
         tab_sc = sbuf("tab_sc", [P, J], U8)
-        result = [sbuf(f"result{h}", [P, PACK * HALF], F32) for h in range(2)]
+        result = [sbuf(f"result{h}", [P, (PACK + h) * HALF], F32) for h in range(2)]
         res_bf = [sbuf(f"res_bf{h}", [P, HALF * PACK], BF16) for h in range(2)]
         res_codes = sbuf("res_codes", [P, J], U32)
         res_scales = sbuf("res_scales", [P, J], U8)
@@ -105,7 +106,7 @@ def tile_list_engram_addLP_kernel(
             nc.vector.quantize_mx(out=w_codes[w][:].bitcast(FP8X4), scales=w_scales[w][:], in_=w_bf[w][:])
 
         def product(w, t, h):
-            acc = bank(f"acc{w}_{t}_{h}", 4 * w + 2 * (t % 2) + h)
+            acc = bank(f"acc{w}_{t}_{h}", BANKS[w][t][h])
             rows = slice(t * P, (t + 1) * P)
             nc.tensor.matmul_mx(
                 out=acc[:],
@@ -119,13 +120,23 @@ def tile_list_engram_addLP_kernel(
             return acc
 
         gate = {}
+        logits = {}
         gated = {}
 
-        def gate_of(t, h):
-            logit = sbuf(f"logit{t}_{h}", [P, HALF], F32)
-            nc.vector.tensor_tensor(logit[:], product(KEY, t, h)[:], st_sb[t][:, halves[h]], ADD)
-            gate[t, h] = sbuf(f"gate{t}_{h}", [P, HALF], F32)
-            nc.scalar.activation(gate[t, h][:], logit[:], SIGMOID)
+        def gate_of(t, h, logit=None, pool_adds=False):
+            if logit is None:
+                logit = sbuf(f"logit{t}_{h}", [P, HALF], F32)
+            if not pool_adds:
+                nc.vector.tensor_tensor(logit[:], product(KEY, t, h)[:], st_sb[t][:, halves[h]], ADD)
+            else:
+                key = sbuf(f"key{t}_{h}", [P, HALF], F32)
+                nc.scalar.copy(key[:], product(KEY, t, h)[:])
+                nc.gpsimd.tensor_tensor(logit[:], key[:], st_sb[t][:, halves[h]], ADD)
+            logits[t, h] = logit
+
+        def squash(t, h, tag=None):
+            gate[t, h] = sbuf(f"gate{t}_{h}", [P, HALF], F32, tag=tag)
+            nc.scalar.activation(gate[t, h][:], logits[t, h][:], SIGMOID)
 
         def gated_value(t, h, place=None):
             if place is None:
@@ -143,7 +154,7 @@ def tile_list_engram_addLP_kernel(
         def weave_result(h, c0, c1, copy):
             copy(
                 res_bf[h][:, c0 * PACK : c1 * PACK].rearrange("p (g e t) -> p g t e", e=RUN, t=PACK),
-                result[h][:].rearrange("p (t j) -> p t j", t=PACK)[:, :, c0:c1].rearrange("p t (g e) -> p g t e", e=RUN),
+                result[h][:, 0 : PACK * HALF].rearrange("p (t j) -> p t j", t=PACK)[:, :, c0:c1].rearrange("p t (g e) -> p g t e", e=RUN),
             )
 
         def quantise_result(h):
@@ -160,22 +171,31 @@ def tile_list_engram_addLP_kernel(
             if SCALAR_M[w] < P:
                 weave_w(w, SCALAR_M[w], P, nc.vector.tensor_copy)
             quantise_w(w)
-            if w == KEY:
-                for h in range(2):
-                    gate_of(0, h)
-
+        early = sbuf("early_logits", [P, 3 * HALF], F32, tag=f"w_bf{VALUE}")
+        gate_of(0, 0, early[:, halves[0]])
+        squash(0, 0)
+        gate_of(1, 1, early[:, J:], True)
+        gate_of(0, 1, early[:, halves[1]])
+        squash(0, 1)
+        parked = PACK * HALF - QUARTER
         for t in range(PACK - 1):
-            for h in range(2):
-                gated_value(t, h)
-            for h in range(2):
-                gate_of(t + 1, h)
+            gated_value(t, 0, result[1][:, parked : parked + HALF])
+            gated_value(t, 1)
+            if t == 0:
+                gate_of(1, 0)
+            else:
+                held = sbuf(f"held{t}", [P, J], F32, tag=f"r_win{t - 1}")
+                gate_of(t + 1, 0, held[:, halves[0]])
+                gate_of(t + 1, 1, held[:, halves[1]], True)
+            squash(t + 1, 1, f"gate{t}_0")
+            squash(t + 1, 0)
             add_record(t, 0, 0, HALF)
             if t < 2:
                 add_record(t, 1, 0, HALF)
         last = PACK - 1
-        parked = last * HALF - QUARTER
+        parked = last * HALF - P
         gated_value(last, 0, result[1][:, parked : parked + HALF])
-        gated_value(last, 1, sbuf("gated_last", [P, HALF], F32)[:])
+        gated_value(last, 1, result[1][:, PACK * HALF :])
         for c0 in (0, QUARTER):
             add_record(last, 0, c0, c0 + QUARTER)
             weave_result(0, c0, c0 + QUARTER, nc.scalar.copy)

@@ -25,7 +25,7 @@ HALF = J // 2
 QUARTER = J // 4
 KEY, VALUE = 0, 1
 BANKS = (((0, 2), (5, 1), (3, 4), (6, 7)), ((3, 4), (6, 7), (0, 2), (1, 5)))
-SCALAR_M = (128, 80)
+SCALAR_M = (96, 88)
 
 
 def tile_list_engram_addLP_kernel(
@@ -51,10 +51,10 @@ def tile_list_engram_addLP_kernel(
         w_scales = [sbuf(f"w_scales{w}", [P, N], U8) for w in (KEY, VALUE)]
         st_sb = [sbuf(f"st{t}", [P, J], F32) for t in range(PACK)]
         r_win = [sbuf(f"r_win{t}", [P, T], F32) for t in range(PACK)]
-        tab_codes = [sbuf(f"tab_codes{h}", [P, HALF], U32) for h in range(2)]
+        tab_codes = sbuf("tab_codes", [P, J], U32)
         tab_sc = sbuf("tab_sc", [P, J], U8)
         result = [sbuf(f"result{h}", [P, (PACK + h) * HALF], F32) for h in range(2)]
-        res_bf = [sbuf(f"res_bf{h}", [P, HALF * PACK], BF16) for h in range(2)]
+        res_bf = [sbuf("res_bf0", [P, HALF * PACK], BF16)]
         res_codes = sbuf("res_codes", [P, J], U32)
         res_scales = sbuf("res_scales", [P, J], U8)
         warm = sbuf("warm", [P, 2], F32)
@@ -112,7 +112,7 @@ def tile_list_engram_addLP_kernel(
                 out=acc[:],
                 lhsT=w_codes[w][:, rows].bitcast(FP8X4),
                 lhsT_scale=w_scales[w][:, rows],
-                rhs=tab_codes[h][:].bitcast(FP8X4),
+                rhs=tab_codes[:, halves[h]].bitcast(FP8X4),
                 rhs_scale=tab_sc[:, halves[h]],
                 start=True,
                 stop=True,
@@ -149,22 +149,23 @@ def tile_list_engram_addLP_kernel(
             nc.vector.tensor_tensor(
                 plane, r_win[t][:].indirect(entries(h * HALF + c0, h * HALF + c1)), gated[t, h][:, c0:c1], ADD
             )
-            nc.sync.dma_start(out_rows[:, t, h * HALF + c0 : h * HALF + c1], plane)
+            if c1 == HALF:
+                nc.sync.dma_start(out_rows[:, t, halves[h]], result[h][:, t * HALF : (t + 1) * HALF])
 
-        def weave_result(h, c0, c1, copy):
-            copy(
-                res_bf[h][:, c0 * PACK : c1 * PACK].rearrange("p (g e t) -> p g t e", e=RUN, t=PACK),
-                result[h][:, 0 : PACK * HALF].rearrange("p (t j) -> p t j", t=PACK)[:, :, c0:c1].rearrange("p t (g e) -> p g t e", e=RUN),
-            )
+        def weave_pair(h, u, c0, c1):
+            planes = result[h][:, 2 * u * HALF : 2 * (u + 1) * HALF].rearrange("p (v j) -> p j v", v=2)
+            nc.scalar.copy(res_bf[h][:].rearrange("p (j u v) -> p u j v", u=2, v=2)[:, u, c0:c1], planes[:, c0:c1])
 
-        def quantise_result(h):
+        def quantise_result(h, c0, c1):
+            cols = slice(h * HALF + c0, h * HALF + c1)
             nc.vector.quantize_mx(
-                out=res_codes[:, halves[h]].bitcast(FP8X4), scales=res_scales[:, halves[h]], in_=res_bf[h][:]
+                out=res_codes[:, cols].bitcast(FP8X4),
+                scales=res_scales[:, cols],
+                in_=res_bf[h][:, c0 * PACK : c1 * PACK],
             )
-            nc.sync.dma_start(out_words[:, halves[h]], res_codes[:, halves[h]].bitcast(I32))
+            nc.sync.dma_start(out_words[:, cols], res_codes[:, cols].bitcast(I32))
 
-        for h in range(2):
-            nc.vector.tensor_copy(tab_codes[h][:], word_win[:].bitcast(U32).indirect(entries(h * HALF, (h + 1) * HALF)))
+        nc.vector.tensor_copy(tab_codes[:], word_win[:].bitcast(U32).indirect(offsets[:]))
         nc.vector.tensor_copy(tab_sc[:], scale_win[:].indirect(offsets[:]))
         for w in (KEY, VALUE):
             weave_w(w, 0, SCALAR_M[w], nc.scalar.copy)
@@ -190,22 +191,25 @@ def tile_list_engram_addLP_kernel(
             squash(t + 1, 1, f"gate{t}_0")
             squash(t + 1, 0)
             add_record(t, 0, 0, HALF)
+            if t == 1:
+                weave_pair(0, 0, 0, HALF)
             if t < 2:
                 add_record(t, 1, 0, HALF)
         last = PACK - 1
         parked = last * HALF - P
         gated_value(last, 0, result[1][:, parked : parked + HALF])
         gated_value(last, 1, result[1][:, PACK * HALF :])
-        for c0 in (0, QUARTER):
-            add_record(last, 0, c0, c0 + QUARTER)
-            weave_result(0, c0, c0 + QUARTER, nc.scalar.copy)
-        add_record(last - 1, 1, 0, HALF)
-        add_record(last, 1, 0, QUARTER)
-        weave_result(1, 0, QUARTER, nc.scalar.copy)
-        add_record(last, 1, QUARTER, HALF)
-        quantise_result(0)
-        weave_result(1, QUARTER, HALF, nc.vector.tensor_copy)
-        quantise_result(1)
+        res_bf.append(sbuf("res_bf1", [P, HALF * PACK], BF16, tag="r_win1"))
+        weave_pair(1, 0, 0, HALF)
+        for h in range(2):
+            if h == 1:
+                add_record(last - 1, 1, 0, HALF)
+            for c0 in (0, QUARTER):
+                add_record(last, h, c0, c0 + QUARTER)
+                weave_pair(h, 1, c0, c0 + QUARTER)
+        quantise_result(0, 0, HALF)
+        quantise_result(1, 0, QUARTER)
+        quantise_result(1, QUARTER, HALF)
         for quad in range(P // QUADRANT):
             queue = nc.sync if quad % 2 else nc.scalar
             queue.dma_start(

@@ -180,14 +180,14 @@ def tile_list_engram_addLP_kernel(
         squash(0, 1)
         parked = PACK * HALF - QUARTER
         for t in range(PACK - 1):
-            gated_value(t, 0, result[1][:, parked : parked + HALF])
+            at = parked - (2 - t) * QUARTER
+            gated_value(t, 0, result[1][:, at : at + HALF])
             gated_value(t, 1)
             if t == 0:
                 gate_of(1, 0)
             else:
-                held = sbuf(f"held{t}", [P, J], F32, tag=f"r_win{t - 1}")
-                gate_of(t + 1, 0, held[:, halves[0]])
-                gate_of(t + 1, 1, held[:, halves[1]], True)
+                gate_of(t + 1, 0, sbuf(f"held{t}", [P, HALF], F32, tag=f"r_win{t - 1}")[:])
+                gate_of(t + 1, 1, result[1][:, at - HALF : at], True)
             squash(t + 1, 1, f"gate{t}_0")
             squash(t + 1, 0)
             add_record(t, 0, 0, HALF)

@@ -152,9 +152,9 @@ def tile_list_engram_addLP_kernel(
             if c1 == HALF:
                 nc.sync.dma_start(out_rows[:, t, halves[h]], result[h][:, t * HALF : (t + 1) * HALF])
 
-        def weave_pair(h, u, c0, c1):
+        def weave_pair(h, u, c0, c1, copy=nc.scalar.copy):
             planes = result[h][:, 2 * u * HALF : 2 * (u + 1) * HALF].rearrange("p (v j) -> p j v", v=2)
-            nc.scalar.copy(res_bf[h][:].rearrange("p (j u v) -> p u j v", u=2, v=2)[:, u, c0:c1], planes[:, c0:c1])
+            copy(res_bf[h][:].rearrange("p (j u v) -> p u j v", u=2, v=2)[:, u, c0:c1], planes[:, c0:c1])
 
         def quantise_result(h, c0, c1):
             cols = slice(h * HALF + c0, h * HALF + c1)
@@ -163,7 +163,8 @@ def tile_list_engram_addLP_kernel(
                 scales=res_scales[:, cols],
                 in_=res_bf[h][:, c0 * PACK : c1 * PACK],
             )
-            nc.sync.dma_start(out_words[:, cols], res_codes[:, cols].bitcast(I32))
+            if c1 == HALF:
+                nc.sync.dma_start(out_words[:, halves[h]], res_codes[:, halves[h]].bitcast(I32))
 
         nc.vector.tensor_copy(tab_codes[:], word_win[:].bitcast(U32).indirect(offsets[:]))
         nc.vector.tensor_copy(tab_sc[:], scale_win[:].indirect(offsets[:]))
@@ -193,21 +194,20 @@ def tile_list_engram_addLP_kernel(
             add_record(t, 0, 0, HALF)
             if t == 1:
                 weave_pair(0, 0, 0, HALF)
-            if t < 2:
-                add_record(t, 1, 0, HALF)
+            add_record(t, 1, 0, HALF)
         last = PACK - 1
-        parked = last * HALF - P
-        gated_value(last, 0, result[1][:, parked : parked + HALF])
-        gated_value(last, 1, result[1][:, PACK * HALF :])
+        gated_value(last, 0, result[1][:, PACK * HALF :])
+        gated_value(last, 1)
         res_bf.append(sbuf("res_bf1", [P, HALF * PACK], BF16, tag="r_win1"))
         weave_pair(1, 0, 0, HALF)
         for h in range(2):
-            if h == 1:
-                add_record(last - 1, 1, 0, HALF)
             for c0 in (0, QUARTER):
                 add_record(last, h, c0, c0 + QUARTER)
-                weave_pair(h, 1, c0, c0 + QUARTER)
-        quantise_result(0, 0, HALF)
+                if (h, c0) != (1, QUARTER):
+                    weave_pair(h, 1, c0, c0 + QUARTER)
+        quantise_result(0, 0, QUARTER)
+        quantise_result(0, QUARTER, HALF)
+        weave_pair(1, 1, QUARTER, HALF, nc.vector.tensor_copy)
         quantise_result(1, 0, QUARTER)
         quantise_result(1, QUARTER, HALF)
         for quad in range(P // QUADRANT):

@@ -1,6 +1,7 @@
 from contextlib import ExitStack
 
 import concourse.mybir as mybir
+from concourse.masks import make_identity
 
 K, N, T, J = 512, 512, 2048, 1024
 FLOPS = 2 * 2 * K * N * J
@@ -18,13 +19,12 @@ SIGMOID = mybir.ActivationFunctionType.Sigmoid
 
 P = 128
 PACK = 4
-RUN = 4
 GROUP = 16
 QUADRANT = 32
 HALF = J // 2
 QUARTER = J // 4
+LAST = PACK - 1
 KEY, VALUE = 0, 1
-BANKS = (((0, 2), (5, 1), (3, 4), (6, 7)), ((3, 4), (6, 7), (0, 2), (1, 5)))
 SCALAR_M = (96, 88)
 
 
@@ -39,7 +39,8 @@ def tile_list_engram_addLP_kernel(
         def sbuf(name, shape, dtype, tag=None):
             return keep.tile(shape, dtype, name=name, tag=tag or name, align_bytes=64)
 
-        def bank(name, number):
+        def bank(name, w, t, h):
+            number = 4 * ((w + t // 2) % 2) + 2 * (t % 2) + h
             return psum.tile([P, HALF], F32, name=name, tag=f"bank{number}")
 
         offsets = keep.tile([P, J // GROUP], U16, name="offsets")
@@ -54,9 +55,9 @@ def tile_list_engram_addLP_kernel(
         tab_codes = sbuf("tab_codes", [P, J], U32)
         tab_sc = sbuf("tab_sc", [P, J], U8)
         result = [sbuf(f"result{h}", [P, (PACK + h) * HALF], F32) for h in range(2)]
-        res_bf = [sbuf("res_bf0", [P, HALF * PACK], BF16)]
         res_codes = sbuf("res_codes", [P, J], U32)
         res_scales = sbuf("res_scales", [P, J], U8)
+        ident = sbuf("ident", [P, P], F32)
         warm = sbuf("warm", [P, 2], F32)
 
         st_rows = st.rearrange("(p t) j -> p t j", t=PACK)
@@ -64,19 +65,12 @@ def tile_list_engram_addLP_kernel(
         out_rows = out_0.rearrange("(p t) j -> p t j", t=PACK)
         out_words = out_1[0].rearrange("p j i -> p (j i)").bitcast(I32)
         halves = [slice(h * HALF, (h + 1) * HALF) for h in range(2)]
+        blocks = [slice(e * P, (e + 1) * P) for e in range(HALF // P)]
 
         nc.gpsimd.memset(scale_win[:].bitcast(I32), 0)
+        make_identity(nc, ident[:])
         nc.vector.memset(warm[:, 0:1], 0.0)
         nc.scalar.activation(warm[:, 1:2], warm[:, 0:1], SIGMOID)
-
-        def load_w(w):
-            nc.sync.dma_start(w_raw[w][:], (wk, wv)[w].rearrange("(p i) c -> p i c", i=PACK))
-
-        def load_st(t):
-            nc.sync.dma_start(st_sb[t][:], st_rows[:, t, :])
-
-        def load_r(t):
-            nc.sync.dma_start(r_win[t][:], r_rows[:, t, :])
 
         nc.sync.dma_start(offsets[:], offs)
         for quad in range(P // QUADRANT):
@@ -85,16 +79,13 @@ def tile_list_engram_addLP_kernel(
                 tab_scales[0, 4 * quad : 4 * quad + 4, :].bitcast(I32),
             )
         nc.sync.dma_start(word_win[:], tab_words[0].rearrange("p t i -> p (t i)").bitcast(I32))
-        load_w(KEY)
-        load_w(VALUE)
-        load_st(0)
+        for w, weight in enumerate((wk, wv)):
+            nc.sync.dma_start(w_raw[w][:], weight.rearrange("(p i) c -> p i c", i=PACK))
+        nc.sync.dma_start(st_sb[0][:], st_rows[:, 0, :])
         for t in range(PACK):
-            if t + 1 < PACK:
-                load_st(t + 1)
-            load_r(t)
-
-        def entries(c0, c1):
-            return offsets[:, c0 // GROUP : c1 // GROUP]
+            if t < LAST:
+                nc.sync.dma_start(st_sb[t + 1][:], st_rows[:, t + 1, :])
+            nc.sync.dma_start(r_win[t][:], r_rows[:, t, :])
 
         def weave_w(w, m0, m1, copy):
             copy(
@@ -102,16 +93,13 @@ def tile_list_engram_addLP_kernel(
                 w_raw[w][:].rearrange("p i (m t) -> p m t i", t=PACK)[:, m0:m1],
             )
 
-        def quantise_w(w):
-            nc.vector.quantize_mx(out=w_codes[w][:].bitcast(FP8X4), scales=w_scales[w][:], in_=w_bf[w][:])
-
         def product(w, t, h):
-            acc = bank(f"acc{w}_{t}_{h}", BANKS[w][t][h])
-            rows = slice(t * P, (t + 1) * P)
+            acc = bank(f"acc{w}_{t}_{h}", w, t, h)
+            plane_cols = slice(t * P, (t + 1) * P)
             nc.tensor.matmul_mx(
                 out=acc[:],
-                lhsT=w_codes[w][:, rows].bitcast(FP8X4),
-                lhsT_scale=w_scales[w][:, rows],
+                lhsT=w_codes[w][:, plane_cols].bitcast(FP8X4),
+                lhsT_scale=w_scales[w][:, plane_cols],
                 rhs=tab_codes[:, halves[h]].bitcast(FP8X4),
                 rhs_scale=tab_sc[:, halves[h]],
                 start=True,
@@ -119,97 +107,130 @@ def tile_list_engram_addLP_kernel(
             )
             return acc
 
+        logit = {}
         gate = {}
-        logits = {}
         gated = {}
 
-        def gate_of(t, h, logit=None, pool_adds=False):
-            if logit is None:
-                logit = sbuf(f"logit{t}_{h}", [P, HALF], F32)
-            if not pool_adds:
-                nc.vector.tensor_tensor(logit[:], product(KEY, t, h)[:], st_sb[t][:, halves[h]], ADD)
-            else:
-                key = sbuf(f"key{t}_{h}", [P, HALF], F32)
-                nc.scalar.copy(key[:], product(KEY, t, h)[:])
-                nc.gpsimd.tensor_tensor(logit[:], key[:], st_sb[t][:, halves[h]], ADD)
-            logits[t, h] = logit
+        def logit_on_vector(t, h, place):
+            logit[t, h] = place
+            nc.vector.tensor_tensor(place, product(KEY, t, h)[:], st_sb[t][:, halves[h]], ADD)
 
-        def squash(t, h, tag=None):
+        def logit_on_gpsimd(t, h, place):
+            logit[t, h] = place
+            key = sbuf(f"key{t}_{h}", [P, HALF], F32)
+            nc.scalar.copy(key[:], product(KEY, t, h)[:])
+            nc.gpsimd.tensor_tensor(place, key[:], st_sb[t][:, halves[h]], ADD)
+
+        def logit_on_tensor(t, h):
+            plane_cols = slice(t * P, (t + 1) * P)
+            acc = bank(f"st_turning{t}", KEY, t, h)
+            for b in blocks:
+                nc.tensor.transpose(acc[:, b], st_sb[t][:, halves[h]][:, b], ident[:])
+            st_turned = sbuf(f"st_turned{t}", [P, HALF], F32)
+            nc.scalar.copy(st_turned[:], acc[:])
+            acc = bank(f"key_turning{t}", KEY, 1, 0)
+            for b in blocks:
+                nc.tensor.matmul_mx(
+                    out=acc[:, b],
+                    lhsT=tab_codes[:, halves[h]][:, b].bitcast(FP8X4),
+                    lhsT_scale=tab_sc[:, halves[h]][:, b],
+                    rhs=w_codes[KEY][:, plane_cols].bitcast(FP8X4),
+                    rhs_scale=w_scales[KEY][:, plane_cols],
+                    start=True,
+                    stop=True,
+                )
+            key_turned = sbuf(f"key_turned{t}", [P, HALF], F32)
+            nc.scalar.copy(key_turned[:], acc[:])
+            acc = bank(f"logit{t}", KEY, t, h)
+            turns = [(turned, b) for turned in (st_turned, key_turned) for b in blocks]
+            for step, (turned, b) in enumerate(turns):
+                nc.tensor.matmul(
+                    acc[:, b], turned[:, b], ident[:],
+                    start=(step == 0), stop=(step == len(turns) - 1), is_transpose=True,
+                )
+            logit[t, h] = acc[:]
+
+        def make_gate(t, h, tag=None):
             gate[t, h] = sbuf(f"gate{t}_{h}", [P, HALF], F32, tag=tag)
-            nc.scalar.activation(gate[t, h][:], logits[t, h][:], SIGMOID)
+            nc.scalar.activation(gate[t, h][:], logit[t, h], SIGMOID)
 
-        def gated_value(t, h, place=None):
-            if place is None:
-                place = sbuf(f"gated{t}_{h}", [P, HALF], F32, tag=f"gated{h}")[:]
-            gated[t, h] = place
-            nc.vector.tensor_tensor(place, product(VALUE, t, h)[:], gate[t, h][:], MULT)
+        def gate_values(t, first_place):
+            for h in range(2):
+                gated[t, h] = sbuf(f"gated{t}", [P, HALF], F32, tag="gated")[:] if h else first_place
+                nc.vector.tensor_tensor(gated[t, h], product(VALUE, t, h)[:], gate[t, h][:], MULT)
 
         def add_record(t, h, c0, c1):
-            plane = result[h][:, t * HALF + c0 : t * HALF + c1]
+            entries = offsets[:, (h * HALF + c0) // GROUP : (h * HALF + c1) // GROUP]
             nc.vector.tensor_tensor(
-                plane, r_win[t][:].indirect(entries(h * HALF + c0, h * HALF + c1)), gated[t, h][:, c0:c1], ADD
+                result[h][:, t * HALF + c0 : t * HALF + c1], r_win[t][:].indirect(entries), gated[t, h][:, c0:c1], ADD
             )
             if c1 == HALF:
                 nc.sync.dma_start(out_rows[:, t, halves[h]], result[h][:, t * HALF : (t + 1) * HALF])
 
-        def weave_pair(h, u, c0, c1, copy=nc.scalar.copy):
+        def weave_pair(woven, h, u, c0, c1, copy):
             planes = result[h][:, 2 * u * HALF : 2 * (u + 1) * HALF].rearrange("p (v j) -> p j v", v=2)
-            copy(res_bf[h][:].rearrange("p (j u v) -> p u j v", u=2, v=2)[:, u, c0:c1], planes[:, c0:c1])
+            pairs = woven[:, h * HALF * PACK : (h + 1) * HALF * PACK].rearrange("p (j u v) -> p u j v", u=2, v=2)
+            copy(pairs[:, u, c0:c1], planes[:, c0:c1])
 
-        def quantise_result(h, c0, c1):
-            cols = slice(h * HALF + c0, h * HALF + c1)
+        def quantise_quarter(woven, q):
+            cols = slice(q * QUARTER, (q + 1) * QUARTER)
             nc.vector.quantize_mx(
                 out=res_codes[:, cols].bitcast(FP8X4),
                 scales=res_scales[:, cols],
-                in_=res_bf[h][:, c0 * PACK : c1 * PACK],
+                in_=woven[:, q * QUARTER * PACK : (q + 1) * QUARTER * PACK],
             )
-            if c1 == HALF:
-                nc.sync.dma_start(out_words[:, halves[h]], res_codes[:, halves[h]].bitcast(I32))
+            if q % 2:
+                nc.sync.dma_start(out_words[:, halves[q // 2]], res_codes[:, halves[q // 2]].bitcast(I32))
 
         nc.vector.tensor_copy(tab_codes[:], word_win[:].bitcast(U32).indirect(offsets[:]))
         nc.vector.tensor_copy(tab_sc[:], scale_win[:].indirect(offsets[:]))
         for w in (KEY, VALUE):
             weave_w(w, 0, SCALAR_M[w], nc.scalar.copy)
-            if SCALAR_M[w] < P:
-                weave_w(w, SCALAR_M[w], P, nc.vector.tensor_copy)
-            quantise_w(w)
+            weave_w(w, SCALAR_M[w], P, nc.vector.tensor_copy)
+            nc.vector.quantize_mx(out=w_codes[w][:].bitcast(FP8X4), scales=w_scales[w][:], in_=w_bf[w][:])
+
         early = sbuf("early_logits", [P, 3 * HALF], F32, tag=f"w_bf{VALUE}")
-        gate_of(0, 0, early[:, halves[0]])
-        squash(0, 0)
-        gate_of(1, 1, early[:, J:], True)
-        gate_of(0, 1, early[:, halves[1]])
-        squash(0, 1)
-        parked = PACK * HALF - QUARTER
-        for t in range(PACK - 1):
-            at = parked - (2 - t) * QUARTER
-            gated_value(t, 0, result[1][:, at : at + HALF])
-            gated_value(t, 1)
+        logit_on_vector(0, 0, early[:, halves[0]])
+        make_gate(0, 0)
+        logit_on_gpsimd(1, 1, early[:, J:])
+        logit_on_vector(0, 1, early[:, halves[1]])
+        make_gate(0, 1)
+
+        def window(t):
+            return PACK * HALF - (LAST - 1 - min(t, LAST - 1)) * QUARTER
+
+        for t in range(LAST):
+            at = window(t)
+            gate_values(t, result[1][:, at : at + HALF])
             if t == 0:
-                gate_of(1, 0)
+                logit_on_vector(1, 0, sbuf("logit1_0", [P, HALF], F32)[:])
             else:
-                gate_of(t + 1, 0, sbuf(f"held{t}", [P, HALF], F32, tag=f"r_win{t - 1}")[:])
-                gate_of(t + 1, 1, result[1][:, at - HALF : at], True)
-            squash(t + 1, 1, f"gate{t}_0")
-            squash(t + 1, 0)
-            add_record(t, 0, 0, HALF)
-            if t == 1:
-                weave_pair(0, 0, 0, HALF)
-            add_record(t, 1, 0, HALF)
-        last = PACK - 1
-        gated_value(last, 0, result[1][:, PACK * HALF :])
-        gated_value(last, 1)
-        res_bf.append(sbuf("res_bf1", [P, HALF * PACK], BF16, tag="r_win1"))
-        weave_pair(1, 0, 0, HALF)
+                logit_on_tensor(t + 1, 0)
+                logit_on_gpsimd(t + 1, 1, result[1][:, at - HALF : at])
+            if t + 1 < LAST:
+                make_gate(t + 1, 1, tag=f"gate{t}_0")
+                make_gate(t + 1, 0)
+            else:
+                make_gate(LAST, 0)
+                make_gate(LAST, 1, tag=f"st_turned{LAST}")
+            for h in range(2):
+                add_record(t, h, 0, HALF)
+
+        at = window(LAST)
+        gate_values(LAST, result[1][:, at : at + HALF])
+        woven = sbuf("woven", [P, J * PACK], BF16, tag=f"key_turned{LAST}")
         for h in range(2):
-            for c0 in (0, QUARTER):
-                add_record(last, h, c0, c0 + QUARTER)
-                if (h, c0) != (1, QUARTER):
-                    weave_pair(h, 1, c0, c0 + QUARTER)
-        quantise_result(0, 0, QUARTER)
-        quantise_result(0, QUARTER, HALF)
-        weave_pair(1, 1, QUARTER, HALF, nc.vector.tensor_copy)
-        quantise_result(1, 0, QUARTER)
-        quantise_result(1, QUARTER, HALF)
+            weave_pair(woven, h, 0, 0, HALF, nc.scalar.copy)
+        quarters = [(h, c0) for h in range(2) for c0 in (0, QUARTER)]
+        for h, c0 in quarters:
+            add_record(LAST, h, c0, c0 + QUARTER)
+            if (h, c0) != quarters[-1]:
+                weave_pair(woven, h, 1, c0, c0 + QUARTER, nc.scalar.copy)
+        quantise_quarter(woven, 0)
+        quantise_quarter(woven, 1)
+        weave_pair(woven, 1, 1, QUARTER, HALF, nc.vector.tensor_copy)
+        quantise_quarter(woven, 2)
+        quantise_quarter(woven, 3)
         for quad in range(P // QUADRANT):
             queue = nc.sync if quad % 2 else nc.scalar
             queue.dma_start(

@@ -1,7 +1,6 @@
 from contextlib import ExitStack
 
 import concourse.mybir as mybir
-from concourse.masks import make_identity
 
 K, N, T, J = 512, 512, 2048, 1024
 FLOPS = 2 * 2 * K * N * J
@@ -25,7 +24,7 @@ HALF = J // 2
 QUARTER = J // 4
 LAST = PACK - 1
 KEY, VALUE = 0, 1
-SCALAR_M = (96, 88)
+SCALAR_M = 56
 
 
 def tile_list_engram_addLP_kernel(
@@ -34,31 +33,29 @@ def tile_list_engram_addLP_kernel(
     nc = tc.nc
     with ExitStack() as ctx:
         keep = ctx.enter_context(tc.tile_pool(name="keep", bufs=1))
+        loads = ctx.enter_context(tc.tile_pool(name="loads", bufs=1))
         psum = ctx.enter_context(tc.psum_pool(name="psum", bufs=1))
 
         def sbuf(name, shape, dtype, tag=None):
             return keep.tile(shape, dtype, name=name, tag=tag or name, align_bytes=64)
 
-        def bank(name, w, t, h):
-            number = 4 * ((w + t // 2) % 2) + 2 * (t % 2) + h
+        def bank(name, number):
             return psum.tile([P, HALF], F32, name=name, tag=f"bank{number}")
 
         offsets = keep.tile([P, J // GROUP], U16, name="offsets")
         scale_win = sbuf("scale_win", [P, T], U8)
-        word_win = sbuf("word_win", [P, T], I32)
-        w_raw = [sbuf(f"w_raw{w}", [P, PACK, N], F32) for w in (KEY, VALUE)]
-        w_bf = [sbuf(f"w_bf{w}", [P, N * PACK], BF16) for w in (KEY, VALUE)]
         w_codes = [sbuf(f"w_codes{w}", [P, N], U32) for w in (KEY, VALUE)]
         w_scales = [sbuf(f"w_scales{w}", [P, N], U8) for w in (KEY, VALUE)]
-        st_sb = [sbuf(f"st{t}", [P, J], F32) for t in range(PACK)]
-        r_win = [sbuf(f"r_win{t}", [P, T], F32) for t in range(PACK)]
         tab_codes = sbuf("tab_codes", [P, J], U32)
         tab_sc = sbuf("tab_sc", [P, J], U8)
-        result = [sbuf(f"result{h}", [P, (PACK + h) * HALF], F32) for h in range(2)]
+        result = sbuf("result", [P, PACK * J], F32)
+        parked = sbuf("parked", [P, 5 * QUARTER], F32)
         res_codes = sbuf("res_codes", [P, J], U32)
         res_scales = sbuf("res_scales", [P, J], U8)
         ident = sbuf("ident", [P, P], F32)
         warm = sbuf("warm", [P, 2], F32)
+        held_floats = T + PACK * (N + J + T)
+        zeros = loads.tile([P, held_floats], F32, name="zeros", tag="zeros", offset=0)
 
         st_rows = st.rearrange("(p t) j -> p t j", t=PACK)
         r_rows = rT.rearrange("(p t) c -> p t c", t=PACK)
@@ -68,33 +65,59 @@ def tile_list_engram_addLP_kernel(
         blocks = [slice(e * P, (e + 1) * P) for e in range(HALF // P)]
 
         nc.gpsimd.memset(scale_win[:].bitcast(I32), 0)
-        make_identity(nc, ident[:])
-        nc.vector.memset(warm[:, 0:1], 0.0)
-        nc.scalar.activation(warm[:, 1:2], warm[:, 0:1], SIGMOID)
+        nc.gpsimd.memset(warm[:, 0:1], 0.0)
+        nc.gpsimd.memset(zeros[:, :P], 0.0)
+        nc.gpsimd.affine_select(
+            out=ident[:], in_=zeros[:, :P], compare_op=mybir.AluOpType.not_equal, fill=1.0, base=0,
+            pattern=[[-1, P]], channel_multiplier=1,
+        )
+
+        def held(name, shape, dtype, first_float):
+            return loads.tile(shape, dtype, name=name, tag=name, offset=4 * first_float)
+
+        word_win = held("word_win", [P, T], I32, 0)
+        wv_raw = held("wv_raw", [P, PACK, N], F32, T)
+        st_at = T + PACK * N
+        st_sb = [held(f"st{t}", [P, J], F32, st_at + J * t) for t in range(LAST)]
+        st_last = [held(f"st{LAST}_{h}", [P, HALF], F32, st_at + J * LAST + HALF * h) for h in range(2)]
+        st_half = {(t, h): st_sb[t][:, halves[h]] for t in range(LAST) for h in range(2)}
+        for h in range(2):
+            st_half[LAST, h] = st_last[h][:]
+        r_win = [held(f"r_win{t}", [P, T], F32, T + PACK * (N + J) + T * t) for t in range(PACK)]
+        wk_raw = held("wk_raw", [P, PACK, N], F32, T + PACK * (N + J + T))
+        w_raw = [wk_raw, wv_raw]
 
         nc.sync.dma_start(offsets[:], offs)
         for quad in range(P // QUADRANT):
-            nc.sync.dma_start(
+            nc.scalar.dma_start(
                 scale_win[QUADRANT * quad : QUADRANT * quad + 4, :].bitcast(I32),
                 tab_scales[0, 4 * quad : 4 * quad + 4, :].bitcast(I32),
             )
+        nc.scalar.activation(warm[:, 1:2], warm[:, 0:1], SIGMOID)
+        nc.sync.dma_start(wk_raw[:], wk.rearrange("(p i) c -> p i c", i=PACK))
         nc.sync.dma_start(word_win[:], tab_words[0].rearrange("p t i -> p (t i)").bitcast(I32))
-        for w, weight in enumerate((wk, wv)):
-            nc.sync.dma_start(w_raw[w][:], weight.rearrange("(p i) c -> p i c", i=PACK))
+        nc.sync.dma_start(wv_raw[:], wv.rearrange("(p i) c -> p i c", i=PACK))
         nc.sync.dma_start(st_sb[0][:], st_rows[:, 0, :])
         for t in range(PACK):
-            if t < LAST:
+            if t + 1 < LAST:
                 nc.sync.dma_start(st_sb[t + 1][:], st_rows[:, t + 1, :])
+            elif t < LAST:
+                for h in range(2):
+                    nc.sync.dma_start(st_half[LAST, h], st_rows[:, LAST, halves[h]])
             nc.sync.dma_start(r_win[t][:], r_rows[:, t, :])
 
-        def weave_w(w, m0, m1, copy):
+        def weave_w(w, woven_w, t0, t1, m0, m1, copy):
             copy(
-                w_bf[w][:].rearrange("p (t m i) -> p m t i", t=PACK, i=PACK)[:, m0:m1],
-                w_raw[w][:].rearrange("p i (m t) -> p m t i", t=PACK)[:, m0:m1],
+                woven_w[:].rearrange("p (t m i) -> p m t i", t=t1 - t0, i=PACK)[:, m0:m1],
+                w_raw[w][:].rearrange("p i (m t) -> p m t i", t=PACK)[:, m0:m1, t0:t1],
             )
 
-        def product(w, t, h):
-            acc = bank(f"acc{w}_{t}_{h}", w, t, h)
+        def quantise_w(w, woven_w, t0, t1):
+            cols = slice(t0 * P, t1 * P)
+            nc.vector.quantize_mx(out=w_codes[w][:, cols].bitcast(FP8X4), scales=w_scales[w][:, cols], in_=woven_w[:])
+
+        def product(w, t, h, number):
+            acc = bank(f"acc{w}_{t}_{h}", number)
             plane_cols = slice(t * P, (t + 1) * P)
             nc.tensor.matmul_mx(
                 out=acc[:],
@@ -110,127 +133,157 @@ def tile_list_engram_addLP_kernel(
         logit = {}
         gate = {}
         gated = {}
+        key = {}
+        turned = {}
+        value = {}
 
-        def logit_on_vector(t, h, place):
-            logit[t, h] = place
-            nc.vector.tensor_tensor(place, product(KEY, t, h)[:], st_sb[t][:, halves[h]], ADD)
+        def copy_key(t, h, number):
+            if t == 1:
+                key[t, h] = held(f"key{t}_{h}", [P, HALF], F32, T + J + h * HALF)
+            else:
+                key[t, h] = sbuf(f"key{t}_{h}", [P, HALF], F32)
+            nc.scalar.copy(key[t, h][:], product(KEY, t, h, number)[:])
 
         def logit_on_gpsimd(t, h, place):
             logit[t, h] = place
-            key = sbuf(f"key{t}_{h}", [P, HALF], F32)
-            nc.scalar.copy(key[:], product(KEY, t, h)[:])
-            nc.gpsimd.tensor_tensor(place, key[:], st_sb[t][:, halves[h]], ADD)
+            nc.gpsimd.tensor_tensor(place, key[t, h][:], st_half[t, h], ADD)
 
-        def logit_on_tensor(t, h):
+        def turn_key(t, number):
             plane_cols = slice(t * P, (t + 1) * P)
-            acc = bank(f"st_turning{t}", KEY, t, h)
-            for b in blocks:
-                nc.tensor.transpose(acc[:, b], st_sb[t][:, halves[h]][:, b], ident[:])
-            st_turned = sbuf(f"st_turned{t}", [P, HALF], F32)
-            nc.scalar.copy(st_turned[:], acc[:])
-            acc = bank(f"key_turning{t}", KEY, 1, 0)
+            acc = bank(f"key_turning{t}", number)
             for b in blocks:
                 nc.tensor.matmul_mx(
                     out=acc[:, b],
-                    lhsT=tab_codes[:, halves[h]][:, b].bitcast(FP8X4),
-                    lhsT_scale=tab_sc[:, halves[h]][:, b],
+                    lhsT=tab_codes[:, b].bitcast(FP8X4),
+                    lhsT_scale=tab_sc[:, b],
                     rhs=w_codes[KEY][:, plane_cols].bitcast(FP8X4),
                     rhs_scale=w_scales[KEY][:, plane_cols],
                     start=True,
                     stop=True,
                 )
-            key_turned = sbuf(f"key_turned{t}", [P, HALF], F32)
-            nc.scalar.copy(key_turned[:], acc[:])
-            acc = bank(f"logit{t}", KEY, t, h)
-            turns = [(turned, b) for turned in (st_turned, key_turned) for b in blocks]
-            for step, (turned, b) in enumerate(turns):
+            turned[KEY, t] = sbuf(f"key_turned{t}", [P, HALF], F32)
+            nc.scalar.copy(turned[KEY, t][:], acc[:])
+
+        def logit_on_tensor(t):
+            acc = bank(f"st_turning{t}", 2)
+            for b in blocks:
+                nc.tensor.transpose(acc[:, b], st_half[t, 0][:, b], ident[:])
+            st_turned = sbuf(f"st_turned{t}", [P, HALF], F32)
+            nc.scalar.copy(st_turned[:], acc[:])
+            acc = bank(f"logit{t}", 3)
+            turns = [(src, b) for src in (turned[KEY, t], st_turned) for b in blocks]
+            for step, (src, b) in enumerate(turns):
                 nc.tensor.matmul(
-                    acc[:, b], turned[:, b], ident[:],
+                    acc[:, b], src[:, b], ident[:],
                     start=(step == 0), stop=(step == len(turns) - 1), is_transpose=True,
                 )
-            logit[t, h] = acc[:]
+            logit[t, 0] = acc[:]
 
-        def make_gate(t, h, tag=None):
-            gate[t, h] = sbuf(f"gate{t}_{h}", [P, HALF], F32, tag=tag)
+        def make_gate(t, h):
+            gate[t, h] = sbuf(f"gate{t}_{h}", [P, HALF], F32)
             nc.scalar.activation(gate[t, h][:], logit[t, h], SIGMOID)
 
-        def gate_values(t, first_place):
+        def window(t):
+            return (1 + min(t, LAST - 1)) * QUARTER
+
+        def gate_values(t):
+            at = window(t)
             for h in range(2):
-                gated[t, h] = sbuf(f"gated{t}", [P, HALF], F32, tag="gated")[:] if h else first_place
-                nc.vector.tensor_tensor(gated[t, h], product(VALUE, t, h)[:], gate[t, h][:], MULT)
+                gated[t, h] = sbuf(f"gated{t}", [P, HALF], F32, tag="gated")[:] if h else parked[:, at : at + HALF]
+                nc.vector.tensor_tensor(gated[t, h], value[t, h][:], gate[t, h][:], MULT)
 
-        def add_record(t, h, c0, c1):
-            entries = offsets[:, (h * HALF + c0) // GROUP : (h * HALF + c1) // GROUP]
+        def add_record(t, c0, c1):
+            h = c0 // HALF
             nc.vector.tensor_tensor(
-                result[h][:, t * HALF + c0 : t * HALF + c1], r_win[t][:].indirect(entries), gated[t, h][:, c0:c1], ADD
+                result[:, t * J + c0 : t * J + c1],
+                r_win[t][:].indirect(offsets[:, c0 // GROUP : c1 // GROUP]),
+                gated[t, h][:, c0 - h * HALF : c1 - h * HALF],
+                ADD,
             )
-            if c1 == HALF:
-                nc.sync.dma_start(out_rows[:, t, halves[h]], result[h][:, t * HALF : (t + 1) * HALF])
 
-        def weave_pair(woven, h, u, c0, c1, copy):
-            planes = result[h][:, 2 * u * HALF : 2 * (u + 1) * HALF].rearrange("p (v j) -> p j v", v=2)
-            pairs = woven[:, h * HALF * PACK : (h + 1) * HALF * PACK].rearrange("p (j u v) -> p u j v", u=2, v=2)
-            copy(pairs[:, u, c0:c1], planes[:, c0:c1])
+        def store_rows(t, c0, c1):
+            nc.sync.dma_start(out_rows[:, t, c0:c1], result[:, t * J + c0 : t * J + c1])
 
-        def quantise_quarter(woven, q):
+        def weave_pair(u, c0, c1, copy):
+            h = c0 // HALF
+            planes = result[:, 2 * u * J : 2 * (u + 1) * J].rearrange("p (v j) -> p j v", v=2)
+            pairs = woven[h][:].rearrange("p (j u v) -> p u j v", u=2, v=2)
+            copy(pairs[:, u, c0 - h * HALF : c1 - h * HALF], planes[:, c0:c1])
+
+        def quantise_quarter(q):
             cols = slice(q * QUARTER, (q + 1) * QUARTER)
             nc.vector.quantize_mx(
                 out=res_codes[:, cols].bitcast(FP8X4),
                 scales=res_scales[:, cols],
-                in_=woven[:, q * QUARTER * PACK : (q + 1) * QUARTER * PACK],
+                in_=woven[q // 2][:, (q % 2) * QUARTER * PACK : (q % 2 + 1) * QUARTER * PACK],
             )
             if q % 2:
                 nc.sync.dma_start(out_words[:, halves[q // 2]], res_codes[:, halves[q // 2]].bitcast(I32))
 
-        nc.vector.tensor_copy(tab_codes[:], word_win[:].bitcast(U32).indirect(offsets[:]))
         nc.vector.tensor_copy(tab_sc[:], scale_win[:].indirect(offsets[:]))
-        for w in (KEY, VALUE):
-            weave_w(w, 0, SCALAR_M[w], nc.scalar.copy)
-            weave_w(w, SCALAR_M[w], P, nc.vector.tensor_copy)
-            nc.vector.quantize_mx(out=w_codes[w][:].bitcast(FP8X4), scales=w_scales[w][:], in_=w_bf[w][:])
-
-        early = sbuf("early_logits", [P, 3 * HALF], F32, tag=f"w_bf{VALUE}")
-        logit_on_vector(0, 0, early[:, halves[0]])
-        make_gate(0, 0)
-        logit_on_gpsimd(1, 1, early[:, J:])
-        logit_on_vector(0, 1, early[:, halves[1]])
-        make_gate(0, 1)
-
-        def window(t):
-            return PACK * HALF - (LAST - 1 - min(t, LAST - 1)) * QUARTER
-
-        for t in range(LAST):
-            at = window(t)
-            gate_values(t, result[1][:, at : at + HALF])
-            if t == 0:
-                logit_on_vector(1, 0, sbuf("logit1_0", [P, HALF], F32)[:])
-            else:
-                logit_on_tensor(t + 1, 0)
-                logit_on_gpsimd(t + 1, 1, result[1][:, at - HALF : at])
-            if t + 1 < LAST:
-                make_gate(t + 1, 1, tag=f"gate{t}_0")
-                make_gate(t + 1, 0)
-            else:
-                make_gate(LAST, 0)
-                make_gate(LAST, 1, tag=f"st_turned{LAST}")
-            for h in range(2):
-                add_record(t, h, 0, HALF)
-
-        at = window(LAST)
-        gate_values(LAST, result[1][:, at : at + HALF])
-        woven = sbuf("woven", [P, J * PACK], BF16, tag=f"key_turned{LAST}")
+        wk_low = sbuf("wk_low", [P, 2 * P * PACK], BF16)
+        wk_high = sbuf("wk_high", [P, 2 * P * PACK], BF16, tag="scale_win")
+        weave_w(KEY, wk_low, 0, 2, 0, P, nc.scalar.copy)
+        weave_w(KEY, wk_high, 2, PACK, 0, P, nc.vector.tensor_copy)
+        quantise_w(KEY, wk_low, 0, 2)
+        quantise_w(KEY, wk_high, 2, PACK)
         for h in range(2):
-            weave_pair(woven, h, 0, 0, HALF, nc.scalar.copy)
-        quarters = [(h, c0) for h in range(2) for c0 in (0, QUARTER)]
-        for h, c0 in quarters:
-            add_record(LAST, h, c0, c0 + QUARTER)
-            if (h, c0) != quarters[-1]:
-                weave_pair(woven, h, 1, c0, c0 + QUARTER, nc.scalar.copy)
-        quantise_quarter(woven, 0)
-        quantise_quarter(woven, 1)
-        weave_pair(woven, 1, 1, QUARTER, HALF, nc.vector.tensor_copy)
-        quantise_quarter(woven, 2)
-        quantise_quarter(woven, 3)
+            entries = offsets[:, h * HALF // GROUP : (h + 1) * HALF // GROUP]
+            nc.vector.tensor_copy(tab_codes[:, halves[h]], word_win[:].bitcast(U32).indirect(entries))
+        wv_bf = sbuf("wv_bf", [P, N * PACK], BF16)
+        weave_w(VALUE, wv_bf, 0, PACK, 0, SCALAR_M, nc.scalar.copy)
+        weave_w(VALUE, wv_bf, 0, PACK, SCALAR_M, P, nc.vector.tensor_copy)
+        quantise_w(VALUE, wv_bf, 0, PACK)
+
+        copy_key(1, 0, 2)
+        copy_key(1, 1, 3)
+        on_vector = held("logits0", [P, J], F32, T)
+        on_gpsimd = sbuf("logits1", [P, J], F32, tag="wv_bf")
+        for h in range(2):
+            logit[0, h] = on_vector[:, halves[h]]
+            nc.vector.tensor_tensor(logit[0, h], product(KEY, 0, h, h)[:], st_half[0, h], ADD)
+            logit_on_gpsimd(1, h, on_gpsimd[:, halves[h]])
+        for t in range(2):
+            for h in range(2):
+                value[t, h] = product(VALUE, t, h, 4 + 2 * t + h)
+                make_gate(t, h)
+        gate_values(0)
+        for t in (2, 3):
+            copy_key(t, 1, t - 2)
+            turn_key(t, t)
+        for h in range(2):
+            value[2, h] = product(VALUE, 2, h, 4 + h)
+            value[3, h] = product(VALUE, 3, h, h)
+
+        woven = []
+        for t in range(LAST):
+            if t:
+                gate_values(t)
+                logit_on_tensor(t + 1)
+                at = window(t)
+                logit_on_gpsimd(t + 1, 1, parked[:, at - HALF : at])
+                make_gate(t + 1, 0)
+                make_gate(t + 1, 1)
+            for h in range(2):
+                add_record(t, h * HALF, (h + 1) * HALF)
+            store_rows(t, 0, J)
+
+        woven.append(held("woven0", [P, HALF * PACK], BF16, st_at + J * LAST - HALF))
+        woven.append(sbuf("woven1", [P, HALF * PACK], BF16, tag=f"key_turned{LAST}"))
+        for h in range(2):
+            weave_pair(0, h * HALF, (h + 1) * HALF, nc.scalar.copy)
+        gate_values(LAST)
+        for q in range(4):
+            add_record(LAST, q * QUARTER, (q + 1) * QUARTER)
+            if q % 2:
+                store_rows(LAST, (q - 1) * QUARTER, (q + 1) * QUARTER)
+            if q < 3:
+                weave_pair(1, q * QUARTER, (q + 1) * QUARTER, nc.scalar.copy)
+        quantise_quarter(0)
+        quantise_quarter(1)
+        weave_pair(1, 3 * QUARTER, J, nc.vector.tensor_copy)
+        quantise_quarter(2)
+        quantise_quarter(3)
         for quad in range(P // QUADRANT):
             queue = nc.sync if quad % 2 else nc.scalar
             queue.dma_start(

@@ -24,7 +24,7 @@ HALF = J // 2
 QUARTER = J // 4
 LAST = PACK - 1
 KEY, VALUE = 0, 1
-SCALAR_M = 56
+SCALAR_M = 100
 
 
 def tile_list_engram_addLP_kernel(
@@ -43,10 +43,7 @@ def tile_list_engram_addLP_kernel(
             return psum.tile([P, HALF], F32, name=name, tag=f"bank{number}")
 
         offsets = keep.tile([P, J // GROUP], U16, name="offsets")
-        scale_win = sbuf("scale_win", [P, T], U8)
         w_codes = [sbuf(f"w_codes{w}", [P, N], U32) for w in (KEY, VALUE)]
-        w_scales = [sbuf(f"w_scales{w}", [P, N], U8) for w in (KEY, VALUE)]
-        tab_codes = sbuf("tab_codes", [P, J], U32)
         tab_sc = sbuf("tab_sc", [P, J], U8)
         result = sbuf("result", [P, PACK * J], F32)
         parked = sbuf("parked", [P, 5 * QUARTER], F32)
@@ -55,8 +52,10 @@ def tile_list_engram_addLP_kernel(
         ident = sbuf("ident", [P, P], F32)
         warm = sbuf("warm", [P, 2], F32)
         held_floats = T + PACK * (N + J + T)
-        zeros = loads.tile([P, held_floats], F32, name="zeros", tag="zeros", offset=0)
+        zeros = sbuf("zeros", [P, P], F32)
 
+        scale_at = 4 * (T + PACK * (2 * N + J + T))
+        scale_win = loads.tile([P, T], U8, name="scale_win", tag="scale_win", offset=scale_at, align_bytes=64)
         st_rows = st.rearrange("(p t) j -> p t j", t=PACK)
         r_rows = rT.rearrange("(p t) c -> p t c", t=PACK)
         out_rows = out_0.rearrange("(p t) j -> p t j", t=PACK)
@@ -89,7 +88,7 @@ def tile_list_engram_addLP_kernel(
 
         nc.sync.dma_start(offsets[:], offs)
         for quad in range(P // QUADRANT):
-            nc.scalar.dma_start(
+            nc.sync.dma_start(
                 scale_win[QUADRANT * quad : QUADRANT * quad + 4, :].bitcast(I32),
                 tab_scales[0, 4 * quad : 4 * quad + 4, :].bitcast(I32),
             )
@@ -141,7 +140,7 @@ def tile_list_engram_addLP_kernel(
             if t == 1:
                 key[t, h] = held(f"key{t}_{h}", [P, HALF], F32, T + J + h * HALF)
             else:
-                key[t, h] = sbuf(f"key{t}_{h}", [P, HALF], F32)
+                key[t, h] = held(f"key{t}_{h}", [P, HALF], F32, T + (t - 2) * HALF)
             nc.scalar.copy(key[t, h][:], product(KEY, t, h, number)[:])
 
         def logit_on_gpsimd(t, h, place):
@@ -221,12 +220,12 @@ def tile_list_engram_addLP_kernel(
                 nc.sync.dma_start(out_words[:, halves[q // 2]], res_codes[:, halves[q // 2]].bitcast(I32))
 
         nc.vector.tensor_copy(tab_sc[:], scale_win[:].indirect(offsets[:]))
-        wk_low = sbuf("wk_low", [P, 2 * P * PACK], BF16)
-        wk_high = sbuf("wk_high", [P, 2 * P * PACK], BF16, tag="scale_win")
-        weave_w(KEY, wk_low, 0, 2, 0, P, nc.scalar.copy)
-        weave_w(KEY, wk_high, 2, PACK, 0, P, nc.vector.tensor_copy)
-        quantise_w(KEY, wk_low, 0, 2)
-        quantise_w(KEY, wk_high, 2, PACK)
+        tab_codes = loads.tile([P, J], U32, name="tab_codes", tag="tab_codes", offset=scale_at + N, align_bytes=64)
+        wk_scales = loads.tile([P, N], U8, name="wk_scales", tag="wk_scales", offset=scale_at, align_bytes=64)
+        w_scales = [wk_scales, sbuf("wv_scales", [P, N], U8)]
+        wk_bf = sbuf("wk_bf", [P, N * PACK], BF16)
+        weave_w(KEY, wk_bf, 0, PACK, 0, P, nc.scalar.copy)
+        quantise_w(KEY, wk_bf, 0, PACK)
         for h in range(2):
             entries = offsets[:, h * HALF // GROUP : (h + 1) * HALF // GROUP]
             nc.vector.tensor_copy(tab_codes[:, halves[h]], word_win[:].bitcast(U32).indirect(entries))
@@ -235,14 +234,15 @@ def tile_list_engram_addLP_kernel(
         weave_w(VALUE, wv_bf, 0, PACK, SCALAR_M, P, nc.vector.tensor_copy)
         quantise_w(VALUE, wv_bf, 0, PACK)
 
+        first_key = product(KEY, 0, 0, 0)
         copy_key(1, 0, 2)
-        copy_key(1, 1, 3)
-        on_vector = held("logits0", [P, J], F32, T)
         on_gpsimd = sbuf("logits1", [P, J], F32, tag="wv_bf")
         for h in range(2):
-            logit[0, h] = on_vector[:, halves[h]]
-            nc.vector.tensor_tensor(logit[0, h], product(KEY, 0, h, h)[:], st_half[0, h], ADD)
-            logit_on_gpsimd(1, h, on_gpsimd[:, halves[h]])
+            logit[0, h] = held(f"logit0_{h}", [P, HALF], F32, h * (T + QUARTER))[:]
+            nc.vector.tensor_tensor(logit[0, h], (product(KEY, 0, h, h) if h else first_key)[:], st_half[0, h], ADD)
+        logit_on_gpsimd(1, 0, on_gpsimd[:, halves[0]])
+        logit[1, 1] = held("logit1_1", [P, HALF], F32, T + J + HALF)[:]
+        nc.vector.tensor_tensor(logit[1, 1], product(KEY, 1, 1, 3)[:], st_half[1, 1], ADD)
         for t in range(2):
             for h in range(2):
                 value[t, h] = product(VALUE, t, h, 4 + 2 * t + h)

@@ -24,7 +24,7 @@ HALF = J // 2
 QUARTER = J // 4
 LAST = PACK - 1
 KEY, VALUE = 0, 1
-SCALAR_M = 100
+SCALAR_M = 92
 
 
 def tile_list_engram_addLP_kernel(
@@ -122,7 +122,7 @@ def tile_list_engram_addLP_kernel(
                 out=acc[:],
                 lhsT=w_codes[w][:, plane_cols].bitcast(FP8X4),
                 lhsT_scale=w_scales[w][:, plane_cols],
-                rhs=tab_codes[:, halves[h]].bitcast(FP8X4),
+                rhs=tab_codes[h][:].bitcast(FP8X4),
                 rhs_scale=tab_sc[:, halves[h]],
                 start=True,
                 stop=True,
@@ -153,7 +153,7 @@ def tile_list_engram_addLP_kernel(
             for b in blocks:
                 nc.tensor.matmul_mx(
                     out=acc[:, b],
-                    lhsT=tab_codes[:, b].bitcast(FP8X4),
+                    lhsT=tab_codes[0][:, b].bitcast(FP8X4),
                     lhsT_scale=tab_sc[:, b],
                     rhs=w_codes[KEY][:, plane_cols].bitcast(FP8X4),
                     rhs_scale=w_scales[KEY][:, plane_cols],
@@ -219,16 +219,20 @@ def tile_list_engram_addLP_kernel(
             if q % 2:
                 nc.sync.dma_start(out_words[:, halves[q // 2]], res_codes[:, halves[q // 2]].bitcast(I32))
 
+        def gather_words(h):
+            entries = offsets[:, h * HALF // GROUP : (h + 1) * HALF // GROUP]
+            nc.vector.tensor_copy(tab_codes[h][:], word_win[:].bitcast(U32).indirect(entries))
+
         nc.vector.tensor_copy(tab_sc[:], scale_win[:].indirect(offsets[:]))
-        tab_codes = loads.tile([P, J], U32, name="tab_codes", tag="tab_codes", offset=scale_at + N, align_bytes=64)
-        wk_scales = loads.tile([P, N], U8, name="wk_scales", tag="wk_scales", offset=scale_at, align_bytes=64)
+        tab_codes = [loads.tile([P, HALF], U32, name="codes0", tag="codes0", offset=scale_at + 64 + N, align_bytes=64)]
+        wk_scales = loads.tile([P, N], U8, name="wk_scales", tag="wk_scales", offset=scale_at + 64, align_bytes=64)
         w_scales = [wk_scales, sbuf("wv_scales", [P, N], U8)]
+        gather_words(0)
         wk_bf = sbuf("wk_bf", [P, N * PACK], BF16)
         weave_w(KEY, wk_bf, 0, PACK, 0, P, nc.scalar.copy)
         quantise_w(KEY, wk_bf, 0, PACK)
-        for h in range(2):
-            entries = offsets[:, h * HALF // GROUP : (h + 1) * HALF // GROUP]
-            nc.vector.tensor_copy(tab_codes[:, halves[h]], word_win[:].bitcast(U32).indirect(entries))
+        tab_codes.append(loads.tile([P, HALF], U32, name="codes1", tag="codes1", offset=scale_at + 64 - 4 * HALF, align_bytes=64))
+        gather_words(1)
         wv_bf = sbuf("wv_bf", [P, N * PACK], BF16)
         weave_w(VALUE, wv_bf, 0, PACK, 0, SCALAR_M, nc.scalar.copy)
         weave_w(VALUE, wv_bf, 0, PACK, SCALAR_M, P, nc.vector.tensor_copy)

@@ -24,7 +24,7 @@ HALF = J // 2
 QUARTER = J // 4
 LAST = PACK - 1
 KEY, VALUE = 0, 1
-SCALAR_M = 92
+SCALAR_M = 84
 
 
 def tile_list_engram_addLP_kernel(
@@ -45,16 +45,18 @@ def tile_list_engram_addLP_kernel(
         offsets = keep.tile([P, J // GROUP], U16, name="offsets")
         w_codes = [sbuf(f"w_codes{w}", [P, N], U32) for w in (KEY, VALUE)]
         tab_sc = sbuf("tab_sc", [P, J], U8)
-        result = sbuf("result", [P, PACK * J], F32)
-        parked = sbuf("parked", [P, 5 * QUARTER], F32)
         res_codes = sbuf("res_codes", [P, J], U32)
         res_scales = sbuf("res_scales", [P, J], U8)
         ident = sbuf("ident", [P, P], F32)
         warm = sbuf("warm", [P, 2], F32)
-        held_floats = T + PACK * (N + J + T)
         zeros = sbuf("zeros", [P, P], F32)
 
-        scale_at = 4 * (T + PACK * (2 * N + J + T))
+        result_at = T + 5 * QUARTER
+        wv_at = result_at + PACK * J - 64
+        st_at = wv_at + PACK * N
+        r_at = st_at + PACK * J
+        wk_at = r_at + PACK * T
+        scale_at = 4 * (wk_at + PACK * N)
         scale_win = loads.tile([P, T], U8, name="scale_win", tag="scale_win", offset=scale_at, align_bytes=64)
         st_rows = st.rearrange("(p t) j -> p t j", t=PACK)
         r_rows = rT.rearrange("(p t) c -> p t c", t=PACK)
@@ -75,15 +77,15 @@ def tile_list_engram_addLP_kernel(
             return loads.tile(shape, dtype, name=name, tag=name, offset=4 * first_float)
 
         word_win = held("word_win", [P, T], I32, 0)
-        wv_raw = held("wv_raw", [P, PACK, N], F32, T)
-        st_at = T + PACK * N
+        wv_raw = held("wv_raw", [P, PACK, N], F32, wv_at)
+        result = held("result", [P, PACK * J], F32, result_at)
         st_sb = [held(f"st{t}", [P, J], F32, st_at + J * t) for t in range(LAST)]
         st_last = [held(f"st{LAST}_{h}", [P, HALF], F32, st_at + J * LAST + HALF * h) for h in range(2)]
         st_half = {(t, h): st_sb[t][:, halves[h]] for t in range(LAST) for h in range(2)}
         for h in range(2):
             st_half[LAST, h] = st_last[h][:]
-        r_win = [held(f"r_win{t}", [P, T], F32, T + PACK * (N + J) + T * t) for t in range(PACK)]
-        wk_raw = held("wk_raw", [P, PACK, N], F32, T + PACK * (N + J + T))
+        r_win = [held(f"r_win{t}", [P, T], F32, r_at + T * t) for t in range(PACK)]
+        wk_raw = held("wk_raw", [P, PACK, N], F32, wk_at)
         w_raw = [wk_raw, wv_raw]
 
         nc.sync.dma_start(offsets[:], offs)
@@ -101,7 +103,7 @@ def tile_list_engram_addLP_kernel(
             if t + 1 < LAST:
                 nc.sync.dma_start(st_sb[t + 1][:], st_rows[:, t + 1, :])
             elif t < LAST:
-                for h in range(2):
+                for h in (1, 0):
                     nc.sync.dma_start(st_half[LAST, h], st_rows[:, LAST, halves[h]])
             nc.sync.dma_start(r_win[t][:], r_rows[:, t, :])
 
@@ -110,6 +112,9 @@ def tile_list_engram_addLP_kernel(
                 woven_w[:].rearrange("p (t m i) -> p m t i", t=t1 - t0, i=PACK)[:, m0:m1],
                 w_raw[w][:].rearrange("p i (m t) -> p m t i", t=PACK)[:, m0:m1, t0:t1],
             )
+
+        def round_on_gpsimd(out, in_):
+            nc.gpsimd.tensor_scalar(out, in_, 1.0, 0.0, MULT, ADD)
 
         def quantise_w(w, woven_w, t0, t1):
             cols = slice(t0 * P, t1 * P)
@@ -133,63 +138,46 @@ def tile_list_engram_addLP_kernel(
         gate = {}
         gated = {}
         key = {}
-        turned = {}
         value = {}
 
-        def copy_key(t, h, number):
-            if t == 1:
-                key[t, h] = held(f"key{t}_{h}", [P, HALF], F32, T + J + h * HALF)
-            else:
-                key[t, h] = held(f"key{t}_{h}", [P, HALF], F32, T + (t - 2) * HALF)
-            nc.scalar.copy(key[t, h][:], product(KEY, t, h, number)[:])
+        def copy_out(w, t, h, number, place=None):
+            if place is None:
+                place = sbuf(f"copied{w}_{t}_{h}", [P, HALF], F32)
+            nc.scalar.copy(place[:], product(w, t, h, number)[:])
+            return place
 
-        def logit_on_gpsimd(t, h, place):
-            logit[t, h] = place
-            nc.gpsimd.tensor_tensor(place, key[t, h][:], st_half[t, h], ADD)
+        def logit_on_gpsimd(t, place):
+            logit[t, 0] = place
+            nc.gpsimd.tensor_tensor(place, key[t, 0][:], st_half[t, 0], ADD)
 
-        def turn_key(t, number):
-            plane_cols = slice(t * P, (t + 1) * P)
-            acc = bank(f"key_turning{t}", number)
-            for b in blocks:
-                nc.tensor.matmul_mx(
-                    out=acc[:, b],
-                    lhsT=tab_codes[0][:, b].bitcast(FP8X4),
-                    lhsT_scale=tab_sc[:, b],
-                    rhs=w_codes[KEY][:, plane_cols].bitcast(FP8X4),
-                    rhs_scale=w_scales[KEY][:, plane_cols],
-                    start=True,
-                    stop=True,
-                )
-            turned[KEY, t] = sbuf(f"key_turned{t}", [P, HALF], F32)
-            nc.scalar.copy(turned[KEY, t][:], acc[:])
-
-        def logit_on_tensor(t):
-            acc = bank(f"st_turning{t}", 2)
-            for b in blocks:
-                nc.tensor.transpose(acc[:, b], st_half[t, 0][:, b], ident[:])
-            st_turned = sbuf(f"st_turned{t}", [P, HALF], F32)
-            nc.scalar.copy(st_turned[:], acc[:])
-            acc = bank(f"logit{t}", 3)
-            turns = [(src, b) for src in (turned[KEY, t], st_turned) for b in blocks]
+        def gate_on_tensor(t, logit_bank, gate_bank, turned):
+            acc = bank(f"logit_turned{t}", logit_bank)
+            turns = [(src, b) for src in (key[t, 1][:], st_half[t, 1]) for b in blocks]
             for step, (src, b) in enumerate(turns):
                 nc.tensor.matmul(
                     acc[:, b], src[:, b], ident[:],
                     start=(step == 0), stop=(step == len(turns) - 1), is_transpose=True,
                 )
-            logit[t, 0] = acc[:]
+            nc.scalar.activation(turned[:], acc[:], SIGMOID)
+            gate[t, 1] = bank(f"gate{t}", gate_bank)[:]
+            for b in blocks:
+                nc.tensor.transpose(gate[t, 1][:, b], turned[:, b], ident[:])
 
-        def make_gate(t, h):
-            gate[t, h] = sbuf(f"gate{t}_{h}", [P, HALF], F32)
-            nc.scalar.activation(gate[t, h][:], logit[t, h], SIGMOID)
+        def make_gate(t, h, place):
+            gate[t, h] = place
+            nc.scalar.activation(place, logit[t, h], SIGMOID)
 
         def window(t):
             return (1 + min(t, LAST - 1)) * QUARTER
 
-        def gate_values(t):
+        def gate_value(t, h):
             at = window(t)
-            for h in range(2):
-                gated[t, h] = sbuf(f"gated{t}", [P, HALF], F32, tag="gated")[:] if h else parked[:, at : at + HALF]
-                nc.vector.tensor_tensor(gated[t, h], value[t, h][:], gate[t, h][:], MULT)
+            if h:
+                gated[t, h] = sbuf(f"gated{t}", [P, HALF], F32, tag="gated")[:]
+            else:
+                gated[t, h] = held(f"gated{t}_0", [P, HALF], F32, T + at)[:]
+            in_psum, in_sbuf = (gate, value) if t > 1 and h else (value, gate)
+            nc.vector.tensor_tensor(gated[t, h], in_psum[t, h][:], in_sbuf[t, h][:], MULT)
 
         def add_record(t, c0, c1):
             h = c0 // HALF
@@ -200,24 +188,25 @@ def tile_list_engram_addLP_kernel(
                 ADD,
             )
 
-        def store_rows(t, c0, c1):
-            nc.sync.dma_start(out_rows[:, t, c0:c1], result[:, t * J + c0 : t * J + c1])
+        def store_rows(t0, t1, c0, c1):
+            nc.sync.dma_start(out_rows[:, t0, c0:c1], result[:, t0 * J + c0 : t0 * J + c1])
 
         def weave_pair(u, c0, c1, copy):
-            h = c0 // HALF
             planes = result[:, 2 * u * J : 2 * (u + 1) * J].rearrange("p (v j) -> p j v", v=2)
+            h = c0 // HALF
             pairs = woven[h][:].rearrange("p (j u v) -> p u j v", u=2, v=2)
             copy(pairs[:, u, c0 - h * HALF : c1 - h * HALF], planes[:, c0:c1])
 
-        def quantise_quarter(q):
-            cols = slice(q * QUARTER, (q + 1) * QUARTER)
+        def quantise_result(c0, c1):
+            h = c0 // HALF
             nc.vector.quantize_mx(
-                out=res_codes[:, cols].bitcast(FP8X4),
-                scales=res_scales[:, cols],
-                in_=woven[q // 2][:, (q % 2) * QUARTER * PACK : (q % 2 + 1) * QUARTER * PACK],
+                out=res_codes[:, c0:c1].bitcast(FP8X4),
+                scales=res_scales[:, c0:c1],
+                in_=woven[h][:, (c0 - h * HALF) * PACK : (c1 - h * HALF) * PACK],
             )
-            if q % 2:
-                nc.sync.dma_start(out_words[:, halves[q // 2]], res_codes[:, halves[q // 2]].bitcast(I32))
+
+        def store_words(c0, c1):
+            nc.sync.dma_start(out_words[:, c0:c1], res_codes[:, c0:c1].bitcast(I32))
 
         def gather_words(h):
             entries = offsets[:, h * HALF // GROUP : (h + 1) * HALF // GROUP]
@@ -235,59 +224,71 @@ def tile_list_engram_addLP_kernel(
         gather_words(1)
         wv_bf = sbuf("wv_bf", [P, N * PACK], BF16)
         weave_w(VALUE, wv_bf, 0, PACK, 0, SCALAR_M, nc.scalar.copy)
-        weave_w(VALUE, wv_bf, 0, PACK, SCALAR_M, P, nc.vector.tensor_copy)
+        weave_w(VALUE, wv_bf, 0, PACK, SCALAR_M, P, round_on_gpsimd)
         quantise_w(VALUE, wv_bf, 0, PACK)
 
         first_key = product(KEY, 0, 0, 0)
-        copy_key(1, 0, 2)
+        key[1, 0] = copy_out(KEY, 1, 0, 2, held("key1_0", [P, HALF], F32, wv_at + HALF))
         on_gpsimd = sbuf("logits1", [P, J], F32, tag="wv_bf")
         for h in range(2):
-            logit[0, h] = held(f"logit0_{h}", [P, HALF], F32, h * (T + QUARTER))[:]
+            logit[0, h] = result[:, :HALF] if h else sbuf("logit0_0", [P, HALF], F32)[:]
             nc.vector.tensor_tensor(logit[0, h], (product(KEY, 0, h, h) if h else first_key)[:], st_half[0, h], ADD)
-        logit_on_gpsimd(1, 0, on_gpsimd[:, halves[0]])
-        logit[1, 1] = held("logit1_1", [P, HALF], F32, T + J + HALF)[:]
+        logit_on_gpsimd(1, on_gpsimd[:, halves[0]])
+        logit[1, 1] = held("logit1_1", [P, HALF], F32, wv_at + J)[:]
         nc.vector.tensor_tensor(logit[1, 1], product(KEY, 1, 1, 3)[:], st_half[1, 1], ADD)
         for t in range(2):
             for h in range(2):
-                value[t, h] = product(VALUE, t, h, 4 + 2 * t + h)
-                make_gate(t, h)
-        gate_values(0)
-        for t in (2, 3):
-            copy_key(t, 1, t - 2)
-            turn_key(t, t)
+                value[t, h] = product(VALUE, t, h, 4 + 2 * t + h if t or h else 0)
+                make_gate(t, h, sbuf(f"gate{t}_{h}", [P, HALF], F32)[:])
         for h in range(2):
-            value[2, h] = product(VALUE, 2, h, 4 + h)
-            value[3, h] = product(VALUE, 3, h, h)
+            gate_value(0, h)
+        key[2, 0] = copy_out(KEY, 2, 0, 1)
+        key[2, 1] = copy_out(KEY, 2, 1, 3)
+        value[2, 1] = copy_out(VALUE, 2, 1, 4)
+        value[2, 0] = product(VALUE, 2, 0, 0)
+        key[3, 0] = copy_out(KEY, 3, 0, 1)
 
         woven = []
-        for t in range(LAST):
-            if t:
-                gate_values(t)
-                logit_on_tensor(t + 1)
-                at = window(t)
-                logit_on_gpsimd(t + 1, 1, parked[:, at - HALF : at])
-                make_gate(t + 1, 0)
-                make_gate(t + 1, 1)
-            for h in range(2):
-                add_record(t, h * HALF, (h + 1) * HALF)
-            store_rows(t, 0, J)
-
-        woven.append(held("woven0", [P, HALF * PACK], BF16, st_at + J * LAST - HALF))
-        woven.append(sbuf("woven1", [P, HALF * PACK], BF16, tag=f"key_turned{LAST}"))
         for h in range(2):
-            weave_pair(0, h * HALF, (h + 1) * HALF, nc.scalar.copy)
-        gate_values(LAST)
+            add_record(0, h * HALF, (h + 1) * HALF)
+        store_rows(0, 1, 0, J)
+        for h in range(2):
+            gate_value(1, h)
+        logit_on_gpsimd(2, held("logit2_0", [P, HALF], F32, T + window(1) - HALF)[:])
+        gate_on_tensor(2, 3, 1, result[:, 2 * J : 2 * J + HALF])
+        make_gate(2, 0, sbuf("gate2_0", [P, HALF], F32)[:])
+        key[3, 1] = copy_out(KEY, 3, 1, 4, held("key3_1", [P, HALF], F32, QUARTER))
+        value[3, 1] = copy_out(VALUE, 3, 1, 2)
+        value[3, 0] = product(VALUE, 3, 0, 5)
+        for h in range(2):
+            add_record(1, h * HALF, (h + 1) * HALF)
+        store_rows(1, 2, 0, J)
+        for h in range(2):
+            gate_value(2, h)
+        logit_on_gpsimd(3, held("logit3_0", [P, HALF], F32, T + window(2) - HALF)[:])
+        gate_on_tensor(3, 4, 3, sbuf("gate_turned3", [P, HALF], F32))
+        woven.append(held("woven0", [P, HALF * PACK], BF16, HALF))
+        weave_pair(0, 0, HALF, nc.scalar.copy)
+        make_gate(3, 0, held("gate3_0", [P, HALF], F32, 0)[:])
+        woven.append(held("woven1", [P, HALF * PACK], BF16, HALF + J))
+        weave_pair(0, HALF, J, nc.scalar.copy)
+        for h in range(2):
+            add_record(2, h * HALF, (h + 1) * HALF)
+        store_rows(2, LAST, 0, J)
+        for h in range(2):
+            gate_value(LAST, h)
         for q in range(4):
             add_record(LAST, q * QUARTER, (q + 1) * QUARTER)
             if q % 2:
-                store_rows(LAST, (q - 1) * QUARTER, (q + 1) * QUARTER)
+                store_rows(LAST, PACK, (q - 1) * QUARTER, (q + 1) * QUARTER)
             if q < 3:
                 weave_pair(1, q * QUARTER, (q + 1) * QUARTER, nc.scalar.copy)
-        quantise_quarter(0)
-        quantise_quarter(1)
-        weave_pair(1, 3 * QUARTER, J, nc.vector.tensor_copy)
-        quantise_quarter(2)
-        quantise_quarter(3)
+        for q in range(4):
+            if q == 2:
+                weave_pair(1, 3 * QUARTER, J, nc.vector.tensor_copy)
+            quantise_result(q * QUARTER, (q + 1) * QUARTER)
+            if q % 2:
+                store_words((q - 1) * QUARTER, (q + 1) * QUARTER)
         for quad in range(P // QUADRANT):
             queue = nc.sync if quad % 2 else nc.scalar
             queue.dma_start(

@@ -24,7 +24,7 @@ HALF = J // 2
 QUARTER = J // 4
 LAST = PACK - 1
 KEY, VALUE = 0, 1
-SCALAR_M = 84
+SCALAR_M = 72
 
 
 def tile_list_engram_addLP_kernel(
@@ -107,10 +107,10 @@ def tile_list_engram_addLP_kernel(
                     nc.sync.dma_start(st_half[LAST, h], st_rows[:, LAST, halves[h]])
             nc.sync.dma_start(r_win[t][:], r_rows[:, t, :])
 
-        def weave_w(w, woven_w, t0, t1, m0, m1, copy):
+        def weave_w(w, woven_w, m0, m1, copy, walk):
             copy(
-                woven_w[:].rearrange("p (t m i) -> p m t i", t=t1 - t0, i=PACK)[:, m0:m1],
-                w_raw[w][:].rearrange("p i (m t) -> p m t i", t=PACK)[:, m0:m1, t0:t1],
+                woven_w[:].rearrange(f"p (t m i) -> p {walk}", t=PACK, i=PACK)[:, m0:m1],
+                w_raw[w][:].rearrange(f"p i (m t) -> p {walk}", t=PACK)[:, m0:m1],
             )
 
         def round_on_gpsimd(out, in_):
@@ -218,13 +218,13 @@ def tile_list_engram_addLP_kernel(
         w_scales = [wk_scales, sbuf("wv_scales", [P, N], U8)]
         gather_words(0)
         wk_bf = sbuf("wk_bf", [P, N * PACK], BF16)
-        weave_w(KEY, wk_bf, 0, PACK, 0, P, nc.scalar.copy)
+        weave_w(KEY, wk_bf, 0, P, nc.scalar.copy, "m i t")
         quantise_w(KEY, wk_bf, 0, PACK)
         tab_codes.append(loads.tile([P, HALF], U32, name="codes1", tag="codes1", offset=scale_at + 64 - 4 * HALF, align_bytes=64))
         gather_words(1)
         wv_bf = sbuf("wv_bf", [P, N * PACK], BF16)
-        weave_w(VALUE, wv_bf, 0, PACK, 0, SCALAR_M, nc.scalar.copy)
-        weave_w(VALUE, wv_bf, 0, PACK, SCALAR_M, P, round_on_gpsimd)
+        weave_w(VALUE, wv_bf, 0, SCALAR_M, nc.scalar.copy, "m i t")
+        weave_w(VALUE, wv_bf, SCALAR_M, P, round_on_gpsimd, "m t i")
         quantise_w(VALUE, wv_bf, 0, PACK)
 
         first_key = product(KEY, 0, 0, 0)

@@ -20,10 +20,15 @@ P = 128
 PACK = 4
 GROUP = 16
 QUADRANT = 32
+SCALE_ROWS = 4
+ALIGN = 64
+FLOAT_BYTES = 4
+OVERLAP = 64
 HALF = J // 2
 QUARTER = J // 4
 LAST = PACK - 1
 KEY, VALUE = 0, 1
+TURNED_FROM = 2
 SCALAR_M = 72
 
 
@@ -37,7 +42,13 @@ def tile_list_engram_addLP_kernel(
         psum = ctx.enter_context(tc.psum_pool(name="psum", bufs=1))
 
         def sbuf(name, shape, dtype, tag=None):
-            return keep.tile(shape, dtype, name=name, tag=tag or name, align_bytes=64)
+            return keep.tile(shape, dtype, name=name, tag=tag or name, align_bytes=ALIGN)
+
+        def held(name, shape, dtype, first_float):
+            return loads.tile(shape, dtype, name=name, tag=name, offset=FLOAT_BYTES * first_float)
+
+        def packed(name, shape, dtype, first_byte):
+            return loads.tile(shape, dtype, name=name, tag=name, offset=first_byte, align_bytes=ALIGN)
 
         def bank(name, number):
             return psum.tile([P, HALF], F32, name=name, tag=f"bank{number}")
@@ -51,19 +62,26 @@ def tile_list_engram_addLP_kernel(
         warm = sbuf("warm", [P, 2], F32)
         zeros = sbuf("zeros", [P, P], F32)
 
-        result_at = T + 5 * QUARTER
-        wv_at = result_at + PACK * J - 64
+        chain_at = T
+        result_at = chain_at + 5 * QUARTER
+        wv_at = result_at + PACK * J - OVERLAP
         st_at = wv_at + PACK * N
         r_at = st_at + PACK * J
         wk_at = r_at + PACK * T
-        scale_at = 4 * (wk_at + PACK * N)
-        scale_win = loads.tile([P, T], U8, name="scale_win", tag="scale_win", offset=scale_at, align_bytes=64)
+        scale_byte = FLOAT_BYTES * (wk_at + PACK * N)
+        scale_win = packed("scale_win", [P, T], U8, scale_byte)
         st_rows = st.rearrange("(p t) j -> p t j", t=PACK)
         r_rows = rT.rearrange("(p t) c -> p t c", t=PACK)
         out_rows = out_0.rearrange("(p t) j -> p t j", t=PACK)
         out_words = out_1[0].rearrange("p j i -> p (j i)").bitcast(I32)
         halves = [slice(h * HALF, (h + 1) * HALF) for h in range(2)]
-        blocks = [slice(e * P, (e + 1) * P) for e in range(HALF // P)]
+        squares = [slice(e * P, (e + 1) * P) for e in range(HALF // P)]
+
+        def scale_partitions(tile, quad):
+            return tile[QUADRANT * quad : QUADRANT * quad + SCALE_ROWS, :].bitcast(I32)
+
+        def scale_rows(dram, quad):
+            return dram[0, SCALE_ROWS * quad : SCALE_ROWS * (quad + 1), :].bitcast(I32)
 
         nc.gpsimd.memset(scale_win[:].bitcast(I32), 0)
         nc.gpsimd.memset(warm[:, 0:1], 0.0)
@@ -72,9 +90,6 @@ def tile_list_engram_addLP_kernel(
             out=ident[:], in_=zeros[:, :P], compare_op=mybir.AluOpType.not_equal, fill=1.0, base=0,
             pattern=[[-1, P]], channel_multiplier=1,
         )
-
-        def held(name, shape, dtype, first_float):
-            return loads.tile(shape, dtype, name=name, tag=name, offset=4 * first_float)
 
         word_win = held("word_win", [P, T], I32, 0)
         wv_raw = held("wv_raw", [P, PACK, N], F32, wv_at)
@@ -90,10 +105,7 @@ def tile_list_engram_addLP_kernel(
 
         nc.sync.dma_start(offsets[:], offs)
         for quad in range(P // QUADRANT):
-            nc.sync.dma_start(
-                scale_win[QUADRANT * quad : QUADRANT * quad + 4, :].bitcast(I32),
-                tab_scales[0, 4 * quad : 4 * quad + 4, :].bitcast(I32),
-            )
+            nc.sync.dma_start(scale_partitions(scale_win, quad), scale_rows(tab_scales, quad))
         nc.scalar.activation(warm[:, 1:2], warm[:, 0:1], SIGMOID)
         nc.sync.dma_start(wk_raw[:], wk.rearrange("(p i) c -> p i c", i=PACK))
         nc.sync.dma_start(word_win[:], tab_words[0].rearrange("p t i -> p (t i)").bitcast(I32))
@@ -102,12 +114,19 @@ def tile_list_engram_addLP_kernel(
         for t in range(PACK):
             if t + 1 < LAST:
                 nc.sync.dma_start(st_sb[t + 1][:], st_rows[:, t + 1, :])
-            elif t < LAST:
+            elif t + 1 == LAST:
                 for h in (1, 0):
                     nc.sync.dma_start(st_half[LAST, h], st_rows[:, LAST, halves[h]])
             nc.sync.dma_start(r_win[t][:], r_rows[:, t, :])
 
-        def weave_w(w, woven_w, m0, m1, copy, walk):
+        logit, gate, gated, key, value = {}, {}, {}, {}, {}
+        woven = []
+
+        def gather_words(h):
+            entries = offsets[:, h * HALF // GROUP : (h + 1) * HALF // GROUP]
+            nc.vector.tensor_copy(tab_codes[h][:], word_win[:].bitcast(U32).indirect(entries))
+
+        def weave_weight(w, woven_w, m0, m1, copy, walk):
             copy(
                 woven_w[:].rearrange(f"p (t m i) -> p {walk}", t=PACK, i=PACK)[:, m0:m1],
                 w_raw[w][:].rearrange(f"p i (m t) -> p {walk}", t=PACK)[:, m0:m1],
@@ -116,9 +135,8 @@ def tile_list_engram_addLP_kernel(
         def round_on_gpsimd(out, in_):
             nc.gpsimd.tensor_scalar(out, in_, 1.0, 0.0, MULT, ADD)
 
-        def quantise_w(w, woven_w, t0, t1):
-            cols = slice(t0 * P, t1 * P)
-            nc.vector.quantize_mx(out=w_codes[w][:, cols].bitcast(FP8X4), scales=w_scales[w][:, cols], in_=woven_w[:])
+        def quantise_weight(w, woven_w):
+            nc.vector.quantize_mx(out=w_codes[w][:].bitcast(FP8X4), scales=w_scales[w][:], in_=woven_w[:])
 
         def product(w, t, h, number):
             acc = bank(f"acc{w}_{t}_{h}", number)
@@ -134,50 +152,51 @@ def tile_list_engram_addLP_kernel(
             )
             return acc
 
-        logit = {}
-        gate = {}
-        gated = {}
-        key = {}
-        value = {}
-
-        def copy_out(w, t, h, number, place=None):
+        def copied_product(w, t, h, number, place=None):
             if place is None:
                 place = sbuf(f"copied{w}_{t}_{h}", [P, HALF], F32)
             nc.scalar.copy(place[:], product(w, t, h, number)[:])
             return place
 
+        def logit_on_vector(t, h, key_bank, place):
+            logit[t, h] = place
+            nc.vector.tensor_tensor(place, key_bank[:], st_half[t, h], ADD)
+
         def logit_on_gpsimd(t, place):
             logit[t, 0] = place
             nc.gpsimd.tensor_tensor(place, key[t, 0][:], st_half[t, 0], ADD)
-
-        def gate_on_tensor(t, logit_bank, gate_bank, turned):
-            acc = bank(f"logit_turned{t}", logit_bank)
-            turns = [(src, b) for src in (key[t, 1][:], st_half[t, 1]) for b in blocks]
-            for step, (src, b) in enumerate(turns):
-                nc.tensor.matmul(
-                    acc[:, b], src[:, b], ident[:],
-                    start=(step == 0), stop=(step == len(turns) - 1), is_transpose=True,
-                )
-            nc.scalar.activation(turned[:], acc[:], SIGMOID)
-            gate[t, 1] = bank(f"gate{t}", gate_bank)[:]
-            for b in blocks:
-                nc.tensor.transpose(gate[t, 1][:, b], turned[:, b], ident[:])
 
         def make_gate(t, h, place):
             gate[t, h] = place
             nc.scalar.activation(place, logit[t, h], SIGMOID)
 
-        def window(t):
-            return (1 + min(t, LAST - 1)) * QUARTER
+        def gate_on_tensor(t, logit_bank, gate_bank, turned):
+            acc = bank(f"logit_turned{t}", logit_bank)
+            turns = [(src, sq) for src in (key[t, 1][:], st_half[t, 1]) for sq in squares]
+            for step, (src, sq) in enumerate(turns):
+                nc.tensor.matmul(
+                    acc[:, sq], src[:, sq], ident[:],
+                    start=(step == 0), stop=(step == len(turns) - 1), is_transpose=True,
+                )
+            nc.scalar.activation(turned[:], acc[:], SIGMOID)
+            gate[t, 1] = bank(f"gate{t}", gate_bank)[:]
+            for sq in squares:
+                nc.tensor.transpose(gate[t, 1][:, sq], turned[:, sq], ident[:])
 
-        def gate_value(t, h):
-            at = window(t)
-            if h:
-                gated[t, h] = sbuf(f"gated{t}", [P, HALF], F32, tag="gated")[:]
-            else:
-                gated[t, h] = held(f"gated{t}_0", [P, HALF], F32, T + at)[:]
-            in_psum, in_sbuf = (gate, value) if t > 1 and h else (value, gate)
-            nc.vector.tensor_tensor(gated[t, h], in_psum[t, h][:], in_sbuf[t, h][:], MULT)
+        def gated_at(t):
+            return chain_at + (1 + min(t, LAST - 1)) * QUARTER
+
+        def chained_logit(t):
+            return held(f"logit{t}_0", [P, HALF], F32, gated_at(t - 1) - HALF)[:]
+
+        def gate_values(t):
+            for h in range(2):
+                if h:
+                    gated[t, h] = sbuf(f"gated{t}", [P, HALF], F32, tag="gated")[:]
+                else:
+                    gated[t, h] = held(f"gated{t}_0", [P, HALF], F32, gated_at(t))[:]
+                in_psum, in_sbuf = (gate, value) if t >= TURNED_FROM and h else (value, gate)
+                nc.vector.tensor_tensor(gated[t, h], in_psum[t, h][:], in_sbuf[t, h][:], MULT)
 
         def add_record(t, c0, c1):
             h = c0 // HALF
@@ -188,110 +207,95 @@ def tile_list_engram_addLP_kernel(
                 ADD,
             )
 
-        def store_rows(t0, t1, c0, c1):
-            nc.sync.dma_start(out_rows[:, t0, c0:c1], result[:, t0 * J + c0 : t0 * J + c1])
+        def store_rows(t, c0, c1):
+            nc.sync.dma_start(out_rows[:, t, c0:c1], result[:, t * J + c0 : t * J + c1])
+
+        def finish_plane(t):
+            for h in range(2):
+                add_record(t, h * HALF, (h + 1) * HALF)
+            store_rows(t, 0, J)
+
+        def woven_cols(c0, c1):
+            part = min(c0 // QUARTER, 1)
+            return woven[part][:, (c0 - part * QUARTER) * PACK : (c1 - part * QUARTER) * PACK]
 
         def weave_pair(u, c0, c1, copy):
             planes = result[:, 2 * u * J : 2 * (u + 1) * J].rearrange("p (v j) -> p j v", v=2)
-            h = c0 // HALF
-            pairs = woven[h][:].rearrange("p (j u v) -> p u j v", u=2, v=2)
-            copy(pairs[:, u, c0 - h * HALF : c1 - h * HALF], planes[:, c0:c1])
+            pairs = woven_cols(c0, c1).rearrange("p (j u v) -> p u j v", u=2, v=2)
+            copy(pairs[:, u], planes[:, c0:c1])
 
         def quantise_result(c0, c1):
-            h = c0 // HALF
             nc.vector.quantize_mx(
-                out=res_codes[:, c0:c1].bitcast(FP8X4),
-                scales=res_scales[:, c0:c1],
-                in_=woven[h][:, (c0 - h * HALF) * PACK : (c1 - h * HALF) * PACK],
+                out=res_codes[:, c0:c1].bitcast(FP8X4), scales=res_scales[:, c0:c1], in_=woven_cols(c0, c1)
             )
 
-        def store_words(c0, c1):
-            nc.sync.dma_start(out_words[:, c0:c1], res_codes[:, c0:c1].bitcast(I32))
-
-        def gather_words(h):
-            entries = offsets[:, h * HALF // GROUP : (h + 1) * HALF // GROUP]
-            nc.vector.tensor_copy(tab_codes[h][:], word_win[:].bitcast(U32).indirect(entries))
-
         nc.vector.tensor_copy(tab_sc[:], scale_win[:].indirect(offsets[:]))
-        tab_codes = [loads.tile([P, HALF], U32, name="codes0", tag="codes0", offset=scale_at + 64 + N, align_bytes=64)]
-        wk_scales = loads.tile([P, N], U8, name="wk_scales", tag="wk_scales", offset=scale_at + 64, align_bytes=64)
+        tab_codes = [packed("codes0", [P, HALF], U32, scale_byte + ALIGN + N)]
+        wk_scales = packed("wk_scales", [P, N], U8, scale_byte + ALIGN)
         w_scales = [wk_scales, sbuf("wv_scales", [P, N], U8)]
         gather_words(0)
         wk_bf = sbuf("wk_bf", [P, N * PACK], BF16)
-        weave_w(KEY, wk_bf, 0, P, nc.scalar.copy, "m i t")
-        quantise_w(KEY, wk_bf, 0, PACK)
-        tab_codes.append(loads.tile([P, HALF], U32, name="codes1", tag="codes1", offset=scale_at + 64 - 4 * HALF, align_bytes=64))
+        weave_weight(KEY, wk_bf, 0, P, nc.scalar.copy, "m i t")
+        quantise_weight(KEY, wk_bf)
+        tab_codes.append(packed("codes1", [P, HALF], U32, scale_byte + ALIGN - FLOAT_BYTES * HALF))
         gather_words(1)
         wv_bf = sbuf("wv_bf", [P, N * PACK], BF16)
-        weave_w(VALUE, wv_bf, 0, SCALAR_M, nc.scalar.copy, "m i t")
-        weave_w(VALUE, wv_bf, SCALAR_M, P, round_on_gpsimd, "m t i")
-        quantise_w(VALUE, wv_bf, 0, PACK)
+        weave_weight(VALUE, wv_bf, 0, SCALAR_M, nc.scalar.copy, "m i t")
+        weave_weight(VALUE, wv_bf, SCALAR_M, P, round_on_gpsimd, "m t i")
+        quantise_weight(VALUE, wv_bf)
+
 
         first_key = product(KEY, 0, 0, 0)
-        key[1, 0] = copy_out(KEY, 1, 0, 2, held("key1_0", [P, HALF], F32, wv_at + HALF))
-        on_gpsimd = sbuf("logits1", [P, J], F32, tag="wv_bf")
-        for h in range(2):
-            logit[0, h] = result[:, :HALF] if h else sbuf("logit0_0", [P, HALF], F32)[:]
-            nc.vector.tensor_tensor(logit[0, h], (product(KEY, 0, h, h) if h else first_key)[:], st_half[0, h], ADD)
-        logit_on_gpsimd(1, on_gpsimd[:, halves[0]])
-        logit[1, 1] = held("logit1_1", [P, HALF], F32, wv_at + J)[:]
-        nc.vector.tensor_tensor(logit[1, 1], product(KEY, 1, 1, 3)[:], st_half[1, 1], ADD)
-        for t in range(2):
-            for h in range(2):
-                value[t, h] = product(VALUE, t, h, 4 + 2 * t + h if t or h else 0)
-                make_gate(t, h, sbuf(f"gate{t}_{h}", [P, HALF], F32)[:])
-        for h in range(2):
-            gate_value(0, h)
-        key[2, 0] = copy_out(KEY, 2, 0, 1)
-        key[2, 1] = copy_out(KEY, 2, 1, 3)
-        value[2, 1] = copy_out(VALUE, 2, 1, 4)
+        key[1, 0] = copied_product(KEY, 1, 0, 2, held("key1_0", [P, HALF], F32, wv_at + HALF))
+        on_woven_wv = sbuf("logits1", [P, J], F32, tag="wv_bf")
+        logit_on_vector(0, 0, first_key, sbuf("logit0_0", [P, HALF], F32)[:])
+        logit_on_vector(0, 1, product(KEY, 0, 1, 1), result[:, :HALF])
+        logit_on_gpsimd(1, on_woven_wv[:, halves[0]])
+        on_raw_wv = held("logit1_1", [P, HALF], F32, wv_at + J)
+        logit_on_vector(1, 1, product(KEY, 1, 1, 3), on_raw_wv[:])
+        for (t, h), number in zip(((0, 0), (0, 1), (1, 0), (1, 1)), (0, 5, 6, 7)):
+            value[t, h] = product(VALUE, t, h, number)
+            make_gate(t, h, sbuf(f"gate{t}_{h}", [P, HALF], F32)[:])
+        gate_values(0)
+        key[2, 0] = copied_product(KEY, 2, 0, 1)
+        key[2, 1] = copied_product(KEY, 2, 1, 3)
+        value[2, 1] = copied_product(VALUE, 2, 1, 4)
         value[2, 0] = product(VALUE, 2, 0, 0)
-        key[3, 0] = copy_out(KEY, 3, 0, 1)
+        key[3, 0] = copied_product(KEY, 3, 0, 1)
+        finish_plane(0)
+        gate_values(1)
 
-        woven = []
-        for h in range(2):
-            add_record(0, h * HALF, (h + 1) * HALF)
-        store_rows(0, 1, 0, J)
-        for h in range(2):
-            gate_value(1, h)
-        logit_on_gpsimd(2, held("logit2_0", [P, HALF], F32, T + window(1) - HALF)[:])
+        logit_on_gpsimd(2, chained_logit(2))
         gate_on_tensor(2, 3, 1, result[:, 2 * J : 2 * J + HALF])
         make_gate(2, 0, sbuf("gate2_0", [P, HALF], F32)[:])
-        key[3, 1] = copy_out(KEY, 3, 1, 4, held("key3_1", [P, HALF], F32, QUARTER))
-        value[3, 1] = copy_out(VALUE, 3, 1, 2)
+        key[3, 1] = copied_product(KEY, 3, 1, 4, held("key3_1", [P, HALF], F32, QUARTER))
+        value[3, 1] = copied_product(VALUE, 3, 1, 2)
         value[3, 0] = product(VALUE, 3, 0, 5)
-        for h in range(2):
-            add_record(1, h * HALF, (h + 1) * HALF)
-        store_rows(1, 2, 0, J)
-        for h in range(2):
-            gate_value(2, h)
-        logit_on_gpsimd(3, held("logit3_0", [P, HALF], F32, T + window(2) - HALF)[:])
+        finish_plane(1)
+        gate_values(2)
+
+        logit_on_gpsimd(3, chained_logit(3))
         gate_on_tensor(3, 4, 3, sbuf("gate_turned3", [P, HALF], F32))
-        woven.append(held("woven0", [P, HALF * PACK], BF16, HALF))
-        weave_pair(0, 0, HALF, nc.scalar.copy)
+        woven.append(held("woven0", [P, QUARTER * PACK], BF16, HALF))
+        weave_pair(0, 0, QUARTER, nc.scalar.copy)
         make_gate(3, 0, held("gate3_0", [P, HALF], F32, 0)[:])
-        woven.append(held("woven1", [P, HALF * PACK], BF16, HALF + J))
-        weave_pair(0, HALF, J, nc.scalar.copy)
-        for h in range(2):
-            add_record(2, h * HALF, (h + 1) * HALF)
-        store_rows(2, LAST, 0, J)
-        for h in range(2):
-            gate_value(LAST, h)
-        for q in range(4):
+        woven.append(held("woven1", [P, (J - QUARTER) * PACK], BF16, J))
+        weave_pair(0, QUARTER, J, nc.scalar.copy)
+        finish_plane(2)
+        gate_values(LAST)
+
+        for q in range(J // QUARTER):
             add_record(LAST, q * QUARTER, (q + 1) * QUARTER)
             if q % 2:
-                store_rows(LAST, PACK, (q - 1) * QUARTER, (q + 1) * QUARTER)
-            if q < 3:
+                store_rows(LAST, (q - 1) * QUARTER, (q + 1) * QUARTER)
+            if (q + 1) * QUARTER < J:
                 weave_pair(1, q * QUARTER, (q + 1) * QUARTER, nc.scalar.copy)
-        for q in range(4):
-            if q == 2:
-                weave_pair(1, 3 * QUARTER, J, nc.vector.tensor_copy)
-            quantise_result(q * QUARTER, (q + 1) * QUARTER)
-            if q % 2:
-                store_words((q - 1) * QUARTER, (q + 1) * QUARTER)
+        for h in range(2):
+            if h:
+                weave_pair(1, J - QUARTER, J, nc.vector.tensor_copy)
+            for c0 in (h * HALF, h * HALF + QUARTER):
+                quantise_result(c0, c0 + QUARTER)
+            nc.sync.dma_start(out_words[:, halves[h]], res_codes[:, halves[h]].bitcast(I32))
         for quad in range(P // QUADRANT):
             queue = nc.sync if quad % 2 else nc.scalar
-            queue.dma_start(
-                out_2[0, 4 * quad : 4 * quad + 4, :].bitcast(I32),
-                res_scales[QUADRANT * quad : QUADRANT * quad + 4, :].bitcast(I32),
-            )
+            queue.dma_start(scale_rows(out_2, quad), scale_partitions(res_scales, quad))

@@ -107,8 +107,8 @@ def tile_list_engram_addLP_kernel(
         for quad in range(P // QUADRANT):
             nc.sync.dma_start(scale_partitions(scale_win, quad), scale_rows(tab_scales, quad))
         nc.scalar.activation(warm[:, 1:2], warm[:, 0:1], SIGMOID)
-        nc.sync.dma_start(wk_raw[:], wk.rearrange("(p i) c -> p i c", i=PACK))
         nc.sync.dma_start(word_win[:], tab_words[0].rearrange("p t i -> p (t i)").bitcast(I32))
+        nc.sync.dma_start(wk_raw[:], wk.rearrange("(p i) c -> p i c", i=PACK))
         nc.sync.dma_start(wv_raw[:], wv.rearrange("(p i) c -> p i c", i=PACK))
         nc.sync.dma_start(st_sb[0][:], st_rows[:, 0, :])
         for t in range(PACK):
@@ -229,13 +229,14 @@ def tile_list_engram_addLP_kernel(
                 out=res_codes[:, c0:c1].bitcast(FP8X4), scales=res_scales[:, c0:c1], in_=woven_cols(c0, c1)
             )
 
+        tab_codes = [sbuf("codes0", [P, HALF], U32)]
+        gather_words(0)
         nc.vector.tensor_copy(tab_sc[:], scale_win[:].indirect(offsets[:]))
-        tab_codes = [packed("codes0", [P, HALF], U32, scale_byte + ALIGN + N)]
         wk_scales = packed("wk_scales", [P, N], U8, scale_byte + ALIGN)
         w_scales = [wk_scales, sbuf("wv_scales", [P, N], U8)]
-        gather_words(0)
         wk_bf = sbuf("wk_bf", [P, N * PACK], BF16)
-        weave_weight(KEY, wk_bf, 0, P, nc.scalar.copy, "m i t")
+        weave_weight(KEY, wk_bf, 0, SCALAR_M, nc.scalar.copy, "m i t")
+        weave_weight(KEY, wk_bf, SCALAR_M, P, round_on_gpsimd, "m t i")
         quantise_weight(KEY, wk_bf)
         tab_codes.append(packed("codes1", [P, HALF], U32, scale_byte + ALIGN - FLOAT_BYTES * HALF))
         gather_words(1)

@@ -30,6 +30,8 @@ LAST = PACK - 1
 KEY, VALUE = 0, 1
 TURNED_FROM = 2
 SCALAR_M = 72
+SCALAR_M_KEY = 66
+GPSIMD_COLS = 256
 
 
 def tile_list_engram_addLP_kernel(
@@ -55,7 +57,6 @@ def tile_list_engram_addLP_kernel(
 
         offsets = keep.tile([P, J // GROUP], U16, name="offsets")
         w_codes = [sbuf(f"w_codes{w}", [P, N], U32) for w in (KEY, VALUE)]
-        tab_sc = sbuf("tab_sc", [P, J], U8)
         res_codes = sbuf("res_codes", [P, J], U32)
         res_scales = sbuf("res_scales", [P, J], U8)
         ident = sbuf("ident", [P, P], F32)
@@ -122,9 +123,9 @@ def tile_list_engram_addLP_kernel(
         logit, gate, gated, key, value = {}, {}, {}, {}, {}
         woven = []
 
-        def gather_words(h):
+        def gather_scales(h):
             entries = offsets[:, h * HALF // GROUP : (h + 1) * HALF // GROUP]
-            nc.vector.tensor_copy(tab_codes[h][:], word_win[:].bitcast(U32).indirect(entries))
+            nc.vector.tensor_copy(tab_sc[h][:], scale_win[:].indirect(entries))
 
         def weave_weight(w, woven_w, m0, m1, copy, walk):
             copy(
@@ -145,8 +146,8 @@ def tile_list_engram_addLP_kernel(
                 out=acc[:],
                 lhsT=w_codes[w][:, plane_cols].bitcast(FP8X4),
                 lhsT_scale=w_scales[w][:, plane_cols],
-                rhs=tab_codes[h][:].bitcast(FP8X4),
-                rhs_scale=tab_sc[:, halves[h]],
+                rhs=tab_codes[:, halves[h]].bitcast(FP8X4),
+                rhs_scale=tab_sc[h][:],
                 start=True,
                 stop=True,
             )
@@ -196,7 +197,11 @@ def tile_list_engram_addLP_kernel(
                 else:
                     gated[t, h] = held(f"gated{t}_0", [P, HALF], F32, gated_at(t))[:]
                 in_psum, in_sbuf = (gate, value) if t >= TURNED_FROM and h else (value, gate)
-                nc.vector.tensor_tensor(gated[t, h], in_psum[t, h][:], in_sbuf[t, h][:], MULT)
+                own = slice(0, HALF - GPSIMD_COLS if (t, h) == (LAST, 0) else HALF)
+                nc.vector.tensor_tensor(gated[t, h][:, own], in_psum[t, h][:, own], in_sbuf[t, h][:, own], MULT)
+            if t == LAST:
+                rest = slice(HALF - GPSIMD_COLS, HALF)
+                nc.gpsimd.tensor_tensor(gated[t, 0][:, rest], value_rest[:], gate[t, 0][:, rest], MULT)
 
         def add_record(t, c0, c1):
             h = c0 // HALF
@@ -229,17 +234,18 @@ def tile_list_engram_addLP_kernel(
                 out=res_codes[:, c0:c1].bitcast(FP8X4), scales=res_scales[:, c0:c1], in_=woven_cols(c0, c1)
             )
 
-        tab_codes = [sbuf("codes0", [P, HALF], U32)]
-        gather_words(0)
-        nc.vector.tensor_copy(tab_sc[:], scale_win[:].indirect(offsets[:]))
-        wk_scales = packed("wk_scales", [P, N], U8, scale_byte + ALIGN)
+        tab_codes = sbuf("tab_codes", [P, J], U32)
+        tab_sc = [sbuf("tab_sc0", [P, HALF], U8)]
+        nc.vector.tensor_copy(tab_codes[:], word_win[:].bitcast(U32).indirect(offsets[:]))
+        gather_scales(0)
+        wk_scales = sbuf("wk_scales", [P, N], U8)
         w_scales = [wk_scales, sbuf("wv_scales", [P, N], U8)]
         wk_bf = sbuf("wk_bf", [P, N * PACK], BF16)
-        weave_weight(KEY, wk_bf, 0, SCALAR_M, nc.scalar.copy, "m i t")
-        weave_weight(KEY, wk_bf, SCALAR_M, P, round_on_gpsimd, "m t i")
+        weave_weight(KEY, wk_bf, 0, SCALAR_M_KEY, nc.scalar.copy, "m i t")
+        weave_weight(KEY, wk_bf, SCALAR_M_KEY, P, round_on_gpsimd, "m t i")
         quantise_weight(KEY, wk_bf)
-        tab_codes.append(packed("codes1", [P, HALF], U32, scale_byte + ALIGN - FLOAT_BYTES * HALF))
-        gather_words(1)
+        tab_sc.append(packed("tab_sc1", [P, HALF], U8, FLOAT_BYTES * wk_at))
+        gather_scales(1)
         wv_bf = sbuf("wv_bf", [P, N * PACK], BF16)
         weave_weight(VALUE, wv_bf, 0, SCALAR_M, nc.scalar.copy, "m i t")
         weave_weight(VALUE, wv_bf, SCALAR_M, P, round_on_gpsimd, "m t i")
@@ -272,6 +278,8 @@ def tile_list_engram_addLP_kernel(
         key[3, 1] = copied_product(KEY, 3, 1, 4, held("key3_1", [P, HALF], F32, QUARTER))
         value[3, 1] = copied_product(VALUE, 3, 1, 2)
         value[3, 0] = product(VALUE, 3, 0, 5)
+        value_rest = sbuf("value_rest", [P, GPSIMD_COLS], F32)
+        nc.scalar.copy(value_rest[:], value[3, 0][:, HALF - GPSIMD_COLS :])
         finish_plane(1)
         gate_values(2)
 

@@ -104,11 +104,11 @@ def tile_list_engram_addLP_kernel(
         wk_raw = held("wk_raw", [P, PACK, N], F32, wk_at)
         w_raw = [wk_raw, wv_raw]
 
+        nc.sync.dma_start(word_win[:], tab_words[0].rearrange("p t i -> p (t i)").bitcast(I32))
         nc.sync.dma_start(offsets[:], offs)
         for quad in range(P // QUADRANT):
             nc.sync.dma_start(scale_partitions(scale_win, quad), scale_rows(tab_scales, quad))
         nc.scalar.activation(warm[:, 1:2], warm[:, 0:1], SIGMOID)
-        nc.sync.dma_start(word_win[:], tab_words[0].rearrange("p t i -> p (t i)").bitcast(I32))
         nc.sync.dma_start(wk_raw[:], wk.rearrange("(p i) c -> p i c", i=PACK))
         nc.sync.dma_start(wv_raw[:], wv.rearrange("(p i) c -> p i c", i=PACK))
         nc.sync.dma_start(st_sb[0][:], st_rows[:, 0, :])
@@ -174,6 +174,8 @@ def tile_list_engram_addLP_kernel(
         def gate_on_tensor(t, logit_bank, gate_bank, turned):
             acc = bank(f"logit_turned{t}", logit_bank)
             turns = [(src, sq) for src in (key[t, 1][:], st_half[t, 1]) for sq in squares]
+            if t == LAST:
+                turns.append(turns.pop(len(squares) - 1))
             for step, (src, sq) in enumerate(turns):
                 nc.tensor.matmul(
                     acc[:, sq], src[:, sq], ident[:],
@@ -192,15 +194,19 @@ def tile_list_engram_addLP_kernel(
 
         def gate_values(t):
             for h in range(2):
-                if h:
+                if t == LAST and h:
+                    gated[t, h] = held("gated3_1", [P, HALF], F32, gated_at(1))[:]
+                elif t == LAST:
+                    gated[t, h] = result[:, 3 * J - QUARTER : 3 * J + QUARTER]
+                elif h:
                     gated[t, h] = sbuf(f"gated{t}", [P, HALF], F32, tag="gated")[:]
                 else:
                     gated[t, h] = held(f"gated{t}_0", [P, HALF], F32, gated_at(t))[:]
                 in_psum, in_sbuf = (gate, value) if t >= TURNED_FROM and h else (value, gate)
-                own = slice(0, HALF - GPSIMD_COLS if (t, h) == (LAST, 0) else HALF)
+                own = slice(GPSIMD_COLS if (t, h) == (LAST, 0) else 0, HALF)
                 nc.vector.tensor_tensor(gated[t, h][:, own], in_psum[t, h][:, own], in_sbuf[t, h][:, own], MULT)
             if t == LAST:
-                rest = slice(HALF - GPSIMD_COLS, HALF)
+                rest = slice(0, GPSIMD_COLS)
                 nc.gpsimd.tensor_tensor(gated[t, 0][:, rest], value_rest[:], gate[t, 0][:, rest], MULT)
 
         def add_record(t, c0, c1):
@@ -221,8 +227,8 @@ def tile_list_engram_addLP_kernel(
             store_rows(t, 0, J)
 
         def woven_cols(c0, c1):
-            part = min(c0 // QUARTER, 1)
-            return woven[part][:, (c0 - part * QUARTER) * PACK : (c1 - part * QUARTER) * PACK]
+            part = c0 // HALF
+            return woven[part][:, (c0 - part * HALF) * PACK : (c1 - part * HALF) * PACK]
 
         def weave_pair(u, c0, c1, copy):
             planes = result[:, 2 * u * J : 2 * (u + 1) * J].rearrange("p (v j) -> p j v", v=2)
@@ -253,58 +259,64 @@ def tile_list_engram_addLP_kernel(
 
 
         first_key = product(KEY, 0, 0, 0)
-        key[1, 0] = copied_product(KEY, 1, 0, 2, held("key1_0", [P, HALF], F32, wv_at + HALF))
+        key[1, 0] = copied_product(KEY, 1, 0, 2)
         on_woven_wv = sbuf("logits1", [P, J], F32, tag="wv_bf")
         logit_on_vector(0, 0, first_key, sbuf("logit0_0", [P, HALF], F32)[:])
         logit_on_vector(0, 1, product(KEY, 0, 1, 1), result[:, :HALF])
         logit_on_gpsimd(1, on_woven_wv[:, halves[0]])
         on_raw_wv = held("logit1_1", [P, HALF], F32, wv_at + J)
         logit_on_vector(1, 1, product(KEY, 1, 1, 3), on_raw_wv[:])
-        for (t, h), number in zip(((0, 0), (0, 1), (1, 0), (1, 1)), (0, 5, 6, 7)):
+        for (t, h), number in zip(((0, 0), (0, 1)), (0, 5)):
             value[t, h] = product(VALUE, t, h, number)
             make_gate(t, h, sbuf(f"gate{t}_{h}", [P, HALF], F32)[:])
         gate_values(0)
         key[2, 0] = copied_product(KEY, 2, 0, 1)
-        key[2, 1] = copied_product(KEY, 2, 1, 3)
+        key[2, 1] = copied_product(KEY, 2, 1, 3, held("key2_1", [P, HALF], F32, chain_at + OVERLAP - HALF))
         value[2, 1] = copied_product(VALUE, 2, 1, 4)
+        for h in range(2):
+            value[1, h] = product(VALUE, 1, h, 6 + h)
+            make_gate(1, h, sbuf(f"gate1_{h}", [P, HALF], F32)[:])
         value[2, 0] = product(VALUE, 2, 0, 0)
         key[3, 0] = copied_product(KEY, 3, 0, 1)
+        key[3, 1] = copied_product(KEY, 3, 1, 4, held("key3_1", [P, HALF], F32, QUARTER))
         finish_plane(0)
         gate_values(1)
 
         logit_on_gpsimd(2, chained_logit(2))
         gate_on_tensor(2, 3, 1, result[:, 2 * J : 2 * J + HALF])
-        make_gate(2, 0, sbuf("gate2_0", [P, HALF], F32)[:])
-        key[3, 1] = copied_product(KEY, 3, 1, 4, held("key3_1", [P, HALF], F32, QUARTER))
         value[3, 1] = copied_product(VALUE, 3, 1, 2)
         value[3, 0] = product(VALUE, 3, 0, 5)
         value_rest = sbuf("value_rest", [P, GPSIMD_COLS], F32)
-        nc.scalar.copy(value_rest[:], value[3, 0][:, HALF - GPSIMD_COLS :])
+        nc.scalar.copy(value_rest[:], value[3, 0][:, :GPSIMD_COLS])
+        make_gate(2, 0, sbuf("gate2_0", [P, HALF], F32)[:])
         finish_plane(1)
         gate_values(2)
 
         logit_on_gpsimd(3, chained_logit(3))
         gate_on_tensor(3, 4, 3, sbuf("gate_turned3", [P, HALF], F32))
-        woven.append(held("woven0", [P, QUARTER * PACK], BF16, HALF))
-        weave_pair(0, 0, QUARTER, nc.scalar.copy)
+        woven.append(held("woven0", [P, HALF * PACK], BF16, HALF))
+        weave_pair(0, 0, HALF, nc.scalar.copy)
         make_gate(3, 0, held("gate3_0", [P, HALF], F32, 0)[:])
-        woven.append(held("woven1", [P, (J - QUARTER) * PACK], BF16, J))
-        weave_pair(0, QUARTER, J, nc.scalar.copy)
-        finish_plane(2)
+        woven.append(held("woven1", [P, HALF * PACK], BF16, J + HALF))
+        weave_pair(0, HALF, J, nc.scalar.copy)
+        add_record(2, 0, HALF)
+        add_record(2, HALF, J - QUARTER)
+        store_rows(2, 0, J - QUARTER)
         gate_values(LAST)
 
-        for q in range(J // QUARTER):
-            add_record(LAST, q * QUARTER, (q + 1) * QUARTER)
-            if q % 2:
-                store_rows(LAST, (q - 1) * QUARTER, (q + 1) * QUARTER)
-            if (q + 1) * QUARTER < J:
-                weave_pair(1, q * QUARTER, (q + 1) * QUARTER, nc.scalar.copy)
-        for h in range(2):
-            if h:
-                weave_pair(1, J - QUARTER, J, nc.vector.tensor_copy)
-            for c0 in (h * HALF, h * HALF + QUARTER):
-                quantise_result(c0, c0 + QUARTER)
-            nc.sync.dma_start(out_words[:, halves[h]], res_codes[:, halves[h]].bitcast(I32))
+        late_planes = result[:, 2 * J :].rearrange("p (v j) -> p v j", v=2)
+        for q in (1, 2, 0, 3):
+            c0, c1 = q * QUARTER, (q + 1) * QUARTER
+            add_record(LAST, c0, c1)
+            if q == 0:
+                store_rows(LAST, 0, J - QUARTER)
+            if q == 3:
+                add_record(2, c0, c1)
+                nc.sync.dma_start(out_rows[:, 2:, c0:c1], late_planes[:, :, c0:c1])
+            weave_pair(1, c0, c1, nc.scalar.copy)
+        for c0, c1 in ((HALF, J - QUARTER), (0, HALF), (J - QUARTER, J)):
+            quantise_result(c0, c1)
+            nc.sync.dma_start(out_words[:, c0:c1], res_codes[:, c0:c1].bitcast(I32))
         for quad in range(P // QUADRANT):
             queue = nc.sync if quad % 2 else nc.scalar
             queue.dma_start(scale_rows(out_2, quad), scale_partitions(res_scales, quad))

@@ -30,8 +30,7 @@ LAST = PACK - 1
 KEY, VALUE = 0, 1
 TURNED_FROM = 2
 SCALAR_M = 72
-SCALAR_M_KEY = 66
-GPSIMD_COLS = 256
+SCALAR_M_KEY = 64
 
 
 def tile_list_engram_addLP_kernel(
@@ -122,6 +121,7 @@ def tile_list_engram_addLP_kernel(
 
         logit, gate, gated, key, value = {}, {}, {}, {}, {}
         woven = []
+        gated_rest = result[:, 3 * J - QUARTER : 3 * J]
 
         def gather_scales(h):
             entries = offsets[:, h * HALF // GROUP : (h + 1) * HALF // GROUP]
@@ -197,24 +197,23 @@ def tile_list_engram_addLP_kernel(
                 if t == LAST and h:
                     gated[t, h] = held("gated3_1", [P, HALF], F32, gated_at(1))[:]
                 elif t == LAST:
-                    gated[t, h] = result[:, 3 * J - QUARTER : 3 * J + QUARTER]
+                    gated[t, h] = held("gated3_0", [P, QUARTER], F32, gated_at(t) + QUARTER)[:]
                 elif h:
                     gated[t, h] = sbuf(f"gated{t}", [P, HALF], F32, tag="gated")[:]
                 else:
                     gated[t, h] = held(f"gated{t}_0", [P, HALF], F32, gated_at(t))[:]
                 in_psum, in_sbuf = (gate, value) if t >= TURNED_FROM and h else (value, gate)
-                own = slice(GPSIMD_COLS if (t, h) == (LAST, 0) else 0, HALF)
+                own = slice(0, QUARTER if (t, h) == (LAST, 0) else HALF)
                 nc.vector.tensor_tensor(gated[t, h][:, own], in_psum[t, h][:, own], in_sbuf[t, h][:, own], MULT)
             if t == LAST:
-                rest = slice(0, GPSIMD_COLS)
-                nc.gpsimd.tensor_tensor(gated[t, 0][:, rest], value_rest[:], gate[t, 0][:, rest], MULT)
+                nc.gpsimd.tensor_tensor(gated_rest, value_rest[:], gate[t, 0][:, QUARTER:], MULT)
 
         def add_record(t, c0, c1):
             h = c0 // HALF
             nc.vector.tensor_tensor(
                 result[:, t * J + c0 : t * J + c1],
                 r_win[t][:].indirect(offsets[:, c0 // GROUP : c1 // GROUP]),
-                gated[t, h][:, c0 - h * HALF : c1 - h * HALF],
+                gated_rest if (t, c0) == (LAST, QUARTER) else gated[t, h][:, c0 - h * HALF : c1 - h * HALF],
                 ADD,
             )
 
@@ -286,8 +285,8 @@ def tile_list_engram_addLP_kernel(
         gate_on_tensor(2, 3, 1, result[:, 2 * J : 2 * J + HALF])
         value[3, 1] = copied_product(VALUE, 3, 1, 2)
         value[3, 0] = product(VALUE, 3, 0, 5)
-        value_rest = sbuf("value_rest", [P, GPSIMD_COLS], F32)
-        nc.scalar.copy(value_rest[:], value[3, 0][:, :GPSIMD_COLS])
+        value_rest = sbuf("value_rest", [P, QUARTER], F32)
+        nc.scalar.copy(value_rest[:], value[3, 0][:, QUARTER:])
         make_gate(2, 0, sbuf("gate2_0", [P, HALF], F32)[:])
         finish_plane(1)
         gate_values(2)
@@ -304,17 +303,18 @@ def tile_list_engram_addLP_kernel(
         store_rows(2, 0, J - QUARTER)
         gate_values(LAST)
 
-        late_planes = result[:, 2 * J :].rearrange("p (v j) -> p v j", v=2)
-        for q in (1, 2, 0, 3):
-            c0, c1 = q * QUARTER, (q + 1) * QUARTER
+        held_from = J - QUARTER
+        for c0, c1 in ((0, P), (P, QUARTER), (QUARTER, HALF), (HALF, held_from)):
             add_record(LAST, c0, c1)
-            if q == 0:
-                store_rows(LAST, 0, J - QUARTER)
-            if q == 3:
-                add_record(2, c0, c1)
-                nc.sync.dma_start(out_rows[:, 2:, c0:c1], late_planes[:, :, c0:c1])
             weave_pair(1, c0, c1, nc.scalar.copy)
-        for c0, c1 in ((HALF, J - QUARTER), (0, HALF), (J - QUARTER, J)):
+        store_rows(LAST, 0, held_from)
+        add_record(LAST, held_from, J)
+        store_rows(LAST, held_from, J)
+        for c0 in (held_from, held_from + P):
+            add_record(2, c0, c0 + P)
+            weave_pair(1, c0, c0 + P, nc.scalar.copy)
+        store_rows(2, held_from, J)
+        for c0, c1 in ((0, HALF), (HALF, J - P), (J - P, J)):
             quantise_result(c0, c1)
             nc.sync.dma_start(out_words[:, c0:c1], res_codes[:, c0:c1].bitcast(I32))
         for quad in range(P // QUADRANT):

@@ -318,5 +318,4 @@ def tile_list_engram_addLP_kernel(
             quantise_result(c0, c1)
             nc.sync.dma_start(out_words[:, c0:c1], res_codes[:, c0:c1].bitcast(I32))
         for quad in range(P // QUADRANT):
-            queue = nc.sync if quad % 2 else nc.scalar
-            queue.dma_start(scale_rows(out_2, quad), scale_partitions(res_scales, quad))
+            nc.scalar.dma_start(scale_rows(out_2, quad), scale_partitions(res_scales, quad))

@@ -22,6 +22,7 @@ GROUP = 16
 QUADRANT = 32
 SCALE_ROWS = 4
 ALIGN = 64
+DMA_ALIGN = 256
 FLOAT_BYTES = 4
 OVERLAP = 64
 HALF = J // 2
@@ -49,7 +50,7 @@ def tile_list_engram_addLP_kernel(
             return loads.tile(shape, dtype, name=name, tag=name, offset=FLOAT_BYTES * first_float)
 
         def packed(name, shape, dtype, first_byte):
-            return loads.tile(shape, dtype, name=name, tag=name, offset=first_byte, align_bytes=ALIGN)
+            return loads.tile(shape, dtype, name=name, tag=name, offset=first_byte, align_bytes=DMA_ALIGN)
 
         def bank(name, number):
             return psum.tile([P, HALF], F32, name=name, tag=f"bank{number}")

@@ -21,7 +21,6 @@ PACK = 4
 GROUP = 16
 QUADRANT = 32
 SCALE_ROWS = 4
-ALIGN = 64
 DMA_ALIGN = 256
 FLOAT_BYTES = 4
 OVERLAP = 64
@@ -44,7 +43,7 @@ def tile_list_engram_addLP_kernel(
         psum = ctx.enter_context(tc.psum_pool(name="psum", bufs=1))
 
         def sbuf(name, shape, dtype, tag=None):
-            return keep.tile(shape, dtype, name=name, tag=tag or name, align_bytes=ALIGN)
+            return keep.tile(shape, dtype, name=name, tag=tag or name, align_bytes=DMA_ALIGN)
 
         def held(name, shape, dtype, first_float):
             return loads.tile(shape, dtype, name=name, tag=name, offset=FLOAT_BYTES * first_float)
@@ -55,7 +54,7 @@ def tile_list_engram_addLP_kernel(
         def bank(name, number):
             return psum.tile([P, HALF], F32, name=name, tag=f"bank{number}")
 
-        offsets = keep.tile([P, J // GROUP], U16, name="offsets")
+        offsets = keep.tile([P, J // GROUP], U16, name="offsets", align_bytes=DMA_ALIGN)
         w_codes = [sbuf(f"w_codes{w}", [P, N], U32) for w in (KEY, VALUE)]
         res_codes = sbuf("res_codes", [P, J], U32)
         res_scales = sbuf("res_scales", [P, J], U8)

@@ -77,11 +77,11 @@ def tile_list_engram_addLP_kernel(
         halves = [slice(h * HALF, (h + 1) * HALF) for h in range(2)]
         squares = [slice(e * P, (e + 1) * P) for e in range(HALF // P)]
 
-        def scale_partitions(tile, quad):
-            return tile[QUADRANT * quad : QUADRANT * quad + SCALE_ROWS, :].bitcast(I32)
+        def scale_partitions(tile, r):
+            return tile[r:P:QUADRANT, :].bitcast(I32)
 
-        def scale_rows(dram, quad):
-            return dram[0, SCALE_ROWS * quad : SCALE_ROWS * (quad + 1), :].bitcast(I32)
+        def scale_rows(dram, r):
+            return dram[0][r : SCALE_ROWS * P // QUADRANT : SCALE_ROWS, :].bitcast(I32)
 
         nc.gpsimd.memset(scale_win[:].bitcast(I32), 0)
         nc.gpsimd.memset(warm[:, 0:1], 0.0)
@@ -105,8 +105,8 @@ def tile_list_engram_addLP_kernel(
 
         nc.sync.dma_start(word_win[:], tab_words[0].rearrange("p t i -> p (t i)").bitcast(I32))
         nc.sync.dma_start(offsets[:], offs)
-        for quad in range(P // QUADRANT):
-            nc.sync.dma_start(scale_partitions(scale_win, quad), scale_rows(tab_scales, quad))
+        for r in range(SCALE_ROWS):
+            nc.sync.dma_start(scale_partitions(scale_win, r), scale_rows(tab_scales, r))
         nc.scalar.activation(warm[:, 1:2], warm[:, 0:1], SIGMOID)
         nc.sync.dma_start(wk_raw[:], wk.rearrange("(p i) c -> p i c", i=PACK))
         nc.sync.dma_start(wv_raw[:], wv.rearrange("(p i) c -> p i c", i=PACK))
@@ -317,5 +317,5 @@ def tile_list_engram_addLP_kernel(
         for c0, c1 in ((0, HALF), (HALF, J - P), (J - P, J)):
             quantise_result(c0, c1)
             nc.sync.dma_start(out_words[:, c0:c1], res_codes[:, c0:c1].bitcast(I32))
-        for quad in range(P // QUADRANT):
-            nc.scalar.dma_start(scale_rows(out_2, quad), scale_partitions(res_scales, quad))
+        for r in range(SCALE_ROWS):
+            nc.scalar.dma_start(scale_rows(out_2, r), scale_partitions(res_scales, r))

@@ -30,7 +30,7 @@ LAST = PACK - 1
 KEY, VALUE = 0, 1
 TURNED_FROM = 2
 SCALAR_M = 72
-SCALAR_M_KEY = 64
+SCALAR_M_KEY = 72
 
 
 def tile_list_engram_addLP_kernel(

from contextlib import ExitStack

import concourse.mybir as mybir

K, N, T, J = 512, 512, 2048, 1024
FLOPS = 2 * 2 * K * N * J

F32 = mybir.dt.float32
BF16 = mybir.dt.bfloat16
I32 = mybir.dt.int32
U32 = mybir.dt.uint32
U16 = mybir.dt.uint16
U8 = mybir.dt.uint8
FP8X4 = mybir.dt.float8_e4m3fn_x4
ADD = mybir.AluOpType.add
MULT = mybir.AluOpType.mult
SIGMOID = mybir.ActivationFunctionType.Sigmoid

P = 128
PACK = 4
GROUP = 16
QUADRANT = 32
SCALE_ROWS = 4
DMA_ALIGN = 256
FLOAT_BYTES = 4
OVERLAP = 64
HALF = J // 2
QUARTER = J // 4
LAST = PACK - 1
KEY, VALUE = 0, 1
TURNED_FROM = 2
SCALAR_M = 72
SCALAR_M_KEY = 72


def tile_list_engram_addLP_kernel(
    tc, tab_words, tab_scales, wk, wv, st, rT, offs, out_0, out_1, out_2
):
    nc = tc.nc
    with ExitStack() as ctx:
        keep = ctx.enter_context(tc.tile_pool(name="keep", bufs=1))
        loads = ctx.enter_context(tc.tile_pool(name="loads", bufs=1))
        psum = ctx.enter_context(tc.psum_pool(name="psum", bufs=1))

        def sbuf(name, shape, dtype, tag=None):
            return keep.tile(shape, dtype, name=name, tag=tag or name, align_bytes=DMA_ALIGN)

        def held(name, shape, dtype, first_float):
            return loads.tile(shape, dtype, name=name, tag=name, offset=FLOAT_BYTES * first_float)

        def packed(name, shape, dtype, first_byte):
            return loads.tile(shape, dtype, name=name, tag=name, offset=first_byte, align_bytes=DMA_ALIGN)

        def bank(name, number):
            return psum.tile([P, HALF], F32, name=name, tag=f"bank{number}")

        offsets = keep.tile([P, J // GROUP], U16, name="offsets", align_bytes=DMA_ALIGN)
        w_codes = [sbuf(f"w_codes{w}", [P, N], U32) for w in (KEY, VALUE)]
        res_codes = sbuf("res_codes", [P, J], U32)
        res_scales = sbuf("res_scales", [P, J], U8)
        ident = sbuf("ident", [P, P], F32)
        warm = sbuf("warm", [P, 2], F32)
        zeros = sbuf("zeros", [P, P], F32)

        chain_at = T
        result_at = chain_at + 5 * QUARTER
        wv_at = result_at + PACK * J - OVERLAP
        st_at = wv_at + PACK * N
        r_at = st_at + PACK * J
        wk_at = r_at + PACK * T
        scale_byte = FLOAT_BYTES * (wk_at + PACK * N)
        scale_win = packed("scale_win", [P, T], U8, scale_byte)
        st_rows = st.rearrange("(p t) j -> p t j", t=PACK)
        r_rows = rT.rearrange("(p t) c -> p t c", t=PACK)
        out_rows = out_0.rearrange("(p t) j -> p t j", t=PACK)
        out_words = out_1[0].rearrange("p j i -> p (j i)").bitcast(I32)
        halves = [slice(h * HALF, (h + 1) * HALF) for h in range(2)]
        squares = [slice(e * P, (e + 1) * P) for e in range(HALF // P)]

        def scale_partitions(tile, r):
            return tile[r:P:QUADRANT, :].bitcast(I32)

        def scale_rows(dram, r):
            return dram[0][r : SCALE_ROWS * P // QUADRANT : SCALE_ROWS, :].bitcast(I32)

        nc.gpsimd.memset(scale_win[:].bitcast(I32), 0)
        nc.gpsimd.memset(warm[:, 0:1], 0.0)
        nc.gpsimd.memset(zeros[:, :P], 0.0)
        nc.gpsimd.affine_select(
            out=ident[:], in_=zeros[:, :P], compare_op=mybir.AluOpType.not_equal, fill=1.0, base=0,
            pattern=[[-1, P]], channel_multiplier=1,
        )

        word_win = held("word_win", [P, T], I32, 0)
        wv_raw = held("wv_raw", [P, PACK, N], F32, wv_at)
        result = held("result", [P, PACK * J], F32, result_at)
        st_sb = [held(f"st{t}", [P, J], F32, st_at + J * t) for t in range(LAST)]
        st_last = [held(f"st{LAST}_{h}", [P, HALF], F32, st_at + J * LAST + HALF * h) for h in range(2)]
        st_half = {(t, h): st_sb[t][:, halves[h]] for t in range(LAST) for h in range(2)}
        for h in range(2):
            st_half[LAST, h] = st_last[h][:]
        r_win = [held(f"r_win{t}", [P, T], F32, r_at + T * t) for t in range(PACK)]
        wk_raw = held("wk_raw", [P, PACK, N], F32, wk_at)
        w_raw = [wk_raw, wv_raw]

        nc.sync.dma_start(word_win[:], tab_words[0].rearrange("p t i -> p (t i)").bitcast(I32))
        nc.sync.dma_start(offsets[:], offs)
        for r in range(SCALE_ROWS):
            nc.sync.dma_start(scale_partitions(scale_win, r), scale_rows(tab_scales, r))
        nc.scalar.activation(warm[:, 1:2], warm[:, 0:1], SIGMOID)
        nc.sync.dma_start(wk_raw[:], wk.rearrange("(p i) c -> p i c", i=PACK))
        nc.sync.dma_start(wv_raw[:], wv.rearrange("(p i) c -> p i c", i=PACK))
        nc.sync.dma_start(st_sb[0][:], st_rows[:, 0, :])
        for t in range(PACK):
            if t + 1 < LAST:
                nc.sync.dma_start(st_sb[t + 1][:], st_rows[:, t + 1, :])
            elif t + 1 == LAST:
                for h in (1, 0):
                    nc.sync.dma_start(st_half[LAST, h], st_rows[:, LAST, halves[h]])
            nc.sync.dma_start(r_win[t][:], r_rows[:, t, :])

        logit, gate, gated, key, value = {}, {}, {}, {}, {}
        woven = []
        gated_rest = result[:, 3 * J - QUARTER : 3 * J]

        def gather_scales(h):
            entries = offsets[:, h * HALF // GROUP : (h + 1) * HALF // GROUP]
            nc.vector.tensor_copy(tab_sc[h][:], scale_win[:].indirect(entries))

        def weave_weight(w, woven_w, m0, m1, copy, walk):
            copy(
                woven_w[:].rearrange(f"p (t m i) -> p {walk}", t=PACK, i=PACK)[:, m0:m1],
                w_raw[w][:].rearrange(f"p i (m t) -> p {walk}", t=PACK)[:, m0:m1],
            )

        def round_on_gpsimd(out, in_):
            nc.gpsimd.tensor_scalar(out, in_, 1.0, 0.0, MULT, ADD)

        def quantise_weight(w, woven_w):
            nc.vector.quantize_mx(out=w_codes[w][:].bitcast(FP8X4), scales=w_scales[w][:], in_=woven_w[:])

        def product(w, t, h, number):
            acc = bank(f"acc{w}_{t}_{h}", number)
            plane_cols = slice(t * P, (t + 1) * P)
            nc.tensor.matmul_mx(
                out=acc[:],
                lhsT=w_codes[w][:, plane_cols].bitcast(FP8X4),
                lhsT_scale=w_scales[w][:, plane_cols],
                rhs=tab_codes[:, halves[h]].bitcast(FP8X4),
                rhs_scale=tab_sc[h][:],
                start=True,
                stop=True,
            )
            return acc

        def copied_product(w, t, h, number, place=None):
            if place is None:
                place = sbuf(f"copied{w}_{t}_{h}", [P, HALF], F32)
            nc.scalar.copy(place[:], product(w, t, h, number)[:])
            return place

        def logit_on_vector(t, h, key_bank, place):
            logit[t, h] = place
            nc.vector.tensor_tensor(place, key_bank[:], st_half[t, h], ADD)

        def logit_on_gpsimd(t, place):
            logit[t, 0] = place
            nc.gpsimd.tensor_tensor(place, key[t, 0][:], st_half[t, 0], ADD)

        def make_gate(t, h, place):
            gate[t, h] = place
            nc.scalar.activation(place, logit[t, h], SIGMOID)

        def gate_on_tensor(t, logit_bank, gate_bank, turned):
            acc = bank(f"logit_turned{t}", logit_bank)
            turns = [(src, sq) for src in (key[t, 1][:], st_half[t, 1]) for sq in squares]
            if t == LAST:
                turns.append(turns.pop(len(squares) - 1))
            for step, (src, sq) in enumerate(turns):
                nc.tensor.matmul(
                    acc[:, sq], src[:, sq], ident[:],
                    start=(step == 0), stop=(step == len(turns) - 1), is_transpose=True,
                )
            nc.scalar.activation(turned[:], acc[:], SIGMOID)
            gate[t, 1] = bank(f"gate{t}", gate_bank)[:]
            for sq in squares:
                nc.tensor.transpose(gate[t, 1][:, sq], turned[:, sq], ident[:])

        def gated_at(t):
            return chain_at + (1 + min(t, LAST - 1)) * QUARTER

        def chained_logit(t):
            return held(f"logit{t}_0", [P, HALF], F32, gated_at(t - 1) - HALF)[:]

        def gate_values(t):
            for h in range(2):
                if t == LAST and h:
                    gated[t, h] = held("gated3_1", [P, HALF], F32, gated_at(1))[:]
                elif t == LAST:
                    gated[t, h] = held("gated3_0", [P, QUARTER], F32, gated_at(t) + QUARTER)[:]
                elif h:
                    gated[t, h] = sbuf(f"gated{t}", [P, HALF], F32, tag="gated")[:]
                else:
                    gated[t, h] = held(f"gated{t}_0", [P, HALF], F32, gated_at(t))[:]
                in_psum, in_sbuf = (gate, value) if t >= TURNED_FROM and h else (value, gate)
                own = slice(0, QUARTER if (t, h) == (LAST, 0) else HALF)
                nc.vector.tensor_tensor(gated[t, h][:, own], in_psum[t, h][:, own], in_sbuf[t, h][:, own], MULT)
            if t == LAST:
                nc.gpsimd.tensor_tensor(gated_rest, value_rest[:], gate[t, 0][:, QUARTER:], MULT)

        def add_record(t, c0, c1):
            h = c0 // HALF
            nc.vector.tensor_tensor(
                result[:, t * J + c0 : t * J + c1],
                r_win[t][:].indirect(offsets[:, c0 // GROUP : c1 // GROUP]),
                gated_rest if (t, c0) == (LAST, QUARTER) else gated[t, h][:, c0 - h * HALF : c1 - h * HALF],
                ADD,
            )

        def store_rows(t, c0, c1):
            nc.sync.dma_start(out_rows[:, t, c0:c1], result[:, t * J + c0 : t * J + c1])

        def finish_plane(t):
            for h in range(2):
                add_record(t, h * HALF, (h + 1) * HALF)
            store_rows(t, 0, J)

        def woven_cols(c0, c1):
            part = c0 // HALF
            return woven[part][:, (c0 - part * HALF) * PACK : (c1 - part * HALF) * PACK]

        def weave_pair(u, c0, c1, copy):
            planes = result[:, 2 * u * J : 2 * (u + 1) * J].rearrange("p (v j) -> p j v", v=2)
            pairs = woven_cols(c0, c1).rearrange("p (j u v) -> p u j v", u=2, v=2)
            copy(pairs[:, u], planes[:, c0:c1])

        def quantise_result(c0, c1):
            nc.vector.quantize_mx(
                out=res_codes[:, c0:c1].bitcast(FP8X4), scales=res_scales[:, c0:c1], in_=woven_cols(c0, c1)
            )

        tab_codes = sbuf("tab_codes", [P, J], U32)
        tab_sc = [sbuf("tab_sc0", [P, HALF], U8)]
        nc.vector.tensor_copy(tab_codes[:], word_win[:].bitcast(U32).indirect(offsets[:]))
        gather_scales(0)
        wk_scales = sbuf("wk_scales", [P, N], U8)
        w_scales = [wk_scales, sbuf("wv_scales", [P, N], U8)]
        wk_bf = sbuf("wk_bf", [P, N * PACK], BF16)
        weave_weight(KEY, wk_bf, 0, SCALAR_M_KEY, nc.scalar.copy, "m i t")
        weave_weight(KEY, wk_bf, SCALAR_M_KEY, P, round_on_gpsimd, "m t i")
        quantise_weight(KEY, wk_bf)
        tab_sc.append(packed("tab_sc1", [P, HALF], U8, FLOAT_BYTES * wk_at))
        gather_scales(1)
        wv_bf = sbuf("wv_bf", [P, N * PACK], BF16)
        weave_weight(VALUE, wv_bf, 0, SCALAR_M, nc.scalar.copy, "m i t")
        weave_weight(VALUE, wv_bf, SCALAR_M, P, round_on_gpsimd, "m t i")
        quantise_weight(VALUE, wv_bf)


        first_key = product(KEY, 0, 0, 0)
        key[1, 0] = copied_product(KEY, 1, 0, 2)
        on_woven_wv = sbuf("logits1", [P, J], F32, tag="wv_bf")
        logit_on_vector(0, 0, first_key, sbuf("logit0_0", [P, HALF], F32)[:])
        logit_on_vector(0, 1, product(KEY, 0, 1, 1), result[:, :HALF])
        logit_on_gpsimd(1, on_woven_wv[:, halves[0]])
        on_raw_wv = held("logit1_1", [P, HALF], F32, wv_at + J)
        logit_on_vector(1, 1, product(KEY, 1, 1, 3), on_raw_wv[:])
        for (t, h), number in zip(((0, 0), (0, 1)), (0, 5)):
            value[t, h] = product(VALUE, t, h, number)
            make_gate(t, h, sbuf(f"gate{t}_{h}", [P, HALF], F32)[:])
        gate_values(0)
        key[2, 0] = copied_product(KEY, 2, 0, 1)
        key[2, 1] = copied_product(KEY, 2, 1, 3, held("key2_1", [P, HALF], F32, chain_at + OVERLAP - HALF))
        value[2, 1] = copied_product(VALUE, 2, 1, 4)
        for h in range(2):
            value[1, h] = product(VALUE, 1, h, 6 + h)
            make_gate(1, h, sbuf(f"gate1_{h}", [P, HALF], F32)[:])
        value[2, 0] = product(VALUE, 2, 0, 0)
        key[3, 0] = copied_product(KEY, 3, 0, 1)
        key[3, 1] = copied_product(KEY, 3, 1, 4, held("key3_1", [P, HALF], F32, QUARTER))
        finish_plane(0)
        gate_values(1)

        logit_on_gpsimd(2, chained_logit(2))
        gate_on_tensor(2, 3, 1, result[:, 2 * J : 2 * J + HALF])
        value[3, 1] = copied_product(VALUE, 3, 1, 2)
        value[3, 0] = product(VALUE, 3, 0, 5)
        value_rest = sbuf("value_rest", [P, QUARTER], F32)
        nc.scalar.copy(value_rest[:], value[3, 0][:, QUARTER:])
        make_gate(2, 0, sbuf("gate2_0", [P, HALF], F32)[:])
        finish_plane(1)
        gate_values(2)

        logit_on_gpsimd(3, chained_logit(3))
        gate_on_tensor(3, 4, 3, sbuf("gate_turned3", [P, HALF], F32))
        woven.append(held("woven0", [P, HALF * PACK], BF16, HALF))
        weave_pair(0, 0, HALF, nc.scalar.copy)
        make_gate(3, 0, held("gate3_0", [P, HALF], F32, 0)[:])
        woven.append(held("woven1", [P, HALF * PACK], BF16, J + HALF))
        weave_pair(0, HALF, J, nc.scalar.copy)
        add_record(2, 0, HALF)
        add_record(2, HALF, J - QUARTER)
        store_rows(2, 0, J - QUARTER)
        gate_values(LAST)

        held_from = J - QUARTER
        for c0, c1 in ((0, P), (P, QUARTER), (QUARTER, HALF), (HALF, held_from)):
            add_record(LAST, c0, c1)
            weave_pair(1, c0, c1, nc.scalar.copy)
        store_rows(LAST, 0, held_from)
        add_record(LAST, held_from, J)
        store_rows(LAST, held_from, J)
        for c0 in (held_from, held_from + P):
            add_record(2, c0, c0 + P)
            weave_pair(1, c0, c0 + P, nc.scalar.copy)
        store_rows(2, held_from, J)
        for c0, c1 in ((0, HALF), (HALF, J - P), (J - P, J)):
            quantise_result(c0, c1)
            nc.sync.dma_start(out_words[:, c0:c1], res_codes[:, c0:c1].bitcast(I32))
        for r in range(SCALE_ROWS):
            nc.scalar.dma_start(scale_rows(out_2, r), scale_partitions(res_scales, r))
